import numpy as np
import ml_dtypes


def mxq(x, axis, fmt="e4m3"):
    dtype, down = {"e4m3": (ml_dtypes.float8_e4m3fn, 7), "e5m2": (ml_dtypes.float8_e5m2, 14)}[fmt]
    v = np.moveaxis(np.asarray(x, np.float32).astype(ml_dtypes.bfloat16).astype(np.float64), axis, -1)
    blocks = v.reshape(v.shape[:-1] + (-1, 32))
    amax = np.abs(blocks).max(-1, keepdims=True)
    byte = np.maximum(np.where(amax > 0, np.frexp(amax)[1] - 1 + 127, 0) - down, 1)
    scale = np.exp2(byte - 127.0)
    codes = (blocks / scale).astype(np.float32).astype(dtype).astype(np.float64)
    return np.moveaxis((codes * scale).reshape(v.shape), -1, axis)


WIDE = False


def mx_kscale(k):
    if not WIDE:
        return np.ones(k)
    levels = np.array([10, -10, 5, -5, 0])
    if k % 512:
        return np.exp2(np.random.permutation(np.resize(levels, k // 32))).repeat(32)
    a = np.empty((k // 512, 16))
    for p in range(k // 512):
        a[p, :8] = np.random.permutation(np.resize(levels, 8))
        for g in range(8):
            far = levels[np.abs(levels - a[p, g]) >= 10]
            a[p, g + 8] = far[np.random.randint(len(far))]
    return np.exp2(a.ravel()).repeat(32)


def f64(x):
    return np.asarray(x).astype(np.float64)


def striped(idx):
    return np.tile(np.asarray(idx).reshape(-1, 16).T, (8, 1)).astype(np.uint16)


def unstriped(offs):
    return offs[:16].T.reshape(-1).astype(np.int64)


E2M1 = np.array([0.0, 0.5, 1.0, 1.5, 2.0, 3.0, 4.0, 6.0, -0.0, -0.5, -1.0, -1.5, -2.0, -3.0, -4.0, -6.0])


def pack_weight(w, fmt):
    k, n = w.shape
    w = f64(np.asarray(w, np.float32).astype(ml_dtypes.bfloat16)).reshape(k // 32, 32, n)
    amax = np.abs(w).max(1)
    if fmt == "e4m3":
        byte = np.frexp(amax)[1] - 1 + 127 - 7
    else:
        mant, ex = np.frexp(amax / 6.0)
        byte = np.where(mant > 0.5, ex, ex - 1) + 127
    byte = np.clip(np.where(amax > 0, byte, 1), 1, 254)
    scaled = (w * np.exp2(127.0 - byte)[:, None, :]).reshape(k, n).astype(np.float32)
    by_word = np.ascontiguousarray(scaled.reshape(k // 512, 128, 4, n).transpose(0, 1, 3, 2))
    if fmt == "e4m3":
        words = by_word.astype(ml_dtypes.float8_e4m3fn).view(np.uint8)
    else:
        c = by_word.astype(ml_dtypes.float4_e2m1fn).view(np.uint8) & 0xF
        words = (c[..., 0::2] | (c[..., 1::2] << 4)).reshape(k // 512, 128, 2 * n)
    return np.ascontiguousarray(words), np.ascontiguousarray(byte.astype(np.uint8).reshape(k // 512, 16, n))


def unpack_weight(words, scales, fmt):
    g, _, n = scales.shape
    words = np.ascontiguousarray(words).reshape(g, 128, n, -1)
    if fmt == "e4m3":
        vals = words.view(ml_dtypes.float8_e4m3fn).astype(np.float64)
    else:
        nib = np.empty((g, 128, n, 4), np.uint8)
        nib[..., 0::2] = words & 0xF
        nib[..., 1::2] = words >> 4
        vals = E2M1[nib]
    vals = vals * np.repeat(np.exp2(scales.astype(np.float64) - 127.0), 8, axis=1)[..., None]
    return vals.transpose(0, 1, 3, 2).reshape(g * 512, n)


B, N, T, D, DV, NQ = 2, 1024, 4096, 1024, 256, 128
PAGE = 512


def setup_inputs():
    n = np.random.standard_normal
    pages = np.random.permutation(T // PAGE)[:B * N // PAGE]
    idx = (pages[:, None] * PAGE + np.arange(PAGE)[None, :]).reshape(-1)
    s = mx_kscale(D)[:, None]
    u = np.ones(T)
    u[idx] = mx_kscale(B * N)
    r = np.random.uniform(0.5, 2.0, T)
    qp = [pack_weight(x, "e4m3") for x in n((B, D, NQ)) * s * (1.00 / np.sqrt(D))]
    k = n((D, T)) / s
    v = n((DV, T)) / (u * r)
    kp = pack_weight(k, "e2m1")
    vp = pack_weight(v.T, "e4m3")
    return {
        "q_words": np.stack([x[0] for x in qp]),
        "q_scales": np.stack([x[1] for x in qp]),
        "k_words": np.ascontiguousarray(kp[0].reshape(D // 1024, 2, 128, T, 2).transpose(0, 2, 3, 1, 4)).reshape(D // 1024, 128, T, 4),
        "k_scales": kp[1],
        "v_words": vp[0],
        "v_scales": vp[1],
        "vs": np.tile(u * r, (128, 1)).astype(np.float32),
        "kb": np.tile(n(T), (128, 1)).astype(np.float32),
        "og": n((B, NQ, DV)).astype(np.float32),
        "offs": striped(idx),
        "voffs": striped((pages[:, None] * DV + np.arange(DV)[None, :]).reshape(-1)),
    }


def reference(q_words, q_scales, k_words, k_scales, v_words, v_scales, vs, kb, og, offs, voffs):
    idx = unstriped(offs)
    k = unpack_weight(k_words.reshape(D // 1024, 128, T, 2, 2).transpose(0, 3, 1, 2, 4).reshape(D // 512, 128, 2 * T), k_scales, "e2m1")
    v = unpack_weight(v_words, v_scales, "e4m3")
    v = v.reshape(T // 512, 512, DV)[unstriped(voffs)[::DV] // DV].reshape(B, N, DV)
    pick = lambda x: x[:, idx].reshape(x.shape[0], B, N).transpose(1, 0, 2)
    q = np.stack([unpack_weight(q_words[b], q_scales[b], "e4m3") for b in range(B)])
    score = q.transpose(0, 2, 1) @ pick(k)
    score = score + pick(f64(kb))[:, :1, :]
    p = score / (1.0 + np.exp(-score))
    w = p * pick(f64(vs))[:, :1, :]
    y = mxq(w, 2, "e4m3") @ v
    y = y / 16.0
    y = y / (1.0 + np.exp(-f64(og)))
    return y

@@ -1,0 +1,184 @@
+from contextlib import ExitStack
+
+import concourse.mybir as mybir
+from concourse.masks import make_identity
+
+B, N, T, D, DV, NQ = 2, 1024, 4096, 1024, 256, 128
+P = 128
+PAGE = 512
+PAGES = N // PAGE
+POOL_PAGES = T // PAGE
+PASSES = D // PAGE
+FLOPS = 2 * B * NQ * N * (D + DV)
+
+F32 = mybir.dt.float32
+BF16 = mybir.dt.bfloat16
+I32 = mybir.dt.int32
+U32 = mybir.dt.uint32
+U16 = mybir.dt.uint16
+U8 = mybir.dt.uint8
+FP8X4 = mybir.dt.float8_e4m3fn_x4
+FP4X4 = mybir.dt.float4_e2m1fn_x4
+ACT = mybir.ActivationFunctionType
+ALU = mybir.AluOpType
+
+
+def tile_attend_pkv4q_silu_kb_gate_kernel(
+    tc, q_words, q_scales, k_words, k_scales, v_words, v_scales, vs, kb, og, offs, voffs, out
+):
+    nc = tc.nc
+    with ExitStack() as ctx:
+        lists = ctx.enter_context(tc.tile_pool(name="lists", bufs=1))
+        keep = ctx.enter_context(tc.tile_pool(name="keep", bufs=1))
+        work = ctx.enter_context(tc.tile_pool(name="work", bufs=2))
+        psum = ctx.enter_context(tc.psum_pool(name="psum", bufs=1))
+
+        voff_t = lists.tile([P, B * PAGES * DV // 16], U16, name="voff_t")
+        nc.sync.dma_start(voff_t[:], voffs)
+        vw_win = keep.tile([P, POOL_PAGES * DV], U32, name="vw_win", tag="win_a", align_bytes=64)
+        nc.sync.dma_start(
+            vw_win[:].bitcast(I32).rearrange("p (u e) -> p u e", u=POOL_PAGES),
+            v_words.rearrange("u p e r -> p u (e r)").bitcast(I32),
+        )
+        off_t = lists.tile([P, B * N // 16], U16, name="off_t")
+        nc.sync.dma_start(off_t[:], offs)
+        kw_win = keep.tile([P, T], U32, name="kw_win", align_bytes=64)
+        nc.sync.dma_start(kw_win[:].bitcast(I32), k_words[0].rearrange("p t r -> p (t r)").bitcast(I32))
+
+        ks_win = keep.tile([P, T], U8, name="ks_win", tag="win_b", align_bytes=64)
+        nc.vector.memset(ks_win[:].bitcast(I32), 0)
+        for quad in range(4):
+            nc.scalar.dma_start(
+                ks_win[32 * quad : 32 * quad + 8, :].bitcast(I32),
+                k_scales[:, 4 * quad : 4 * quad + 4, :].bitcast(I32),
+            )
+
+        qs = keep.tile([P, B * PASSES * NQ], U8, name="qs", align_bytes=64)
+        nc.vector.memset(qs[:].bitcast(I32), 0)
+        vsc_win = keep.tile([P, POOL_PAGES * DV], U8, name="vsc_win", align_bytes=64)
+        nc.vector.memset(vsc_win[:].bitcast(I32), 0)
+        ks1 = keep.tile([P, B * N], U8, name="ks1", align_bytes=64)
+        nc.vector.memset(ks1[:].bitcast(I32), 0)
+
+        qw = keep.tile([P, B * PASSES * NQ], U32, name="qw", align_bytes=64)
+        nc.gpsimd.dma_start(
+            qw[:].bitcast(I32).rearrange("p (g q) -> p g q", q=NQ),
+            q_words.rearrange("b o p q r -> p (b o) (q r)").bitcast(I32),
+        )
+        og_t = keep.tile([P, B, DV], F32, name="og_t")
+        nc.gpsimd.dma_start(og_t[:], og.rearrange("b q e -> q b e"))
+        for quad in range(4):
+            nc.gpsimd.dma_start(
+                qs[32 * quad : 32 * quad + 4, :].bitcast(I32).rearrange("i (g q) -> i g q", g=B * PASSES),
+                q_scales[:, :, 4 * quad : 4 * quad + 4, :].rearrange("b o i q -> i (b o) q").bitcast(I32),
+            )
+        ident = keep.tile([P, P], F32, name="ident")
+        make_identity(nc, ident[:])
+        for quad in range(4):
+            nc.gpsimd.dma_start(
+                vsc_win[32 * quad : 32 * quad + 4, :].bitcast(I32).rearrange("i (u e) -> i u e", u=POOL_PAGES),
+                v_scales[:, 4 * quad : 4 * quad + 4, :].rearrange("u i e -> i u e").bitcast(I32),
+            )
+
+        gate = keep.tile([P, B, DV], F32, name="gate")
+        nc.scalar.activation(gate[:], og_t[:], ACT.Sigmoid)
+        warm = keep.tile([P, 1], F32, name="warm")
+        nc.scalar.activation(warm[:], gate[:, 0, 0:1], ACT.Silu)
+
+        vw = keep.tile([P, B * PAGES * DV], U32, name="vw", align_bytes=64)
+        nc.vector.tensor_copy(vw[:], vw_win[:].indirect(voff_t[:]))
+        kb_win = keep.tile([P, T], F32, name="kb_win", tag="win_a", align_bytes=64)
+        nc.sync.dma_start(kb_win[:], kb)
+
+        ks0 = keep.tile([P, B * N], U8, name="ks0", align_bytes=64)
+        nc.vector.tensor_copy(ks0[:], ks_win[:].indirect(off_t[:]))
+        for quad in range(4):
+            nc.scalar.dma_start(
+                ks1[32 * quad : 32 * quad + 4, :].bitcast(I32),
+                ks0[32 * quad + 4 : 32 * quad + 8, :].bitcast(I32),
+            )
+        vs_win = keep.tile([P, T], F32, name="vs_win", tag="win_b", align_bytes=64)
+        nc.sync.dma_start(vs_win[:], vs)
+        ks = (ks0, ks1)
+
+        cols = N // 16
+        scores = []
+        for b in range(B):
+            kw = work.tile([P, N], U32, name="kw", align_bytes=64)
+            nc.vector.tensor_copy(kw[:], kw_win[:].indirect(off_t[:, b * cols : (b + 1) * cols]))
+            kp = work.tile([P, PASSES * N], U16, name="kp", align_bytes=64)
+            nc.vector.tensor_copy(
+                kp[:].rearrange("p (o n) -> p o n", o=PASSES),
+                kw[:].bitcast(U16).rearrange("p (n o) -> p o n", o=PASSES),
+            )
+            a = work.tile([P, N], F32, name="a")
+            for e in range(PAGES):
+                bank = psum.tile([P, PAGE], F32, name="sc", bufs=3)
+                for o in range(PASSES):
+                    g = b * PASSES + o
+                    nc.tensor.matmul_mx(
+                        out=bank[:],
+                        lhsT=qw[:, g * NQ : (g + 1) * NQ].bitcast(FP8X4),
+                        lhsT_scale=qs[:, g * NQ : (g + 1) * NQ],
+                        rhs=kp[:, o * N + e * PAGE : o * N + (e + 1) * PAGE].bitcast(FP4X4),
+                        rhs_scale=ks[o][:, b * N + e * PAGE : b * N + (e + 1) * PAGE],
+                        start=(o == 0),
+                        stop=(o == PASSES - 1),
+                    )
+                nc.scalar.copy(a[:, e * PAGE : (e + 1) * PAGE], bank[:])
+            scores.append(a)
+
+        ps = []
+        for b in range(B):
+            z = work.tile([P, N], F32, name="z")
+            nc.vector.tensor_tensor(z[:], kb_win[:].indirect(off_t[:, b * cols : (b + 1) * cols]), scores[b][:], ALU.add)
+            p = work.tile([P, N], F32, name="p", tag="p", align_bytes=64)
+            nc.scalar.activation(p[:], z[:], ACT.Silu)
+            ps.append(p)
+
+        pcols = PAGE // 16
+        wis = []
+        wq = []
+
+        def quantise(j):
+            wc = work.tile([P, NQ], U32, name="wc", bufs=4, align_bytes=64)
+            wsc = work.tile([P, NQ], U8, name="wsc", bufs=4, align_bytes=64)
+            nc.vector.quantize_mx(out=wc[:].bitcast(FP8X4), scales=wsc[:], in_=wis[j][:])
+            wq.append((wc, wsc))
+
+        for j in range(B * PAGES):
+            b, e = divmod(j, PAGES)
+            w = work.tile([P, PAGE], F32, name="w", bufs=4)
+            nc.vector.tensor_tensor(
+                w[:], vs_win[:].indirect(off_t[:, j * pcols : (j + 1) * pcols]), ps[b][:, e * PAGE : (e + 1) * PAGE], ALU.mult
+            )
+            bank = psum.tile([P, 4, NQ], F32, name="tr", bufs=3)
+            for t in range(4):
+                nc.tensor.transpose(bank[:, t, :], w[:, t:PAGE:4], ident[:])
+            wi = work.tile([P, 4 * NQ], BF16, name="wi", bufs=4, align_bytes=64)
+            nc.scalar.copy(wi[:].rearrange("p (q t) -> p q t", t=4), bank[:].rearrange("p t q -> p q t"))
+            wis.append(wi)
+            if j >= 2:
+                quantise(j - 2)
+
+        vsc = work.tile([P, B * PAGES * DV], U8, name="vsc", tag="p", align_bytes=64)
+        nc.vector.tensor_copy(vsc[:], vsc_win[:].indirect(voff_t[:]))
+        quantise(2)
+        quantise(3)
+
+        for b in range(B):
+            y = psum.tile([P, DV], F32, name="y", bufs=2)
+            for e in range(PAGES):
+                j = b * PAGES + e
+                nc.tensor.matmul_mx(
+                    out=y[:],
+                    lhsT=wq[j][0][:].bitcast(FP8X4),
+                    lhsT_scale=wq[j][1][:],
+                    rhs=vw[:, j * DV : (j + 1) * DV].bitcast(FP8X4),
+                    rhs_scale=vsc[:, j * DV : (j + 1) * DV],
+                    start=(e == 0),
+                    stop=(e == PAGES - 1),
+                )
+            res = work.tile([P, DV], F32, name="res")
+            nc.vector.scalar_tensor_tensor(res[:], y[:], 1.0 / 16.0, gate[:, b, :], ALU.mult, ALU.mult)
+            nc.sync.dma_start(out[b], res[:])

@@ -30,22 +30,30 @@ def tile_attend_pkv4q_silu_kb_gate_kernel(
     with ExitStack() as ctx:
         lists = ctx.enter_context(tc.tile_pool(name="lists", bufs=1))
         keep = ctx.enter_context(tc.tile_pool(name="keep", bufs=1))
+        shared = ctx.enter_context(tc.tile_pool(name="shared", bufs=1))
         work = ctx.enter_context(tc.tile_pool(name="work", bufs=2))
         psum = ctx.enter_context(tc.psum_pool(name="psum", bufs=1))
 
         voff_t = lists.tile([P, B * PAGES * DV // 16], U16, name="voff_t")
         nc.sync.dma_start(voff_t[:], voffs)
+        off_t = lists.tile([P, B * N // 16], U16, name="off_t")
+        nc.sync.dma_start(off_t[:], offs)
         vw_win = keep.tile([P, POOL_PAGES * DV], U32, name="vw_win", tag="win_a", align_bytes=64)
         nc.sync.dma_start(
             vw_win[:].bitcast(I32).rearrange("p (u e) -> p u e", u=POOL_PAGES),
             v_words.rearrange("u p e r -> p u (e r)").bitcast(I32),
         )
-        off_t = lists.tile([P, B * N // 16], U16, name="off_t")
-        nc.sync.dma_start(off_t[:], offs)
         kw_win = keep.tile([P, T], U32, name="kw_win", align_bytes=64)
         nc.sync.dma_start(kw_win[:].bitcast(I32), k_words[0].rearrange("p t r -> p (t r)").bitcast(I32))
+        qw = keep.tile([P, B * PASSES * NQ], U32, name="qw", align_bytes=64)
+        nc.sync.dma_start(
+            qw[:].bitcast(I32).rearrange("p (g q) -> p g q", q=NQ),
+            q_words.rearrange("b o p q r -> p (b o) (q r)").bitcast(I32),
+        )
+        og_t = keep.tile([P, B, DV], F32, name="og_t")
+        nc.sync.dma_start(og_t[:], og.rearrange("b q e -> q b e"))
 
-        ks_win = keep.tile([P, T], U8, name="ks_win", tag="win_b", align_bytes=64)
+        ks_win = shared.tile([P, T], U8, name="ks_win", offset=0, align_bytes=64)
         nc.vector.memset(ks_win[:].bitcast(I32), 0)
         for quad in range(4):
             nc.scalar.dma_start(
@@ -53,32 +61,24 @@ def tile_attend_pkv4q_silu_kb_gate_kernel(
                 k_scales[:, 4 * quad : 4 * quad + 4, :].bitcast(I32),
             )
 
-        qs = keep.tile([P, B * PASSES * NQ], U8, name="qs", align_bytes=64)
-        nc.vector.memset(qs[:].bitcast(I32), 0)
         vsc_win = keep.tile([P, POOL_PAGES * DV], U8, name="vsc_win", align_bytes=64)
         nc.vector.memset(vsc_win[:].bitcast(I32), 0)
-        ks1 = keep.tile([P, B * N], U8, name="ks1", align_bytes=64)
-        nc.vector.memset(ks1[:].bitcast(I32), 0)
-
-        qw = keep.tile([P, B * PASSES * NQ], U32, name="qw", align_bytes=64)
-        nc.gpsimd.dma_start(
-            qw[:].bitcast(I32).rearrange("p (g q) -> p g q", q=NQ),
-            q_words.rearrange("b o p q r -> p (b o) (q r)").bitcast(I32),
-        )
-        og_t = keep.tile([P, B, DV], F32, name="og_t")
-        nc.gpsimd.dma_start(og_t[:], og.rearrange("b q e -> q b e"))
         for quad in range(4):
-            nc.gpsimd.dma_start(
-                qs[32 * quad : 32 * quad + 4, :].bitcast(I32).rearrange("i (g q) -> i g q", g=B * PASSES),
-                q_scales[:, :, 4 * quad : 4 * quad + 4, :].rearrange("b o i q -> i (b o) q").bitcast(I32),
-            )
-        ident = keep.tile([P, P], F32, name="ident")
-        make_identity(nc, ident[:])
-        for quad in range(4):
-            nc.gpsimd.dma_start(
+            nc.sync.dma_start(
                 vsc_win[32 * quad : 32 * quad + 4, :].bitcast(I32).rearrange("i (u e) -> i u e", u=POOL_PAGES),
                 v_scales[:, 4 * quad : 4 * quad + 4, :].rearrange("u i e -> i u e").bitcast(I32),
             )
+        qs = keep.tile([P, B * PASSES * NQ], U8, name="qs", align_bytes=64)
+        nc.vector.memset(qs[:].bitcast(I32), 0)
+        for quad in range(4):
+            nc.scalar.dma_start(
+                qs[32 * quad : 32 * quad + 4, :].bitcast(I32).rearrange("i (g q) -> i g q", g=B * PASSES),
+                q_scales[:, :, 4 * quad : 4 * quad + 4, :].rearrange("b o i q -> i (b o) q").bitcast(I32),
+            )
+        ks1 = keep.tile([P, B * N], U8, name="ks1", align_bytes=64)
+        nc.vector.memset(ks1[:].bitcast(I32), 0)
+        ident = keep.tile([P, P], F32, name="ident")
+        make_identity(nc, ident[:])
 
         gate = keep.tile([P, B, DV], F32, name="gate")
         nc.scalar.activation(gate[:], og_t[:], ACT.Sigmoid)
@@ -97,46 +97,44 @@ def tile_attend_pkv4q_silu_kb_gate_kernel(
                 ks1[32 * quad : 32 * quad + 4, :].bitcast(I32),
                 ks0[32 * quad + 4 : 32 * quad + 8, :].bitcast(I32),
             )
-        vs_win = keep.tile([P, T], F32, name="vs_win", tag="win_b", align_bytes=64)
+        vs_win = shared.tile([P, T], F32, name="vs_win", offset=0, align_bytes=64)
         nc.sync.dma_start(vs_win[:], vs)
         ks = (ks0, ks1)
 
+        pcols = PAGE // 16
         cols = N // 16
-        scores = []
-        for b in range(B):
-            kw = work.tile([P, N], U32, name="kw", align_bytes=64)
-            nc.vector.tensor_copy(kw[:], kw_win[:].indirect(off_t[:, b * cols : (b + 1) * cols]))
-            kp = work.tile([P, PASSES * N], U16, name="kp", align_bytes=64)
+        scores = [work.tile([P, N], F32, name="a") for b in range(B)]
+        for j in range(B * PAGES):
+            b, e = divmod(j, PAGES)
+            kw = work.tile([P, PAGE], U32, name="kw", align_bytes=64)
+            nc.vector.tensor_copy(kw[:], kw_win[:].indirect(off_t[:, j * pcols : (j + 1) * pcols]))
+            kp = work.tile([P, PASSES * PAGE], U16, name="kp", bufs=4, align_bytes=64)
             nc.vector.tensor_copy(
                 kp[:].rearrange("p (o n) -> p o n", o=PASSES),
                 kw[:].bitcast(U16).rearrange("p (n o) -> p o n", o=PASSES),
             )
-            a = work.tile([P, N], F32, name="a")
-            for e in range(PAGES):
-                bank = psum.tile([P, PAGE], F32, name="sc", bufs=3)
-                for o in range(PASSES):
-                    g = b * PASSES + o
-                    nc.tensor.matmul_mx(
-                        out=bank[:],
-                        lhsT=qw[:, g * NQ : (g + 1) * NQ].bitcast(FP8X4),
-                        lhsT_scale=qs[:, g * NQ : (g + 1) * NQ],
-                        rhs=kp[:, o * N + e * PAGE : o * N + (e + 1) * PAGE].bitcast(FP4X4),
-                        rhs_scale=ks[o][:, b * N + e * PAGE : b * N + (e + 1) * PAGE],
-                        start=(o == 0),
-                        stop=(o == PASSES - 1),
-                    )
-                nc.scalar.copy(a[:, e * PAGE : (e + 1) * PAGE], bank[:])
-            scores.append(a)
+            bank = psum.tile([P, PAGE], F32, name="sc", bufs=3)
+            for o in range(PASSES):
+                g = b * PASSES + o
+                nc.tensor.matmul_mx(
+                    out=bank[:],
+                    lhsT=qw[:, g * NQ : (g + 1) * NQ].bitcast(FP8X4),
+                    lhsT_scale=qs[:, g * NQ : (g + 1) * NQ],
+                    rhs=kp[:, o * PAGE : (o + 1) * PAGE].bitcast(FP4X4),
+                    rhs_scale=ks[o][:, j * PAGE : (j + 1) * PAGE],
+                    start=(o == 0),
+                    stop=(o == PASSES - 1),
+                )
+            nc.scalar.copy(scores[b][:, e * PAGE : (e + 1) * PAGE], bank[:])
 
         ps = []
         for b in range(B):
             z = work.tile([P, N], F32, name="z")
             nc.vector.tensor_tensor(z[:], kb_win[:].indirect(off_t[:, b * cols : (b + 1) * cols]), scores[b][:], ALU.add)
-            p = work.tile([P, N], F32, name="p", tag="p", align_bytes=64)
+            p = work.tile([P, N], F32, name="p")
             nc.scalar.activation(p[:], z[:], ACT.Silu)
             ps.append(p)
 
-        pcols = PAGE // 16
         wis = []
         wq = []
 
@@ -152,21 +150,14 @@ def tile_attend_pkv4q_silu_kb_gate_kernel(
             nc.vector.tensor_tensor(
                 w[:], vs_win[:].indirect(off_t[:, j * pcols : (j + 1) * pcols]), ps[b][:, e * PAGE : (e + 1) * PAGE], ALU.mult
             )
-            bank = psum.tile([P, 4, NQ], F32, name="tr", bufs=3)
+            turned = psum.tile([P, 4, NQ], F32, name="turned", bufs=3)
             for t in range(4):
-                nc.tensor.transpose(bank[:, t, :], w[:, t:PAGE:4], ident[:])
+                nc.tensor.transpose(turned[:, t, :], w[:, t:PAGE:4], ident[:])
             wi = work.tile([P, 4 * NQ], BF16, name="wi", bufs=4, align_bytes=64)
-            nc.scalar.copy(wi[:].rearrange("p (q t) -> p q t", t=4), bank[:].rearrange("p t q -> p q t"))
+            nc.scalar.copy(wi[:].rearrange("p (q t) -> p q t", t=4), turned[:].rearrange("p t q -> p q t"))
             wis.append(wi)
-            if j >= 2:
-                quantise(j - 2)
 
-        vsc = work.tile([P, B * PAGES * DV], U8, name="vsc", tag="p", align_bytes=64)
-        nc.vector.tensor_copy(vsc[:], vsc_win[:].indirect(voff_t[:]))
-        quantise(2)
-        quantise(3)
-
-        for b in range(B):
+        def weigh_values(b, vsc):
             y = psum.tile([P, DV], F32, name="y", bufs=2)
             for e in range(PAGES):
                 j = b * PAGES + e
@@ -175,10 +166,27 @@ def tile_attend_pkv4q_silu_kb_gate_kernel(
                     lhsT=wq[j][0][:].bitcast(FP8X4),
                     lhsT_scale=wq[j][1][:],
                     rhs=vw[:, j * DV : (j + 1) * DV].bitcast(FP8X4),
-                    rhs_scale=vsc[:, j * DV : (j + 1) * DV],
+                    rhs_scale=vsc[:, e * DV : (e + 1) * DV],
                     start=(e == 0),
                     stop=(e == PAGES - 1),
                 )
+            return y
+
+        def finish(b, y):
             res = work.tile([P, DV], F32, name="res")
             nc.vector.scalar_tensor_tensor(res[:], y[:], 1.0 / 16.0, gate[:, b, :], ALU.mult, ALU.mult)
             nc.sync.dma_start(out[b], res[:])
+
+        vcols = PAGES * DV // 16
+        quantise(0)
+        quantise(1)
+        vsc0 = shared.tile([P, PAGES * DV], U8, name="vsc0", offset=0, align_bytes=64)
+        nc.vector.tensor_copy(vsc0[:], vsc_win[:].indirect(voff_t[:, 0:vcols]))
+        y0 = weigh_values(0, vsc0)
+        quantise(2)
+        vsc1 = shared.tile([P, PAGES * DV], U8, name="vsc1", offset=512, align_bytes=64)
+        nc.vector.tensor_copy(vsc1[:], vsc_win[:].indirect(voff_t[:, vcols : 2 * vcols]))
+        finish(0, y0)
+        quantise(3)
+        y1 = weigh_values(1, vsc1)
+        finish(1, y1)

@@ -31,36 +31,33 @@ def tile_attend_pkv4q_silu_kb_gate_kernel(
         lists = ctx.enter_context(tc.tile_pool(name="lists", bufs=1))
         keep = ctx.enter_context(tc.tile_pool(name="keep", bufs=1))
         shared = ctx.enter_context(tc.tile_pool(name="shared", bufs=1))
+        late = ctx.enter_context(tc.tile_pool(name="late", bufs=1))
+        last = ctx.enter_context(tc.tile_pool(name="last", bufs=1))
         work = ctx.enter_context(tc.tile_pool(name="work", bufs=2))
         psum = ctx.enter_context(tc.psum_pool(name="psum", bufs=1))
 
-        voff_t = lists.tile([P, B * PAGES * DV // 16], U16, name="voff_t")
-        nc.sync.dma_start(voff_t[:], voffs)
         off_t = lists.tile([P, B * N // 16], U16, name="off_t")
         nc.sync.dma_start(off_t[:], offs)
-        vw_win = keep.tile([P, POOL_PAGES * DV], U32, name="vw_win", tag="win_a", align_bytes=64)
-        nc.sync.dma_start(
-            vw_win[:].bitcast(I32).rearrange("p (u e) -> p u e", u=POOL_PAGES),
-            v_words.rearrange("u p e r -> p u (e r)").bitcast(I32),
-        )
-        kw_win = keep.tile([P, T], U32, name="kw_win", align_bytes=64)
+        kw_win = late.tile([P, T], U32, name="kw_win", offset=8192, align_bytes=64)
         nc.sync.dma_start(kw_win[:].bitcast(I32), k_words[0].rearrange("p t r -> p (t r)").bitcast(I32))
+        voff_t = lists.tile([P, B * PAGES * DV // 16], U16, name="voff_t")
+        nc.sync.dma_start(voff_t[:], voffs)
         qw = keep.tile([P, B * PASSES * NQ], U32, name="qw", align_bytes=64)
         nc.sync.dma_start(
             qw[:].bitcast(I32).rearrange("p (g q) -> p g q", q=NQ),
             q_words.rearrange("b o p q r -> p (b o) (q r)").bitcast(I32),
         )
-        og_t = keep.tile([P, B, DV], F32, name="og_t")
-        nc.sync.dma_start(og_t[:], og.rearrange("b q e -> q b e"))
 
-        ks_win = shared.tile([P, T], U8, name="ks_win", offset=0, align_bytes=64)
+        og_t = keep.tile([P, B, DV], F32, name="og_t")
+        nc.gpsimd.dma_start(og_t[:], og.rearrange("b q e -> q b e"))
+
+        ks_win = shared.tile([P, T], U8, name="ks_win", offset=15360, align_bytes=64)
         nc.vector.memset(ks_win[:].bitcast(I32), 0)
         for quad in range(4):
             nc.scalar.dma_start(
                 ks_win[32 * quad : 32 * quad + 8, :].bitcast(I32),
                 k_scales[:, 4 * quad : 4 * quad + 4, :].bitcast(I32),
             )
-
         vsc_win = keep.tile([P, POOL_PAGES * DV], U8, name="vsc_win", align_bytes=64)
         nc.vector.memset(vsc_win[:].bitcast(I32), 0)
         for quad in range(4):
@@ -80,33 +77,26 @@ def tile_attend_pkv4q_silu_kb_gate_kernel(
         ident = keep.tile([P, P], F32, name="ident")
         make_identity(nc, ident[:])
 
-        gate = keep.tile([P, B, DV], F32, name="gate")
-        nc.scalar.activation(gate[:], og_t[:], ACT.Sigmoid)
-        warm = keep.tile([P, 1], F32, name="warm")
-        nc.scalar.activation(warm[:], gate[:, 0, 0:1], ACT.Silu)
-
-        vw = keep.tile([P, B * PAGES * DV], U32, name="vw", align_bytes=64)
-        nc.vector.tensor_copy(vw[:], vw_win[:].indirect(voff_t[:]))
-        kb_win = keep.tile([P, T], F32, name="kb_win", tag="win_a", align_bytes=64)
-        nc.sync.dma_start(kb_win[:], kb)
-
         ks0 = keep.tile([P, B * N], U8, name="ks0", align_bytes=64)
         nc.vector.tensor_copy(ks0[:], ks_win[:].indirect(off_t[:]))
         for quad in range(4):
-            nc.scalar.dma_start(
+            nc.sync.dma_start(
                 ks1[32 * quad : 32 * quad + 4, :].bitcast(I32),
                 ks0[32 * quad + 4 : 32 * quad + 8, :].bitcast(I32),
             )
-        vs_win = shared.tile([P, T], F32, name="vs_win", offset=0, align_bytes=64)
-        nc.sync.dma_start(vs_win[:], vs)
+        kb_win = shared.tile([P, T], F32, name="kb_win", offset=0, align_bytes=64)
+        nc.sync.dma_start(kb_win[:], kb)
         ks = (ks0, ks1)
+
+        gate = keep.tile([P, B, DV], F32, name="gate")
+        nc.scalar.activation(gate[:], og_t[:], ACT.Sigmoid)
 
         pcols = PAGE // 16
         cols = N // 16
         scores = [work.tile([P, N], F32, name="a") for b in range(B)]
         for j in range(B * PAGES):
             b, e = divmod(j, PAGES)
-            kw = work.tile([P, PAGE], U32, name="kw", align_bytes=64)
+            kw = shared.tile([P, PAGE], U32, name="kw", offset=16384, bufs=2, align_bytes=64)
             nc.vector.tensor_copy(kw[:], kw_win[:].indirect(off_t[:, j * pcols : (j + 1) * pcols]))
             kp = work.tile([P, PASSES * PAGE], U16, name="kp", bufs=4, align_bytes=64)
             nc.vector.tensor_copy(
@@ -114,7 +104,7 @@ def tile_attend_pkv4q_silu_kb_gate_kernel(
                 kw[:].bitcast(U16).rearrange("p (n o) -> p o n", o=PASSES),
             )
             bank = psum.tile([P, PAGE], F32, name="sc", bufs=3)
-            for o in range(PASSES):
+            for o in reversed(range(PASSES)):
                 g = b * PASSES + o
                 nc.tensor.matmul_mx(
                     out=bank[:],
@@ -122,10 +112,18 @@ def tile_attend_pkv4q_silu_kb_gate_kernel(
                     lhsT_scale=qs[:, g * NQ : (g + 1) * NQ],
                     rhs=kp[:, o * PAGE : (o + 1) * PAGE].bitcast(FP4X4),
                     rhs_scale=ks[o][:, j * PAGE : (j + 1) * PAGE],
-                    start=(o == 0),
-                    stop=(o == PASSES - 1),
+                    start=(o == PASSES - 1),
+                    stop=(o == 0),
                 )
             nc.scalar.copy(scores[b][:, e * PAGE : (e + 1) * PAGE], bank[:])
+
+        vs_win = late.tile([P, T], F32, name="vs_win", offset=0, align_bytes=64)
+        nc.sync.dma_start(vs_win[:], vs)
+        vw_win = late.tile([P, POOL_PAGES * DV], U32, name="vw_win", offset=16384, align_bytes=64)
+        nc.sync.dma_start(
+            vw_win[:].bitcast(I32).rearrange("p (u e) -> p u e", u=POOL_PAGES),
+            v_words.rearrange("u p e r -> p u (e r)").bitcast(I32),
+        )
 
         ps = []
         for b in range(B):
@@ -134,6 +132,9 @@ def tile_attend_pkv4q_silu_kb_gate_kernel(
             p = work.tile([P, N], F32, name="p")
             nc.scalar.activation(p[:], z[:], ACT.Silu)
             ps.append(p)
+
+        vsc = shared.tile([P, B * PAGES * DV], U8, name="vsc", offset=0, align_bytes=64)
+        nc.vector.tensor_copy(vsc[:], vsc_win[:].indirect(voff_t[:]))
 
         wis = []
         wq = []
@@ -153,11 +154,11 @@ def tile_attend_pkv4q_silu_kb_gate_kernel(
             turned = psum.tile([P, 4, NQ], F32, name="turned", bufs=3)
             for t in range(4):
                 nc.tensor.transpose(turned[:, t, :], w[:, t:PAGE:4], ident[:])
-            wi = work.tile([P, 4 * NQ], BF16, name="wi", bufs=4, align_bytes=64)
+            wi = last.tile([P, 4 * NQ], BF16, name="wi%d" % j, offset=1024 * j, align_bytes=64)
             nc.scalar.copy(wi[:].rearrange("p (q t) -> p q t", t=4), turned[:].rearrange("p t q -> p q t"))
             wis.append(wi)
 
-        def weigh_values(b, vsc):
+        def weigh_values(b, pages):
             y = psum.tile([P, DV], F32, name="y", bufs=2)
             for e in range(PAGES):
                 j = b * PAGES + e
@@ -165,8 +166,8 @@ def tile_attend_pkv4q_silu_kb_gate_kernel(
                     out=y[:],
                     lhsT=wq[j][0][:].bitcast(FP8X4),
                     lhsT_scale=wq[j][1][:],
-                    rhs=vw[:, j * DV : (j + 1) * DV].bitcast(FP8X4),
-                    rhs_scale=vsc[:, e * DV : (e + 1) * DV],
+                    rhs=pages[e].bitcast(FP8X4),
+                    rhs_scale=vsc[:, j * DV : (j + 1) * DV],
                     start=(e == 0),
                     stop=(e == PAGES - 1),
                 )
@@ -177,16 +178,18 @@ def tile_attend_pkv4q_silu_kb_gate_kernel(
             nc.vector.scalar_tensor_tensor(res[:], y[:], 1.0 / 16.0, gate[:, b, :], ALU.mult, ALU.mult)
             nc.sync.dma_start(out[b], res[:])
 
-        vcols = PAGES * DV // 16
+        vcols = DV // 16
+        vw0 = late.tile([P, PAGES * DV], U32, name="vw0", offset=0, align_bytes=64)
+        nc.vector.tensor_copy(vw0[:], vw_win[:].indirect(voff_t[:, 0 : 2 * vcols]))
         quantise(0)
         quantise(1)
-        vsc0 = shared.tile([P, PAGES * DV], U8, name="vsc0", offset=0, align_bytes=64)
-        nc.vector.tensor_copy(vsc0[:], vsc_win[:].indirect(voff_t[:, 0:vcols]))
-        y0 = weigh_values(0, vsc0)
+        y0 = weigh_values(0, (vw0[:, 0:DV], vw0[:, DV : 2 * DV]))
+        vw2 = last.tile([P, DV], U32, name="vw2", offset=0, align_bytes=64)
+        nc.vector.tensor_copy(vw2[:], vw_win[:].indirect(voff_t[:, 2 * vcols : 3 * vcols]))
         quantise(2)
-        vsc1 = shared.tile([P, PAGES * DV], U8, name="vsc1", offset=512, align_bytes=64)
-        nc.vector.tensor_copy(vsc1[:], vsc_win[:].indirect(voff_t[:, vcols : 2 * vcols]))
-        finish(0, y0)
         quantise(3)
-        y1 = weigh_values(1, vsc1)
+        vw3 = last.tile([P, DV], U32, name="vw3", offset=2048, align_bytes=64)
+        nc.vector.tensor_copy(vw3[:], vw_win[:].indirect(voff_t[:, 3 * vcols : 4 * vcols]))
+        finish(0, y0)
+        y1 = weigh_values(1, (vw2[:], vw3[:]))
         finish(1, y1)

@@ -36,28 +36,15 @@ def tile_attend_pkv4q_silu_kb_gate_kernel(
         work = ctx.enter_context(tc.tile_pool(name="work", bufs=2))
         psum = ctx.enter_context(tc.psum_pool(name="psum", bufs=1))
 
-        off_t = lists.tile([P, B * N // 16], U16, name="off_t")
-        nc.sync.dma_start(off_t[:], offs)
-        kw_win = late.tile([P, T], U32, name="kw_win", offset=8192, align_bytes=64)
-        nc.sync.dma_start(kw_win[:].bitcast(I32), k_words[0].rearrange("p t r -> p (t r)").bitcast(I32))
         voff_t = lists.tile([P, B * PAGES * DV // 16], U16, name="voff_t")
         nc.sync.dma_start(voff_t[:], voffs)
-        qw = keep.tile([P, B * PASSES * NQ], U32, name="qw", align_bytes=64)
-        nc.sync.dma_start(
-            qw[:].bitcast(I32).rearrange("p (g q) -> p g q", q=NQ),
-            q_words.rearrange("b o p q r -> p (b o) (q r)").bitcast(I32),
-        )
+        off_t = lists.tile([P, B * N // 16], U16, name="off_t")
+        nc.sync.dma_start(off_t[:], offs)
+        og_t = late.tile([P, B, DV], F32, name="og_t", offset=23552, align_bytes=64)
+        nc.scalar.dma_start(og_t[:], og.rearrange("b q e -> q b e"))
+        gate = keep.tile([P, B, DV], F32, name="gate")
+        nc.scalar.activation(gate[:], og_t[:], ACT.Sigmoid)
 
-        og_t = keep.tile([P, B, DV], F32, name="og_t")
-        nc.gpsimd.dma_start(og_t[:], og.rearrange("b q e -> q b e"))
-
-        ks_win = shared.tile([P, T], U8, name="ks_win", offset=15360, align_bytes=64)
-        nc.vector.memset(ks_win[:].bitcast(I32), 0)
-        for quad in range(4):
-            nc.scalar.dma_start(
-                ks_win[32 * quad : 32 * quad + 8, :].bitcast(I32),
-                k_scales[:, 4 * quad : 4 * quad + 4, :].bitcast(I32),
-            )
         vsc_win = keep.tile([P, POOL_PAGES * DV], U8, name="vsc_win", align_bytes=64)
         nc.vector.memset(vsc_win[:].bitcast(I32), 0)
         for quad in range(4):
@@ -65,10 +52,17 @@ def tile_attend_pkv4q_silu_kb_gate_kernel(
                 vsc_win[32 * quad : 32 * quad + 4, :].bitcast(I32).rearrange("i (u e) -> i u e", u=POOL_PAGES),
                 v_scales[:, 4 * quad : 4 * quad + 4, :].rearrange("u i e -> i u e").bitcast(I32),
             )
+        ks_win = shared.tile([P, T], U8, name="ks_win", offset=15360, align_bytes=64)
+        nc.vector.memset(ks_win[:].bitcast(I32), 0)
+        for quad in range(4):
+            nc.sync.dma_start(
+                ks_win[32 * quad : 32 * quad + 8, :].bitcast(I32),
+                k_scales[:, 4 * quad : 4 * quad + 4, :].bitcast(I32),
+            )
         qs = keep.tile([P, B * PASSES * NQ], U8, name="qs", align_bytes=64)
         nc.vector.memset(qs[:].bitcast(I32), 0)
         for quad in range(4):
-            nc.scalar.dma_start(
+            nc.sync.dma_start(
                 qs[32 * quad : 32 * quad + 4, :].bitcast(I32).rearrange("i (g q) -> i g q", g=B * PASSES),
                 q_scales[:, :, 4 * quad : 4 * quad + 4, :].rearrange("b o i q -> i (b o) q").bitcast(I32),
             )
@@ -77,6 +71,16 @@ def tile_attend_pkv4q_silu_kb_gate_kernel(
         ident = keep.tile([P, P], F32, name="ident")
         make_identity(nc, ident[:])
 
+        kw_win = late.tile([P, T], U32, name="kw_win", offset=8192, align_bytes=64)
+        nc.sync.dma_start(kw_win[:].bitcast(I32), k_words[0].rearrange("p t r -> p (t r)").bitcast(I32))
+        qw = late.tile([P, B * PASSES * NQ], U32, name="qw", offset=24576, align_bytes=64)
+        nc.sync.dma_start(
+            qw[:].bitcast(I32).rearrange("p (g q) -> p g q", q=NQ),
+            q_words.rearrange("b o p q r -> p (b o) (q r)").bitcast(I32),
+        )
+
+        vsc = keep.tile([P, B * PAGES * DV], U8, name="vsc", align_bytes=64)
+        nc.vector.tensor_copy(vsc[:], vsc_win[:].indirect(voff_t[:]))
         ks0 = keep.tile([P, B * N], U8, name="ks0", align_bytes=64)
         nc.vector.tensor_copy(ks0[:], ks_win[:].indirect(off_t[:]))
         for quad in range(4):
@@ -87,9 +91,6 @@ def tile_attend_pkv4q_silu_kb_gate_kernel(
         kb_win = shared.tile([P, T], F32, name="kb_win", offset=0, align_bytes=64)
         nc.sync.dma_start(kb_win[:], kb)
         ks = (ks0, ks1)
-
-        gate = keep.tile([P, B, DV], F32, name="gate")
-        nc.scalar.activation(gate[:], og_t[:], ACT.Sigmoid)
 
         pcols = PAGE // 16
         cols = N // 16
@@ -130,11 +131,9 @@ def tile_attend_pkv4q_silu_kb_gate_kernel(
             z = work.tile([P, N], F32, name="z")
             nc.vector.tensor_tensor(z[:], kb_win[:].indirect(off_t[:, b * cols : (b + 1) * cols]), scores[b][:], ALU.add)
             p = work.tile([P, N], F32, name="p")
-            nc.scalar.activation(p[:], z[:], ACT.Silu)
+            for e in range(PAGES):
+                nc.scalar.activation(p[:, e * PAGE : (e + 1) * PAGE], z[:, e * PAGE : (e + 1) * PAGE], ACT.Silu)
             ps.append(p)
-
-        vsc = shared.tile([P, B * PAGES * DV], U8, name="vsc", offset=0, align_bytes=64)
-        nc.vector.tensor_copy(vsc[:], vsc_win[:].indirect(voff_t[:]))
 
         wis = []
         wq = []

@@ -22,6 +22,12 @@ FP4X4 = mybir.dt.float4_e2m1fn_x4
 ACT = mybir.ActivationFunctionType
 ALU = mybir.AluOpType
 
+QW_AT = 0
+KW_AT = QW_AT + 4 * B * PASSES * NQ
+KB_AT = KW_AT + 4 * T
+VS_AT = KB_AT + 4 * T
+VW_AT = VS_AT + 4 * T
+
 
 def tile_attend_pkv4q_silu_kb_gate_kernel(
     tc, q_words, q_scales, k_words, k_scales, v_words, v_scales, vs, kb, og, offs, voffs, out
@@ -30,7 +36,6 @@ def tile_attend_pkv4q_silu_kb_gate_kernel(
     with ExitStack() as ctx:
         lists = ctx.enter_context(tc.tile_pool(name="lists", bufs=1))
         keep = ctx.enter_context(tc.tile_pool(name="keep", bufs=1))
-        shared = ctx.enter_context(tc.tile_pool(name="shared", bufs=1))
         late = ctx.enter_context(tc.tile_pool(name="late", bufs=1))
         last = ctx.enter_context(tc.tile_pool(name="last", bufs=1))
         work = ctx.enter_context(tc.tile_pool(name="work", bufs=2))
@@ -40,7 +45,7 @@ def tile_attend_pkv4q_silu_kb_gate_kernel(
         nc.sync.dma_start(voff_t[:], voffs)
         off_t = lists.tile([P, B * N // 16], U16, name="off_t")
         nc.sync.dma_start(off_t[:], offs)
-        og_t = late.tile([P, B, DV], F32, name="og_t", offset=23552, align_bytes=64)
+        og_t = late.tile([P, B, DV], F32, name="og_t", offset=KW_AT - 1024, align_bytes=64)
         nc.scalar.dma_start(og_t[:], og.rearrange("b q e -> q b e"))
         gate = keep.tile([P, B, DV], F32, name="gate")
         nc.scalar.activation(gate[:], og_t[:], ACT.Sigmoid)
@@ -52,7 +57,7 @@ def tile_attend_pkv4q_silu_kb_gate_kernel(
                 vsc_win[32 * quad : 32 * quad + 4, :].bitcast(I32).rearrange("i (u e) -> i u e", u=POOL_PAGES),
                 v_scales[:, 4 * quad : 4 * quad + 4, :].rearrange("u i e -> i u e").bitcast(I32),
             )
-        ks_win = shared.tile([P, T], U8, name="ks_win", offset=15360, align_bytes=64)
+        ks_win = late.tile([P, T], U8, name="ks_win", offset=VS_AT - T // 2, align_bytes=64)
         nc.vector.memset(ks_win[:].bitcast(I32), 0)
         for quad in range(4):
             nc.sync.dma_start(
@@ -71,9 +76,9 @@ def tile_attend_pkv4q_silu_kb_gate_kernel(
         ident = keep.tile([P, P], F32, name="ident")
         make_identity(nc, ident[:])
 
-        kw_win = late.tile([P, T], U32, name="kw_win", offset=8192, align_bytes=64)
+        kw_win = late.tile([P, T], U32, name="kw_win", offset=KW_AT, align_bytes=64)
         nc.sync.dma_start(kw_win[:].bitcast(I32), k_words[0].rearrange("p t r -> p (t r)").bitcast(I32))
-        qw = late.tile([P, B * PASSES * NQ], U32, name="qw", offset=24576, align_bytes=64)
+        qw = late.tile([P, B * PASSES * NQ], U32, name="qw", offset=QW_AT, align_bytes=64)
         nc.sync.dma_start(
             qw[:].bitcast(I32).rearrange("p (g q) -> p g q", q=NQ),
             q_words.rearrange("b o p q r -> p (b o) (q r)").bitcast(I32),
@@ -88,17 +93,28 @@ def tile_attend_pkv4q_silu_kb_gate_kernel(
                 ks1[32 * quad : 32 * quad + 4, :].bitcast(I32),
                 ks0[32 * quad + 4 : 32 * quad + 8, :].bitcast(I32),
             )
-        kb_win = shared.tile([P, T], F32, name="kb_win", offset=0, align_bytes=64)
+        kb_win = late.tile([P, T], F32, name="kb_win", offset=KB_AT, align_bytes=64)
         nc.sync.dma_start(kb_win[:], kb)
+        vs_win = late.tile([P, T], F32, name="vs_win", offset=VS_AT, align_bytes=64)
+        nc.sync.dma_start(vs_win[:], vs)
         ks = (ks0, ks1)
 
         pcols = PAGE // 16
         cols = N // 16
         scores = [work.tile([P, N], F32, name="a") for b in range(B)]
+        kws = []
+
+        def gather_keys(j):
+            kw = late.tile([P, PAGE], U32, name="kw%d" % j, offset=VW_AT + 4 * POOL_PAGES * DV + 4 * PAGE * (j - 1), align_bytes=64)
+            nc.vector.tensor_copy(kw[:], kw_win[:].indirect(off_t[:, j * pcols : (j + 1) * pcols]))
+            kws.append(kw)
+
+        gather_keys(0)
         for j in range(B * PAGES):
             b, e = divmod(j, PAGES)
-            kw = shared.tile([P, PAGE], U32, name="kw", offset=16384, bufs=2, align_bytes=64)
-            nc.vector.tensor_copy(kw[:], kw_win[:].indirect(off_t[:, j * pcols : (j + 1) * pcols]))
+            if j + 1 < B * PAGES:
+                gather_keys(j + 1)
+            kw = kws[j]
             kp = work.tile([P, PASSES * PAGE], U16, name="kp", bufs=4, align_bytes=64)
             nc.vector.tensor_copy(
                 kp[:].rearrange("p (o n) -> p o n", o=PASSES),
@@ -118,9 +134,7 @@ def tile_attend_pkv4q_silu_kb_gate_kernel(
                 )
             nc.scalar.copy(scores[b][:, e * PAGE : (e + 1) * PAGE], bank[:])
 
-        vs_win = late.tile([P, T], F32, name="vs_win", offset=0, align_bytes=64)
-        nc.sync.dma_start(vs_win[:], vs)
-        vw_win = late.tile([P, POOL_PAGES * DV], U32, name="vw_win", offset=16384, align_bytes=64)
+        vw_win = late.tile([P, POOL_PAGES * DV], U32, name="vw_win", offset=VW_AT, align_bytes=64)
         nc.sync.dma_start(
             vw_win[:].bitcast(I32).rearrange("p (u e) -> p u e", u=POOL_PAGES),
             v_words.rearrange("u p e r -> p u (e r)").bitcast(I32),
@@ -178,7 +192,7 @@ def tile_attend_pkv4q_silu_kb_gate_kernel(
             nc.sync.dma_start(out[b], res[:])
 
         vcols = DV // 16
-        vw0 = late.tile([P, PAGES * DV], U32, name="vw0", offset=0, align_bytes=64)
+        vw0 = late.tile([P, PAGES * DV], U32, name="vw0", offset=VS_AT, align_bytes=64)
         nc.vector.tensor_copy(vw0[:], vw_win[:].indirect(voff_t[:, 0 : 2 * vcols]))
         quantise(0)
         quantise(1)

@@ -23,10 +23,12 @@ ACT = mybir.ActivationFunctionType
 ALU = mybir.AluOpType
 
 QW_AT = 0
+SPREAD = 3 * T // 4
+RUN = SPREAD // P
 KW_AT = QW_AT + 4 * B * PASSES * NQ
-KB_AT = KW_AT + 4 * T
-VS_AT = KB_AT + 4 * T
-VW_AT = VS_AT + 4 * T
+VS_AT = KW_AT + 4 * T
+KB_AT = VS_AT + 4 * T
+VW_AT = KB_AT + 4 * T
 
 
 def tile_attend_pkv4q_silu_kb_gate_kernel(
@@ -45,6 +47,8 @@ def tile_attend_pkv4q_silu_kb_gate_kernel(
         nc.sync.dma_start(voff_t[:], voffs)
         off_t = lists.tile([P, B * N // 16], U16, name="off_t")
         nc.sync.dma_start(off_t[:], offs)
+        kb_col = keep.tile([P, RUN], F32, name="kb_col", align_bytes=64)
+        nc.gpsimd.dma_start(kb_col[:], kb[0, 0:SPREAD].rearrange("(c m) -> c m", c=P))
         og_t = late.tile([P, B, DV], F32, name="og_t", offset=KW_AT - 1024, align_bytes=64)
         nc.scalar.dma_start(og_t[:], og.rearrange("b q e -> q b e"))
         gate = keep.tile([P, B, DV], F32, name="gate")
@@ -57,7 +61,7 @@ def tile_attend_pkv4q_silu_kb_gate_kernel(
                 vsc_win[32 * quad : 32 * quad + 4, :].bitcast(I32).rearrange("i (u e) -> i u e", u=POOL_PAGES),
                 v_scales[:, 4 * quad : 4 * quad + 4, :].rearrange("u i e -> i u e").bitcast(I32),
             )
-        ks_win = late.tile([P, T], U8, name="ks_win", offset=VS_AT - T // 2, align_bytes=64)
+        ks_win = late.tile([P, T], U8, name="ks_win", offset=KB_AT - T // 2, align_bytes=64)
         nc.vector.memset(ks_win[:].bitcast(I32), 0)
         for quad in range(4):
             nc.sync.dma_start(
@@ -94,7 +98,7 @@ def tile_attend_pkv4q_silu_kb_gate_kernel(
                 ks0[32 * quad + 4 : 32 * quad + 8, :].bitcast(I32),
             )
         kb_win = late.tile([P, T], F32, name="kb_win", offset=KB_AT, align_bytes=64)
-        nc.sync.dma_start(kb_win[:], kb)
+        nc.sync.dma_start(kb_win[:, SPREAD:T], kb[:, SPREAD:T])
         vs_win = late.tile([P, T], F32, name="vs_win", offset=VS_AT, align_bytes=64)
         nc.sync.dma_start(vs_win[:], vs)
         ks = (ks0, ks1)
@@ -133,6 +137,16 @@ def tile_attend_pkv4q_silu_kb_gate_kernel(
                     stop=(o == 0),
                 )
             nc.scalar.copy(scores[b][:, e * PAGE : (e + 1) * PAGE], bank[:])
+
+        for g in range(RUN // 4):
+            bank = psum.tile([P, 4, P], F32, name="turned", bufs=3)
+            for t in range(4):
+                m = 4 * g + t
+                nc.tensor.transpose(bank[:, t, :], kb_col[:, m : m + 1].to_broadcast([P, P]), ident[:])
+            nc.scalar.copy(
+                kb_win[:, 0:SPREAD].rearrange("p (c m) -> p c m", c=P)[:, :, 4 * g : 4 * g + 4],
+                bank[:].rearrange("p t c -> p c t"),
+            )
 
         vw_win = late.tile([P, POOL_PAGES * DV], U32, name="vw_win", offset=VW_AT, align_bytes=64)
         nc.sync.dma_start(

@@ -23,12 +23,15 @@ ACT = mybir.ActivationFunctionType
 ALU = mybir.AluOpType
 
 QW_AT = 0
-SPREAD = 3 * T // 4
-RUN = SPREAD // P
+RUN = T // P
 KW_AT = QW_AT + 4 * B * PASSES * NQ
 VS_AT = KW_AT + 4 * T
-KB_AT = VS_AT + 4 * T
+VSC_AT = VS_AT + 4 * T - 1024
+KB_AT = VSC_AT + POOL_PAGES * DV
+KS_ROWS = 16 * PASSES
+VS_ROWS = 16
 VW_AT = KB_AT + 4 * T
+KS_AT = VW_AT + 4 * POOL_PAGES * DV + 4 * PAGE * (B * PAGES - 1)
 
 
 def tile_attend_pkv4q_silu_kb_gate_kernel(
@@ -43,43 +46,22 @@ def tile_attend_pkv4q_silu_kb_gate_kernel(
         work = ctx.enter_context(tc.tile_pool(name="work", bufs=2))
         psum = ctx.enter_context(tc.psum_pool(name="psum", bufs=1))
 
-        voff_t = lists.tile([P, B * PAGES * DV // 16], U16, name="voff_t")
-        nc.sync.dma_start(voff_t[:], voffs)
         off_t = lists.tile([P, B * N // 16], U16, name="off_t")
         nc.sync.dma_start(off_t[:], offs)
+        ks_win = late.tile([P, T], U8, name="ks_win", offset=KS_AT, align_bytes=64)
+        nc.sync.dma_start(
+            ks_win[P - KS_ROWS : P, :].bitcast(I32),
+            k_scales.rearrange("o f t -> f o t").bitcast(I32),
+        )
+        voff_t = lists.tile([P, B * PAGES * DV // 16], U16, name="voff_t")
+        nc.sync.dma_start(voff_t[:], voffs)
+        vsc_win = late.tile([P, POOL_PAGES * DV], U8, name="vsc_win", offset=VSC_AT, align_bytes=64)
+        nc.sync.dma_start(
+            vsc_win[P - VS_ROWS : P, :].bitcast(I32).rearrange("f (u e) -> f u e", u=POOL_PAGES),
+            v_scales.rearrange("u f e -> f u e").bitcast(I32),
+        )
         kb_col = keep.tile([P, RUN], F32, name="kb_col", align_bytes=64)
-        nc.gpsimd.dma_start(kb_col[:], kb[0, 0:SPREAD].rearrange("(c m) -> c m", c=P))
-        og_t = late.tile([P, B, DV], F32, name="og_t", offset=KW_AT - 1024, align_bytes=64)
-        nc.scalar.dma_start(og_t[:], og.rearrange("b q e -> q b e"))
-        gate = keep.tile([P, B, DV], F32, name="gate")
-        nc.scalar.activation(gate[:], og_t[:], ACT.Sigmoid)
-
-        vsc_win = keep.tile([P, POOL_PAGES * DV], U8, name="vsc_win", align_bytes=64)
-        nc.vector.memset(vsc_win[:].bitcast(I32), 0)
-        for quad in range(4):
-            nc.sync.dma_start(
-                vsc_win[32 * quad : 32 * quad + 4, :].bitcast(I32).rearrange("i (u e) -> i u e", u=POOL_PAGES),
-                v_scales[:, 4 * quad : 4 * quad + 4, :].rearrange("u i e -> i u e").bitcast(I32),
-            )
-        ks_win = late.tile([P, T], U8, name="ks_win", offset=KB_AT - T // 2, align_bytes=64)
-        nc.vector.memset(ks_win[:].bitcast(I32), 0)
-        for quad in range(4):
-            nc.sync.dma_start(
-                ks_win[32 * quad : 32 * quad + 8, :].bitcast(I32),
-                k_scales[:, 4 * quad : 4 * quad + 4, :].bitcast(I32),
-            )
-        qs = keep.tile([P, B * PASSES * NQ], U8, name="qs", align_bytes=64)
-        nc.vector.memset(qs[:].bitcast(I32), 0)
-        for quad in range(4):
-            nc.sync.dma_start(
-                qs[32 * quad : 32 * quad + 4, :].bitcast(I32).rearrange("i (g q) -> i g q", g=B * PASSES),
-                q_scales[:, :, 4 * quad : 4 * quad + 4, :].rearrange("b o i q -> i (b o) q").bitcast(I32),
-            )
-        ks1 = keep.tile([P, B * N], U8, name="ks1", align_bytes=64)
-        nc.vector.memset(ks1[:].bitcast(I32), 0)
-        ident = keep.tile([P, P], F32, name="ident")
-        make_identity(nc, ident[:])
-
+        nc.scalar.dma_start(kb_col[:], kb[0, :].rearrange("(c m) -> c m", c=P))
         kw_win = late.tile([P, T], U32, name="kw_win", offset=KW_AT, align_bytes=64)
         nc.sync.dma_start(kw_win[:].bitcast(I32), k_words[0].rearrange("p t r -> p (t r)").bitcast(I32))
         qw = late.tile([P, B * PASSES * NQ], U32, name="qw", offset=QW_AT, align_bytes=64)
@@ -87,21 +69,46 @@ def tile_attend_pkv4q_silu_kb_gate_kernel(
             qw[:].bitcast(I32).rearrange("p (g q) -> p g q", q=NQ),
             q_words.rearrange("b o p q r -> p (b o) (q r)").bitcast(I32),
         )
+        ident = keep.tile([P, P], F32, name="ident")
+        make_identity(nc, ident[:])
 
-        vsc = keep.tile([P, B * PAGES * DV], U8, name="vsc", align_bytes=64)
-        nc.vector.tensor_copy(vsc[:], vsc_win[:].indirect(voff_t[:]))
-        ks0 = keep.tile([P, B * N], U8, name="ks0", align_bytes=64)
-        nc.vector.tensor_copy(ks0[:], ks_win[:].indirect(off_t[:]))
+        nc.vector.memset(ks_win[0 : P - KS_ROWS, :].bitcast(I32), 0)
+        nc.vector.memset(vsc_win[0 : P - VS_ROWS, :].bitcast(I32), 0)
+        qs = keep.tile([P, B * PASSES * NQ], U8, name="qs", align_bytes=64)
+        nc.vector.memset(qs[:].bitcast(I32), 0)
         for quad in range(4):
             nc.sync.dma_start(
-                ks1[32 * quad : 32 * quad + 4, :].bitcast(I32),
-                ks0[32 * quad + 4 : 32 * quad + 8, :].bitcast(I32),
+                qs[32 * quad : 32 * quad + 4, :].bitcast(I32).rearrange("i (g q) -> i g q", g=B * PASSES),
+                q_scales[:, :, 4 * quad : 4 * quad + 4, :].rearrange("b o i q -> i (b o) q").bitcast(I32),
+            )
+
+        og_t = keep.tile([P, B, DV], F32, name="og_t", align_bytes=64)
+        nc.sync.dma_start(og_t[:], og.rearrange("b q e -> q b e"))
+        gate = keep.tile([P, B, DV], F32, name="gate")
+        nc.scalar.activation(gate[:], og_t[:], ACT.Sigmoid)
+
+        ks_rows = keep.tile([P, B * N], U8, name="ks_rows", align_bytes=64)
+        nc.vector.tensor_copy(ks_rows[:], ks_win[:].indirect(off_t[:]))
+        ks = late.tile([P, PASSES * B * N], U8, name="ks", offset=KS_AT, align_bytes=64)
+        for quad in range(4):
+            first = P - KS_ROWS + 4 * PASSES * quad
+            nc.sync.dma_start(
+                ks[32 * quad : 32 * quad + 4, :].bitcast(I32),
+                ks_rows[first : first + 4 * PASSES, :].bitcast(I32),
             )
         kb_win = late.tile([P, T], F32, name="kb_win", offset=KB_AT, align_bytes=64)
-        nc.sync.dma_start(kb_win[:, SPREAD:T], kb[:, SPREAD:T])
+
+        vsc_rows = keep.tile([P, B * PAGES * DV], U8, name="vsc_rows", align_bytes=64)
+        nc.vector.tensor_copy(vsc_rows[:], vsc_win[:].indirect(voff_t[:]))
         vs_win = late.tile([P, T], F32, name="vs_win", offset=VS_AT, align_bytes=64)
         nc.sync.dma_start(vs_win[:], vs)
-        ks = (ks0, ks1)
+        vsc = late.tile([P, B * PAGES * DV], U8, name="vsc", offset=VSC_AT + 1024, align_bytes=64)
+        for quad in range(4):
+            first = P - VS_ROWS + 4 * quad
+            nc.sync.dma_start(
+                vsc[32 * quad : 32 * quad + 4, :].bitcast(I32),
+                vsc_rows[first : first + 4, :].bitcast(I32),
+            )
 
         pcols = PAGE // 16
         cols = N // 16
@@ -132,7 +139,7 @@ def tile_attend_pkv4q_silu_kb_gate_kernel(
                     lhsT=qw[:, g * NQ : (g + 1) * NQ].bitcast(FP8X4),
                     lhsT_scale=qs[:, g * NQ : (g + 1) * NQ],
                     rhs=kp[:, o * PAGE : (o + 1) * PAGE].bitcast(FP4X4),
-                    rhs_scale=ks[o][:, j * PAGE : (j + 1) * PAGE],
+                    rhs_scale=ks[:, o * B * N + j * PAGE : o * B * N + (j + 1) * PAGE],
                     start=(o == PASSES - 1),
                     stop=(o == 0),
                 )
@@ -144,7 +151,7 @@ def tile_attend_pkv4q_silu_kb_gate_kernel(
                 m = 4 * g + t
                 nc.tensor.transpose(bank[:, t, :], kb_col[:, m : m + 1].to_broadcast([P, P]), ident[:])
             nc.scalar.copy(
-                kb_win[:, 0:SPREAD].rearrange("p (c m) -> p c m", c=P)[:, :, 4 * g : 4 * g + 4],
+                kb_win[:].rearrange("p (c m) -> p c m", c=P)[:, :, 4 * g : 4 * g + 4],
                 bank[:].rearrange("p t c -> p c t"),
             )
 

@@ -22,16 +22,14 @@ FP4X4 = mybir.dt.float4_e2m1fn_x4
 ACT = mybir.ActivationFunctionType
 ALU = mybir.AluOpType
 
-QW_AT = 0
 RUN = T // P
-KW_AT = QW_AT + 4 * B * PASSES * NQ
-VS_AT = KW_AT + 4 * T
-VSC_AT = VS_AT + 4 * T - 1024
-KB_AT = VSC_AT + POOL_PAGES * DV
+VS_AT = 0
+OG_AT = VS_AT + 4 * T
+KS_AT = OG_AT - 1024
+VW_AT = OG_AT + 4 * B * DV
+VSC_AT = VW_AT + 4 * POOL_PAGES * DV
 KS_ROWS = 16 * PASSES
 VS_ROWS = 16
-VW_AT = KB_AT + 4 * T
-KS_AT = VW_AT + 4 * POOL_PAGES * DV + 4 * PAGE * (B * PAGES - 1)
 
 
 def tile_attend_pkv4q_silu_kb_gate_kernel(
@@ -42,17 +40,25 @@ def tile_attend_pkv4q_silu_kb_gate_kernel(
         lists = ctx.enter_context(tc.tile_pool(name="lists", bufs=1))
         keep = ctx.enter_context(tc.tile_pool(name="keep", bufs=1))
         late = ctx.enter_context(tc.tile_pool(name="late", bufs=1))
-        last = ctx.enter_context(tc.tile_pool(name="last", bufs=1))
         work = ctx.enter_context(tc.tile_pool(name="work", bufs=2))
         psum = ctx.enter_context(tc.psum_pool(name="psum", bufs=1))
 
-        off_t = lists.tile([P, B * N // 16], U16, name="off_t")
-        nc.sync.dma_start(off_t[:], offs)
+        qs = keep.tile([P, B * PASSES * NQ], U8, name="qs", align_bytes=64)
+        nc.gpsimd.memset(qs[:].bitcast(I32), 0)
+        kb_col = keep.tile([P, RUN], F32, name="kb_col", align_bytes=64)
+        nc.gpsimd.dma_start(kb_col[:], kb[0, :].rearrange("(c m) -> c m", c=P))
+        ident = keep.tile([P, P], F32, name="ident")
+        make_identity(nc, ident[:])
+        warm = keep.tile([P, 1], F32, name="warm")
+        nc.scalar.activation(warm[:], ident[:, 0:1], ACT.Silu)
+
         ks_win = late.tile([P, T], U8, name="ks_win", offset=KS_AT, align_bytes=64)
         nc.sync.dma_start(
             ks_win[P - KS_ROWS : P, :].bitcast(I32),
             k_scales.rearrange("o f t -> f o t").bitcast(I32),
         )
+        off_t = lists.tile([P, B * N // 16], U16, name="off_t")
+        nc.sync.dma_start(off_t[:], offs)
         voff_t = lists.tile([P, B * PAGES * DV // 16], U16, name="voff_t")
         nc.sync.dma_start(voff_t[:], voffs)
         vsc_win = late.tile([P, POOL_PAGES * DV], U8, name="vsc_win", offset=VSC_AT, align_bytes=64)
@@ -60,49 +66,45 @@ def tile_attend_pkv4q_silu_kb_gate_kernel(
             vsc_win[P - VS_ROWS : P, :].bitcast(I32).rearrange("f (u e) -> f u e", u=POOL_PAGES),
             v_scales.rearrange("u f e -> f u e").bitcast(I32),
         )
-        kb_col = keep.tile([P, RUN], F32, name="kb_col", align_bytes=64)
-        nc.scalar.dma_start(kb_col[:], kb[0, :].rearrange("(c m) -> c m", c=P))
-        kw_win = late.tile([P, T], U32, name="kw_win", offset=KW_AT, align_bytes=64)
-        nc.sync.dma_start(kw_win[:].bitcast(I32), k_words[0].rearrange("p t r -> p (t r)").bitcast(I32))
-        qw = late.tile([P, B * PASSES * NQ], U32, name="qw", offset=QW_AT, align_bytes=64)
-        nc.sync.dma_start(
-            qw[:].bitcast(I32).rearrange("p (g q) -> p g q", q=NQ),
-            q_words.rearrange("b o p q r -> p (b o) (q r)").bitcast(I32),
-        )
-        ident = keep.tile([P, P], F32, name="ident")
-        make_identity(nc, ident[:])
-
-        nc.vector.memset(ks_win[0 : P - KS_ROWS, :].bitcast(I32), 0)
-        nc.vector.memset(vsc_win[0 : P - VS_ROWS, :].bitcast(I32), 0)
-        qs = keep.tile([P, B * PASSES * NQ], U8, name="qs", align_bytes=64)
-        nc.vector.memset(qs[:].bitcast(I32), 0)
         for quad in range(4):
             nc.sync.dma_start(
                 qs[32 * quad : 32 * quad + 4, :].bitcast(I32).rearrange("i (g q) -> i g q", g=B * PASSES),
                 q_scales[:, :, 4 * quad : 4 * quad + 4, :].rearrange("b o i q -> i (b o) q").bitcast(I32),
             )
+        kw_win = keep.tile([P, T], U32, name="kw_win", align_bytes=64)
+        nc.sync.dma_start(kw_win[:].bitcast(I32), k_words[0].rearrange("p t r -> p (t r)").bitcast(I32))
+        qw = keep.tile([P, B * PASSES * NQ], U32, name="qw", align_bytes=64)
+        nc.sync.dma_start(
+            qw[:].bitcast(I32).rearrange("p (g q) -> p g q", q=NQ),
+            q_words.rearrange("b o p q r -> p (b o) (q r)").bitcast(I32),
+        )
 
-        og_t = keep.tile([P, B, DV], F32, name="og_t", align_bytes=64)
-        nc.sync.dma_start(og_t[:], og.rearrange("b q e -> q b e"))
-        gate = keep.tile([P, B, DV], F32, name="gate")
-        nc.scalar.activation(gate[:], og_t[:], ACT.Sigmoid)
+        nc.vector.memset(ks_win[0 : P - KS_ROWS, :].bitcast(I32), 0)
+        ks = keep.tile([P, PASSES * B * N], U8, name="ks", align_bytes=64)
+        nc.vector.memset(ks[:].bitcast(I32), 0)
+        nc.vector.memset(vsc_win[0 : P - VS_ROWS, :].bitcast(I32), 0)
 
         ks_rows = keep.tile([P, B * N], U8, name="ks_rows", align_bytes=64)
         nc.vector.tensor_copy(ks_rows[:], ks_win[:].indirect(off_t[:]))
-        ks = late.tile([P, PASSES * B * N], U8, name="ks", offset=KS_AT, align_bytes=64)
         for quad in range(4):
             first = P - KS_ROWS + 4 * PASSES * quad
             nc.sync.dma_start(
                 ks[32 * quad : 32 * quad + 4, :].bitcast(I32),
                 ks_rows[first : first + 4 * PASSES, :].bitcast(I32),
             )
-        kb_win = late.tile([P, T], F32, name="kb_win", offset=KB_AT, align_bytes=64)
+        vs_win = late.tile([P, T], F32, name="vs_win", offset=VS_AT, align_bytes=64)
+        nc.sync.dma_start(vs_win[:], vs)
+        og_t = late.tile([P, B, DV], F32, name="og_t", offset=OG_AT, align_bytes=64)
+        nc.sync.dma_start(og_t[:], og.rearrange("b q e -> q b e"))
+        vw_win = late.tile([P, POOL_PAGES * DV], U32, name="vw_win", offset=VW_AT, align_bytes=64)
+        nc.sync.dma_start(
+            vw_win[:].bitcast(I32).rearrange("p (u e) -> p u e", u=POOL_PAGES),
+            v_words.rearrange("u p e r -> p u (e r)").bitcast(I32),
+        )
 
         vsc_rows = keep.tile([P, B * PAGES * DV], U8, name="vsc_rows", align_bytes=64)
         nc.vector.tensor_copy(vsc_rows[:], vsc_win[:].indirect(voff_t[:]))
-        vs_win = late.tile([P, T], F32, name="vs_win", offset=VS_AT, align_bytes=64)
-        nc.sync.dma_start(vs_win[:], vs)
-        vsc = late.tile([P, B * PAGES * DV], U8, name="vsc", offset=VSC_AT + 1024, align_bytes=64)
+        vsc = late.tile([P, B * PAGES * DV], U8, name="vsc", offset=VSC_AT, align_bytes=64)
         for quad in range(4):
             first = P - VS_ROWS + 4 * quad
             nc.sync.dma_start(
@@ -110,41 +112,7 @@ def tile_attend_pkv4q_silu_kb_gate_kernel(
                 vsc_rows[first : first + 4, :].bitcast(I32),
             )
 
-        pcols = PAGE // 16
-        cols = N // 16
-        scores = [work.tile([P, N], F32, name="a") for b in range(B)]
-        kws = []
-
-        def gather_keys(j):
-            kw = late.tile([P, PAGE], U32, name="kw%d" % j, offset=VW_AT + 4 * POOL_PAGES * DV + 4 * PAGE * (j - 1), align_bytes=64)
-            nc.vector.tensor_copy(kw[:], kw_win[:].indirect(off_t[:, j * pcols : (j + 1) * pcols]))
-            kws.append(kw)
-
-        gather_keys(0)
-        for j in range(B * PAGES):
-            b, e = divmod(j, PAGES)
-            if j + 1 < B * PAGES:
-                gather_keys(j + 1)
-            kw = kws[j]
-            kp = work.tile([P, PASSES * PAGE], U16, name="kp", bufs=4, align_bytes=64)
-            nc.vector.tensor_copy(
-                kp[:].rearrange("p (o n) -> p o n", o=PASSES),
-                kw[:].bitcast(U16).rearrange("p (n o) -> p o n", o=PASSES),
-            )
-            bank = psum.tile([P, PAGE], F32, name="sc", bufs=3)
-            for o in reversed(range(PASSES)):
-                g = b * PASSES + o
-                nc.tensor.matmul_mx(
-                    out=bank[:],
-                    lhsT=qw[:, g * NQ : (g + 1) * NQ].bitcast(FP8X4),
-                    lhsT_scale=qs[:, g * NQ : (g + 1) * NQ],
-                    rhs=kp[:, o * PAGE : (o + 1) * PAGE].bitcast(FP4X4),
-                    rhs_scale=ks[:, o * B * N + j * PAGE : o * B * N + (j + 1) * PAGE],
-                    start=(o == PASSES - 1),
-                    stop=(o == 0),
-                )
-            nc.scalar.copy(scores[b][:, e * PAGE : (e + 1) * PAGE], bank[:])
-
+        kb_win = keep.tile([P, T], F32, name="kb_win", align_bytes=64)
         for g in range(RUN // 4):
             bank = psum.tile([P, 4, P], F32, name="turned", bufs=3)
             for t in range(4):
@@ -155,42 +123,65 @@ def tile_attend_pkv4q_silu_kb_gate_kernel(
                 bank[:].rearrange("p t c -> p c t"),
             )
 
-        vw_win = late.tile([P, POOL_PAGES * DV], U32, name="vw_win", offset=VW_AT, align_bytes=64)
-        nc.sync.dma_start(
-            vw_win[:].bitcast(I32).rearrange("p (u e) -> p u e", u=POOL_PAGES),
-            v_words.rearrange("u p e r -> p u (e r)").bitcast(I32),
-        )
+        pcols = PAGE // 16
+        kws, scores, ps, wis, wq = {}, {}, {}, {}, {}
 
-        ps = []
-        for b in range(B):
-            z = work.tile([P, N], F32, name="z")
-            nc.vector.tensor_tensor(z[:], kb_win[:].indirect(off_t[:, b * cols : (b + 1) * cols]), scores[b][:], ALU.add)
-            p = work.tile([P, N], F32, name="p")
-            for e in range(PAGES):
-                nc.scalar.activation(p[:, e * PAGE : (e + 1) * PAGE], z[:, e * PAGE : (e + 1) * PAGE], ACT.Silu)
-            ps.append(p)
+        def gather_keys(j):
+            kw = work.tile([P, PAGE], U32, name="kw", bufs=4, align_bytes=64)
+            nc.vector.tensor_copy(kw[:], kw_win[:].indirect(off_t[:, j * pcols : (j + 1) * pcols]))
+            kws[j] = kw
 
-        wis = []
-        wq = []
+        def score(j):
+            b = j // PAGES
+            kp = work.tile([P, PASSES * PAGE], U16, name="kp", bufs=4, align_bytes=64)
+            nc.vector.tensor_copy(
+                kp[:].rearrange("p (o n) -> p o n", o=PASSES),
+                kws[j][:].bitcast(U16).rearrange("p (n o) -> p o n", o=PASSES),
+            )
+            bank = psum.tile([P, PAGE], F32, name="sc", bufs=3)
+            for o in range(PASSES):
+                g = b * PASSES + o
+                nc.tensor.matmul_mx(
+                    out=bank[:],
+                    lhsT=qw[:, g * NQ : (g + 1) * NQ].bitcast(FP8X4),
+                    lhsT_scale=qs[:, g * NQ : (g + 1) * NQ],
+                    rhs=kp[:, o * PAGE : (o + 1) * PAGE].bitcast(FP4X4),
+                    rhs_scale=ks[:, o * B * N + j * PAGE : o * B * N + (j + 1) * PAGE],
+                    start=(o == 0),
+                    stop=(o == PASSES - 1),
+                )
+            a = work.tile([P, PAGE], F32, name="a", bufs=4)
+            nc.scalar.copy(a[:], bank[:])
+            scores[j] = a
+
+        def bias_and_silu(j):
+            z = work.tile([P, PAGE], F32, name="z", bufs=4)
+            nc.vector.tensor_tensor(z[:], kb_win[:].indirect(off_t[:, j * pcols : (j + 1) * pcols]), scores[j][:], ALU.add)
+            p = work.tile([P, PAGE], F32, name="p", bufs=4)
+            nc.scalar.activation(p[:], z[:], ACT.Silu)
+            ps[j] = p
+
+        def weigh(j):
+            w = work.tile([P, PAGE], F32, name="w", bufs=4)
+            nc.vector.tensor_tensor(w[:], vs_win[:].indirect(off_t[:, j * pcols : (j + 1) * pcols]), ps[j][:], ALU.mult)
+            turned = psum.tile([P, 4, NQ], F32, name="turned", bufs=3)
+            for t in range(4):
+                nc.tensor.transpose(turned[:, t, :], w[:, t:PAGE:4], ident[:])
+            wi = work.tile([P, 4 * NQ], BF16, name="wi", bufs=4, align_bytes=64)
+            nc.scalar.copy(wi[:].rearrange("p (q t) -> p q t", t=4), turned[:].rearrange("p t q -> p q t"))
+            wis[j] = wi
 
         def quantise(j):
             wc = work.tile([P, NQ], U32, name="wc", bufs=4, align_bytes=64)
             wsc = work.tile([P, NQ], U8, name="wsc", bufs=4, align_bytes=64)
             nc.vector.quantize_mx(out=wc[:].bitcast(FP8X4), scales=wsc[:], in_=wis[j][:])
-            wq.append((wc, wsc))
+            wq[j] = (wc, wsc)
 
-        for j in range(B * PAGES):
-            b, e = divmod(j, PAGES)
-            w = work.tile([P, PAGE], F32, name="w", bufs=4)
-            nc.vector.tensor_tensor(
-                w[:], vs_win[:].indirect(off_t[:, j * pcols : (j + 1) * pcols]), ps[b][:, e * PAGE : (e + 1) * PAGE], ALU.mult
-            )
-            turned = psum.tile([P, 4, NQ], F32, name="turned", bufs=3)
-            for t in range(4):
-                nc.tensor.transpose(turned[:, t, :], w[:, t:PAGE:4], ident[:])
-            wi = last.tile([P, 4 * NQ], BF16, name="wi%d" % j, offset=1024 * j, align_bytes=64)
-            nc.scalar.copy(wi[:].rearrange("p (q t) -> p q t", t=4), turned[:].rearrange("p t q -> p q t"))
-            wis.append(wi)
+        def gather_values(b):
+            vcols = PAGES * DV // 16
+            vw = work.tile([P, PAGES * DV], U32, name="vw", align_bytes=64)
+            nc.vector.tensor_copy(vw[:], vw_win[:].indirect(voff_t[:, b * vcols : (b + 1) * vcols]))
+            return (vw[:, 0:DV], vw[:, DV : 2 * DV])
 
         def weigh_values(b, pages):
             y = psum.tile([P, DV], F32, name="y", bufs=2)
@@ -209,21 +200,32 @@ def tile_attend_pkv4q_silu_kb_gate_kernel(
 
         def finish(b, y):
             res = work.tile([P, DV], F32, name="res")
-            nc.vector.scalar_tensor_tensor(res[:], y[:], 1.0 / 16.0, gate[:, b, :], ALU.mult, ALU.mult)
+            nc.vector.tensor_tensor(res[:], y[:], gate[:, b, :], ALU.mult)
             nc.sync.dma_start(out[b], res[:])
 
-        vcols = DV // 16
-        vw0 = late.tile([P, PAGES * DV], U32, name="vw0", offset=VS_AT, align_bytes=64)
-        nc.vector.tensor_copy(vw0[:], vw_win[:].indirect(voff_t[:, 0 : 2 * vcols]))
+        gather_keys(0)
+        for j in range(B * PAGES):
+            if j + 1 < B * PAGES:
+                gather_keys(j + 1)
+            score(j)
+        bias_and_silu(0)
+        for j in range(B * PAGES):
+            if j + 1 < B * PAGES:
+                bias_and_silu(j + 1)
+            weigh(j)
+
+        half = keep.tile([P, B, DV], F32, name="half")
+        nc.scalar.activation(half[:], og_t[:], ACT.Tanh, scale=0.5)
+        gate = keep.tile([P, B, DV], F32, name="gate")
+        nc.scalar.activation(gate[:], half[:], ACT.Copy, scale=1.0 / 32.0, bias=1.0 / 32.0)
+
+        values0 = gather_values(0)
         quantise(0)
         quantise(1)
-        y0 = weigh_values(0, (vw0[:, 0:DV], vw0[:, DV : 2 * DV]))
-        vw2 = last.tile([P, DV], U32, name="vw2", offset=0, align_bytes=64)
-        nc.vector.tensor_copy(vw2[:], vw_win[:].indirect(voff_t[:, 2 * vcols : 3 * vcols]))
+        y0 = weigh_values(0, values0)
+        values1 = gather_values(1)
         quantise(2)
         quantise(3)
-        vw3 = last.tile([P, DV], U32, name="vw3", offset=2048, align_bytes=64)
-        nc.vector.tensor_copy(vw3[:], vw_win[:].indirect(voff_t[:, 3 * vcols : 4 * vcols]))
         finish(0, y0)
-        y1 = weigh_values(1, (vw2[:], vw3[:]))
+        y1 = weigh_values(1, values1)
         finish(1, y1)

@@ -23,11 +23,16 @@ ACT = mybir.ActivationFunctionType
 ALU = mybir.AluOpType
 
 RUN = T // P
+VS_SPREAD = T // 4
+VS_RUN = VS_SPREAD // P
 VS_AT = 0
-OG_AT = VS_AT + 4 * T
-KS_AT = OG_AT - 1024
+EDGE = 64
+KS_AT = VS_AT + 4 * T
+OG_AT = KS_AT + T
 VW_AT = OG_AT + 4 * B * DV
 VSC_AT = VW_AT + 4 * POOL_PAGES * DV
+P_AT = VSC_AT + POOL_PAGES * DV
+W_AT = P_AT + 4 * B * N
 KS_ROWS = 16 * PASSES
 VS_ROWS = 16
 
@@ -46,15 +51,18 @@ def tile_attend_pkv4q_silu_kb_gate_kernel(
         qs = keep.tile([P, B * PASSES * NQ], U8, name="qs", align_bytes=64)
         nc.gpsimd.memset(qs[:].bitcast(I32), 0)
         kb_col = keep.tile([P, RUN], F32, name="kb_col", align_bytes=64)
-        nc.gpsimd.dma_start(kb_col[:], kb[0, :].rearrange("(c m) -> c m", c=P))
+        nc.scalar.dma_start(kb_col[:], kb[0, :].rearrange("(c m) -> c m", c=P))
+        vs_col = keep.tile([P, VS_RUN], F32, name="vs_col", align_bytes=64)
+        nc.scalar.dma_start(vs_col[:], vs[0, 0:VS_SPREAD].rearrange("(c m) -> c m", c=P))
         ident = keep.tile([P, P], F32, name="ident")
         make_identity(nc, ident[:])
         warm = keep.tile([P, 1], F32, name="warm")
         nc.scalar.activation(warm[:], ident[:, 0:1], ACT.Silu)
 
-        ks_win = late.tile([P, T], U8, name="ks_win", offset=KS_AT, align_bytes=64)
+        ks_room = late.tile([P, EDGE + T + 4 * B * DV + EDGE], U8, name="ks_room", offset=KS_AT - EDGE, align_bytes=64)
+        ks_win = ks_room[:, EDGE : EDGE + T]
         nc.sync.dma_start(
-            ks_win[P - KS_ROWS : P, :].bitcast(I32),
+            ks_room[P - KS_ROWS : P, EDGE : EDGE + T].bitcast(I32),
             k_scales.rearrange("o f t -> f o t").bitcast(I32),
         )
         off_t = lists.tile([P, B * N // 16], U16, name="off_t")
@@ -66,36 +74,35 @@ def tile_attend_pkv4q_silu_kb_gate_kernel(
             vsc_win[P - VS_ROWS : P, :].bitcast(I32).rearrange("f (u e) -> f u e", u=POOL_PAGES),
             v_scales.rearrange("u f e -> f u e").bitcast(I32),
         )
+        kw_win = keep.tile([P, T], U32, name="kw_win", align_bytes=64)
+        nc.sync.dma_start(kw_win[:].bitcast(I32), k_words[0].rearrange("p t r -> p (t r)").bitcast(I32))
         for quad in range(4):
             nc.sync.dma_start(
                 qs[32 * quad : 32 * quad + 4, :].bitcast(I32).rearrange("i (g q) -> i g q", g=B * PASSES),
                 q_scales[:, :, 4 * quad : 4 * quad + 4, :].rearrange("b o i q -> i (b o) q").bitcast(I32),
             )
-        kw_win = keep.tile([P, T], U32, name="kw_win", align_bytes=64)
-        nc.sync.dma_start(kw_win[:].bitcast(I32), k_words[0].rearrange("p t r -> p (t r)").bitcast(I32))
         qw = keep.tile([P, B * PASSES * NQ], U32, name="qw", align_bytes=64)
         nc.sync.dma_start(
             qw[:].bitcast(I32).rearrange("p (g q) -> p g q", q=NQ),
             q_words.rearrange("b o p q r -> p (b o) (q r)").bitcast(I32),
         )
 
-        nc.vector.memset(ks_win[0 : P - KS_ROWS, :].bitcast(I32), 0)
-        ks = keep.tile([P, PASSES * B * N], U8, name="ks", align_bytes=64)
-        nc.vector.memset(ks[:].bitcast(I32), 0)
+        nc.vector.memset(ks_room[0 : P - KS_ROWS, EDGE : EDGE + T].bitcast(I32), 0)
         nc.vector.memset(vsc_win[0 : P - VS_ROWS, :].bitcast(I32), 0)
 
         ks_rows = keep.tile([P, B * N], U8, name="ks_rows", align_bytes=64)
-        nc.vector.tensor_copy(ks_rows[:], ks_win[:].indirect(off_t[:]))
+        nc.vector.tensor_copy(ks_rows[:], ks_win.indirect(off_t[:]))
+        ks = late.tile([P, PASSES * B * N], U8, name="ks", offset=KS_AT, align_bytes=64)
         for quad in range(4):
             first = P - KS_ROWS + 4 * PASSES * quad
             nc.sync.dma_start(
                 ks[32 * quad : 32 * quad + 4, :].bitcast(I32),
                 ks_rows[first : first + 4 * PASSES, :].bitcast(I32),
             )
-        vs_win = late.tile([P, T], F32, name="vs_win", offset=VS_AT, align_bytes=64)
-        nc.sync.dma_start(vs_win[:], vs)
         og_t = late.tile([P, B, DV], F32, name="og_t", offset=OG_AT, align_bytes=64)
         nc.sync.dma_start(og_t[:], og.rearrange("b q e -> q b e"))
+        vs_win = late.tile([P, T], F32, name="vs_win", offset=VS_AT, align_bytes=64)
+        nc.sync.dma_start(vs_win[:, VS_SPREAD:T], vs[:, VS_SPREAD:T])
         vw_win = late.tile([P, POOL_PAGES * DV], U32, name="vw_win", offset=VW_AT, align_bytes=64)
         nc.sync.dma_start(
             vw_win[:].bitcast(I32).rearrange("p (u e) -> p u e", u=POOL_PAGES),
@@ -112,16 +119,25 @@ def tile_attend_pkv4q_silu_kb_gate_kernel(
                 vsc_rows[first : first + 4, :].bitcast(I32),
             )
 
+        def spread(col, win, run):
+            for g in range(run // 4):
+                bank = psum.tile([P, 4, P], F32, name="turned", bufs=3)
+                for t in range(4):
+                    m = 4 * g + t
+                    nc.tensor.transpose(bank[:, t, :], col[:, m : m + 1].to_broadcast([P, P]), ident[:])
+                nc.scalar.copy(
+                    win.rearrange("p (c m) -> p c m", c=P)[:, :, 4 * g : 4 * g + 4],
+                    bank[:].rearrange("p t c -> p c t"),
+                )
+
         kb_win = keep.tile([P, T], F32, name="kb_win", align_bytes=64)
-        for g in range(RUN // 4):
-            bank = psum.tile([P, 4, P], F32, name="turned", bufs=3)
-            for t in range(4):
-                m = 4 * g + t
-                nc.tensor.transpose(bank[:, t, :], kb_col[:, m : m + 1].to_broadcast([P, P]), ident[:])
-            nc.scalar.copy(
-                kb_win[:].rearrange("p (c m) -> p c m", c=P)[:, :, 4 * g : 4 * g + 4],
-                bank[:].rearrange("p t c -> p c t"),
-            )
+        spread(kb_col, kb_win[:], RUN)
+        spread(vs_col, vs_win[:, 0:VS_SPREAD], VS_RUN)
+
+        half = keep.tile([P, B, DV], F32, name="half")
+        nc.scalar.activation(half[:], og_t[:], ACT.Tanh, scale=0.5)
+        gate = keep.tile([P, B, DV], F32, name="gate")
+        nc.scalar.activation(gate[:], half[:], ACT.Copy, scale=1.0 / 32.0, bias=1.0 / 32.0)
 
         pcols = PAGE // 16
         kws, scores, ps, wis, wq = {}, {}, {}, {}, {}
@@ -157,12 +173,12 @@ def tile_attend_pkv4q_silu_kb_gate_kernel(
         def bias_and_silu(j):
             z = work.tile([P, PAGE], F32, name="z", bufs=4)
             nc.vector.tensor_tensor(z[:], kb_win[:].indirect(off_t[:, j * pcols : (j + 1) * pcols]), scores[j][:], ALU.add)
-            p = work.tile([P, PAGE], F32, name="p", bufs=4)
+            p = late.tile([P, PAGE], F32, name="p%d" % j, offset=P_AT + 4 * PAGE * j, align_bytes=64)
             nc.scalar.activation(p[:], z[:], ACT.Silu)
             ps[j] = p
 
         def weigh(j):
-            w = work.tile([P, PAGE], F32, name="w", bufs=4)
+            w = late.tile([P, PAGE], F32, name="w%d" % j, offset=W_AT + 4 * PAGE * j, align_bytes=64)
             nc.vector.tensor_tensor(w[:], vs_win[:].indirect(off_t[:, j * pcols : (j + 1) * pcols]), ps[j][:], ALU.mult)
             turned = psum.tile([P, 4, NQ], F32, name="turned", bufs=3)
             for t in range(4):
@@ -179,7 +195,7 @@ def tile_attend_pkv4q_silu_kb_gate_kernel(
 
         def gather_values(b):
             vcols = PAGES * DV // 16
-            vw = work.tile([P, PAGES * DV], U32, name="vw", align_bytes=64)
+            vw = late.tile([P, PAGES * DV], U32, name="vw%d" % b, offset=(P_AT, W_AT)[b] + 4 * PAGE * 2, align_bytes=64)
             nc.vector.tensor_copy(vw[:], vw_win[:].indirect(voff_t[:, b * vcols : (b + 1) * vcols]))
             return (vw[:, 0:DV], vw[:, DV : 2 * DV])
 
@@ -213,11 +229,6 @@ def tile_attend_pkv4q_silu_kb_gate_kernel(
             if j + 1 < B * PAGES:
                 bias_and_silu(j + 1)
             weigh(j)
-
-        half = keep.tile([P, B, DV], F32, name="half")
-        nc.scalar.activation(half[:], og_t[:], ACT.Tanh, scale=0.5)
-        gate = keep.tile([P, B, DV], F32, name="gate")
-        nc.scalar.activation(gate[:], half[:], ACT.Copy, scale=1.0 / 32.0, bias=1.0 / 32.0)
 
         values0 = gather_values(0)
         quantise(0)

@@ -23,8 +23,6 @@ ACT = mybir.ActivationFunctionType
 ALU = mybir.AluOpType
 
 RUN = T // P
-VS_SPREAD = T // 4
-VS_RUN = VS_SPREAD // P
 VS_AT = 0
 EDGE = 64
 KS_AT = VS_AT + 4 * T
@@ -52,8 +50,15 @@ def tile_attend_pkv4q_silu_kb_gate_kernel(
         nc.gpsimd.memset(qs[:].bitcast(I32), 0)
         kb_col = keep.tile([P, RUN], F32, name="kb_col", align_bytes=64)
         nc.scalar.dma_start(kb_col[:], kb[0, :].rearrange("(c m) -> c m", c=P))
-        vs_col = keep.tile([P, VS_RUN], F32, name="vs_col", align_bytes=64)
-        nc.scalar.dma_start(vs_col[:], vs[0, 0:VS_SPREAD].rearrange("(c m) -> c m", c=P))
+
+        def load_query_scales(queue, quad):
+            queue.dma_start(
+                qs[32 * quad : 32 * quad + 4, :].bitcast(I32).rearrange("i (g q) -> i g q", g=B * PASSES),
+                q_scales[:, :, 4 * quad : 4 * quad + 4, :].rearrange("b o i q -> i (b o) q").bitcast(I32),
+            )
+
+        load_query_scales(nc.scalar, 0)
+        load_query_scales(nc.scalar, 1)
         ident = keep.tile([P, P], F32, name="ident")
         make_identity(nc, ident[:])
         warm = keep.tile([P, 1], F32, name="warm")
@@ -76,16 +81,13 @@ def tile_attend_pkv4q_silu_kb_gate_kernel(
         )
         kw_win = keep.tile([P, T], U32, name="kw_win", align_bytes=64)
         nc.sync.dma_start(kw_win[:].bitcast(I32), k_words[0].rearrange("p t r -> p (t r)").bitcast(I32))
-        for quad in range(4):
-            nc.sync.dma_start(
-                qs[32 * quad : 32 * quad + 4, :].bitcast(I32).rearrange("i (g q) -> i g q", g=B * PASSES),
-                q_scales[:, :, 4 * quad : 4 * quad + 4, :].rearrange("b o i q -> i (b o) q").bitcast(I32),
-            )
         qw = keep.tile([P, B * PASSES * NQ], U32, name="qw", align_bytes=64)
         nc.sync.dma_start(
             qw[:].bitcast(I32).rearrange("p (g q) -> p g q", q=NQ),
             q_words.rearrange("b o p q r -> p (b o) (q r)").bitcast(I32),
         )
+        load_query_scales(nc.sync, 2)
+        load_query_scales(nc.sync, 3)
 
         nc.vector.memset(ks_room[0 : P - KS_ROWS, EDGE : EDGE + T].bitcast(I32), 0)
         nc.vector.memset(vsc_win[0 : P - VS_ROWS, :].bitcast(I32), 0)
@@ -102,7 +104,7 @@ def tile_attend_pkv4q_silu_kb_gate_kernel(
         og_t = late.tile([P, B, DV], F32, name="og_t", offset=OG_AT, align_bytes=64)
         nc.sync.dma_start(og_t[:], og.rearrange("b q e -> q b e"))
         vs_win = late.tile([P, T], F32, name="vs_win", offset=VS_AT, align_bytes=64)
-        nc.sync.dma_start(vs_win[:, VS_SPREAD:T], vs[:, VS_SPREAD:T])
+        nc.sync.dma_start(vs_win[:], vs)
         vw_win = late.tile([P, POOL_PAGES * DV], U32, name="vw_win", offset=VW_AT, align_bytes=64)
         nc.sync.dma_start(
             vw_win[:].bitcast(I32).rearrange("p (u e) -> p u e", u=POOL_PAGES),
@@ -132,7 +134,6 @@ def tile_attend_pkv4q_silu_kb_gate_kernel(
 
         kb_win = keep.tile([P, T], F32, name="kb_win", align_bytes=64)
         spread(kb_col, kb_win[:], RUN)
-        spread(vs_col, vs_win[:, 0:VS_SPREAD], VS_RUN)
 
         half = keep.tile([P, B, DV], F32, name="half")
         nc.scalar.activation(half[:], og_t[:], ACT.Tanh, scale=0.5)

@@ -7,6 +7,7 @@ B, N, T, D, DV, NQ = 2, 1024, 4096, 1024, 256, 128
 P = 128
 PAGE = 512
 PAGES = N // PAGE
+LISTED = B * PAGES
 POOL_PAGES = T // PAGE
 PASSES = D // PAGE
 FLOPS = 2 * B * NQ * N * (D + DV)
@@ -22,17 +23,17 @@ FP4X4 = mybir.dt.float4_e2m1fn_x4
 ACT = mybir.ActivationFunctionType
 ALU = mybir.AluOpType
 
-RUN = T // P
-VS_AT = 0
-EDGE = 64
-KS_AT = VS_AT + 4 * T
-OG_AT = KS_AT + T
-VW_AT = OG_AT + 4 * B * DV
-VSC_AT = VW_AT + 4 * POOL_PAGES * DV
-P_AT = VSC_AT + POOL_PAGES * DV
-W_AT = P_AT + 4 * B * N
 KS_ROWS = 16 * PASSES
 VS_ROWS = 16
+PLANE = N + NQ
+VS_AT = 0
+ROWS_AT = VS_AT + 4 * T
+BIAS_AT = ROWS_AT + N
+POOL_FROM = 3800
+BUILT = 4
+BANK = 2048
+SCORE_BANKS = 6
+TURN_BANK = 7
 
 
 def tile_attend_pkv4q_silu_kb_gate_kernel(
@@ -42,78 +43,101 @@ def tile_attend_pkv4q_silu_kb_gate_kernel(
     with ExitStack() as ctx:
         lists = ctx.enter_context(tc.tile_pool(name="lists", bufs=1))
         keep = ctx.enter_context(tc.tile_pool(name="keep", bufs=1))
-        late = ctx.enter_context(tc.tile_pool(name="late", bufs=1))
-        work = ctx.enter_context(tc.tile_pool(name="work", bufs=2))
+        shared = ctx.enter_context(tc.tile_pool(name="shared", bufs=1))
+        work = ctx.enter_context(tc.tile_pool(name="work", bufs=4))
         psum = ctx.enter_context(tc.psum_pool(name="psum", bufs=1))
 
-        qs = keep.tile([P, B * PASSES * NQ], U8, name="qs", align_bytes=64)
-        nc.gpsimd.memset(qs[:].bitcast(I32), 0)
-        kb_col = keep.tile([P, RUN], F32, name="kb_col", align_bytes=64)
-        nc.scalar.dma_start(kb_col[:], kb[0, :].rearrange("(c m) -> c m", c=P))
-
-        def load_query_scales(queue, quad):
-            queue.dma_start(
-                qs[32 * quad : 32 * quad + 4, :].bitcast(I32).rearrange("i (g q) -> i g q", g=B * PASSES),
-                q_scales[:, :, 4 * quad : 4 * quad + 4, :].rearrange("b o i q -> i (b o) q").bitcast(I32),
+        kb_rows = keep.tile([P, PAGE], F32, name="kb_rows", align_bytes=64)
+        nc.scalar.dma_start(kb_rows[P - POOL_PAGES : P, :], kb[0, :].rearrange("(u c) -> u c", u=POOL_PAGES))
+        vs_rows = keep.tile([P, PAGE], F32, name="vs_rows", align_bytes=64)
+        nc.scalar.dma_start(vs_rows[P - POOL_PAGES : P, :], vs[0, :].rearrange("(u c) -> u c", u=POOL_PAGES))
+        dealt = [keep.tile([P, PLANE], U8, name="dealt%d" % b, align_bytes=64) for b in range(B)]
+        for b in range(B):
+            nc.scalar.dma_start(
+                dealt[b][P - KS_ROWS : P, N:PLANE].bitcast(I32),
+                q_scales[b].rearrange("o f q -> f o q").bitcast(I32),
             )
+        ks_win = keep.tile([P, T], U8, name="ks_win", align_bytes=64)
+        nc.sync.dma_start(ks_win[P - KS_ROWS : P, :].bitcast(I32), k_scales.rearrange("o f t -> f o t").bitcast(I32))
+        off_t = lists.tile([P, B * N // 16], U16, name="off_t")
+        nc.sync.dma_start(off_t[:], offs)
+        voff_t = lists.tile([P, LISTED * DV // 16], U16, name="voff_t")
+        nc.sync.dma_start(voff_t[:], voffs)
+        kw_win = keep.tile([P, T], U32, name="kw_win", align_bytes=64)
+        nc.sync.dma_start(kw_win[:].bitcast(I32), k_words[0].rearrange("p t r -> p (t r)").bitcast(I32))
 
-        load_query_scales(nc.scalar, 0)
-        load_query_scales(nc.scalar, 1)
         ident = keep.tile([P, P], F32, name="ident")
         make_identity(nc, ident[:])
         warm = keep.tile([P, 1], F32, name="warm")
         nc.scalar.activation(warm[:], ident[:, 0:1], ACT.Silu)
 
-        ks_room = late.tile([P, EDGE + T + 4 * B * DV + EDGE], U8, name="ks_room", offset=KS_AT - EDGE, align_bytes=64)
-        ks_win = ks_room[:, EDGE : EDGE + T]
-        nc.sync.dma_start(
-            ks_room[P - KS_ROWS : P, EDGE : EDGE + T].bitcast(I32),
-            k_scales.rearrange("o f t -> f o t").bitcast(I32),
-        )
-        off_t = lists.tile([P, B * N // 16], U16, name="off_t")
-        nc.sync.dma_start(off_t[:], offs)
-        voff_t = lists.tile([P, B * PAGES * DV // 16], U16, name="voff_t")
-        nc.sync.dma_start(voff_t[:], voffs)
-        vsc_win = late.tile([P, POOL_PAGES * DV], U8, name="vsc_win", offset=VSC_AT, align_bytes=64)
-        nc.sync.dma_start(
+        kb_win = keep.tile([P, T], F32, name="kb_win", align_bytes=64)
+        vsc_win = keep.tile([P, POOL_PAGES * DV], U8, name="vsc_win", align_bytes=64)
+        nc.vector.memset(ks_win[0 : P - KS_ROWS, :].bitcast(I32), 0)
+        nc.vector.memset(kb_win[:, 0:POOL_FROM], 0.0)
+        nc.gpsimd.memset(kb_win[:, POOL_FROM - 8 : T], 0.0)
+        nc.gpsimd.memset(vsc_win[:].bitcast(I32), 0)
+        nc.scalar.dma_start(
             vsc_win[P - VS_ROWS : P, :].bitcast(I32).rearrange("f (u e) -> f u e", u=POOL_PAGES),
             v_scales.rearrange("u f e -> f u e").bitcast(I32),
         )
-        kw_win = keep.tile([P, T], U32, name="kw_win", align_bytes=64)
-        nc.sync.dma_start(kw_win[:].bitcast(I32), k_words[0].rearrange("p t r -> p (t r)").bitcast(I32))
+
+        def turn(rows, name):
+            bank = psum.tile([P, 4, P], F32, name=name, offset=TURN_BANK * BANK)
+            for t in range(4):
+                nc.tensor.transpose(bank[:, t, :], rows[:, t:PAGE:4], ident[:])
+            return bank[:, :, P - POOL_PAGES : P].rearrange("p t u -> p u t")
+
+        nc.scalar.copy(kb_win[:].rearrange("p (u c) -> p u c", u=POOL_PAGES)[:, :, 0:4], turn(kb_rows, "kb_turned"))
+        vs_own = turn(vs_rows, "vs_turned")
+        bias = shared.tile([P, B * N], F32, name="bias", offset=BIAS_AT, align_bytes=64)
+        nc.scalar.activation(bias[:], kb_win[:].indirect(off_t[:]), ACT.Copy)
+
+        ks_rows = [
+            shared.tile([P, N], U8, name="ks_rows%d" % b, offset=(ROWS_AT, VS_AT)[b], align_bytes=64) for b in range(B)
+        ]
+        for b in range(B):
+            nc.vector.tensor_copy(ks_rows[b][:], ks_win[:].indirect(off_t[:, b * N // 16 : (b + 1) * N // 16]))
+        planes = [keep.tile([P, PASSES * PLANE], U8, name="planes%d" % b, align_bytes=64) for b in range(B)]
         qw = keep.tile([P, B * PASSES * NQ], U32, name="qw", align_bytes=64)
-        nc.sync.dma_start(
-            qw[:].bitcast(I32).rearrange("p (g q) -> p g q", q=NQ),
-            q_words.rearrange("b o p q r -> p (b o) (q r)").bitcast(I32),
-        )
-        load_query_scales(nc.sync, 2)
-        load_query_scales(nc.sync, 3)
-
-        nc.vector.memset(ks_room[0 : P - KS_ROWS, EDGE : EDGE + T].bitcast(I32), 0)
-        nc.vector.memset(vsc_win[0 : P - VS_ROWS, :].bitcast(I32), 0)
-
-        ks_rows = keep.tile([P, B * N], U8, name="ks_rows", align_bytes=64)
-        nc.vector.tensor_copy(ks_rows[:], ks_win.indirect(off_t[:]))
-        ks = late.tile([P, PASSES * B * N], U8, name="ks", offset=KS_AT, align_bytes=64)
-        for quad in range(4):
-            first = P - KS_ROWS + 4 * PASSES * quad
-            nc.sync.dma_start(
-                ks[32 * quad : 32 * quad + 4, :].bitcast(I32),
-                ks_rows[first : first + 4 * PASSES, :].bitcast(I32),
+        for b in range(B):
+            nc.vector.tensor_copy(
+                dealt[b][:, 0:N].rearrange("p (j t m) -> p j t m", j=PAGES, t=4),
+                ks_rows[b][:].rearrange("p (j m t) -> p j t m", j=PAGES, t=4),
             )
-        og_t = late.tile([P, B, DV], F32, name="og_t", offset=OG_AT, align_bytes=64)
-        nc.sync.dma_start(og_t[:], og.rearrange("b q e -> q b e"))
-        vs_win = late.tile([P, T], F32, name="vs_win", offset=VS_AT, align_bytes=64)
-        nc.sync.dma_start(vs_win[:], vs)
-        vw_win = late.tile([P, POOL_PAGES * DV], U32, name="vw_win", offset=VW_AT, align_bytes=64)
+            for quad in range(4):
+                first = P - KS_ROWS + 4 * PASSES * quad
+                nc.sync.dma_start(
+                    planes[b][32 * quad : 32 * quad + 4, :].bitcast(I32),
+                    dealt[b][first : first + 4 * PASSES, :].bitcast(I32),
+                )
+            if b == 0:
+                nc.sync.dma_start(
+                    qw[:].bitcast(I32).rearrange("p (g q) -> p g q", q=NQ),
+                    q_words.rearrange("b o p q r -> p (b o) (q r)").bitcast(I32),
+                )
+
+        vs_win = shared.tile([P, T], F32, name="vs_win", offset=VS_AT, align_bytes=64)
+        nc.gpsimd.memset(vs_win[:, BUILT * PAGE : T], 0.0)
+        nc.scalar.copy(
+            vs_win[:, 0 : BUILT * PAGE].rearrange("p (u r t) -> p u r t", u=BUILT, t=4),
+            vs_own[:, 0:BUILT, :].rearrange("p u (r t) -> p u r t", r=1).to_broadcast([P, BUILT, PAGE // 4, 4]),
+        )
+        nc.scalar.copy(vs_win[:].rearrange("p (u c) -> p u c", u=POOL_PAGES)[:, BUILT:, 0:4], vs_own[:, BUILT:, :])
+        scale = keep.tile([P, B * N], F32, name="scale", align_bytes=64)
+        nc.scalar.activation(scale[:], vs_win[:].indirect(off_t[:]), ACT.Copy)
+
+        vw_win = keep.tile([P, POOL_PAGES * DV], U32, name="vw_win", align_bytes=64)
         nc.sync.dma_start(
             vw_win[:].bitcast(I32).rearrange("p (u e) -> p u e", u=POOL_PAGES),
             v_words.rearrange("u p e r -> p u (e r)").bitcast(I32),
         )
+        og_t = keep.tile([P, B, DV], F32, name="og_t", align_bytes=64)
+        nc.sync.dma_start(og_t[:], og.rearrange("b q e -> q b e"))
 
-        vsc_rows = keep.tile([P, B * PAGES * DV], U8, name="vsc_rows", align_bytes=64)
+        vsc_rows = shared.tile([P, LISTED * DV], U8, name="vsc_rows", offset=ROWS_AT, align_bytes=64)
         nc.vector.tensor_copy(vsc_rows[:], vsc_win[:].indirect(voff_t[:]))
-        vsc = late.tile([P, B * PAGES * DV], U8, name="vsc", offset=VSC_AT, align_bytes=64)
+        vsc = keep.tile([P, LISTED * DV], U8, name="vsc", align_bytes=64)
         for quad in range(4):
             first = P - VS_ROWS + 4 * quad
             nc.sync.dma_start(
@@ -121,123 +145,108 @@ def tile_attend_pkv4q_silu_kb_gate_kernel(
                 vsc_rows[first : first + 4, :].bitcast(I32),
             )
 
-        def spread(col, win, run):
-            for g in range(run // 4):
-                bank = psum.tile([P, 4, P], F32, name="turned", bufs=3)
-                for t in range(4):
-                    m = 4 * g + t
-                    nc.tensor.transpose(bank[:, t, :], col[:, m : m + 1].to_broadcast([P, P]), ident[:])
-                nc.scalar.copy(
-                    win.rearrange("p (c m) -> p c m", c=P)[:, :, 4 * g : 4 * g + 4],
-                    bank[:].rearrange("p t c -> p c t"),
-                )
-
-        kb_win = keep.tile([P, T], F32, name="kb_win", align_bytes=64)
-        spread(kb_col, kb_win[:], RUN)
-
-        half = keep.tile([P, B, DV], F32, name="half")
-        nc.scalar.activation(half[:], og_t[:], ACT.Tanh, scale=0.5)
-        gate = keep.tile([P, B, DV], F32, name="gate")
-        nc.scalar.activation(gate[:], half[:], ACT.Copy, scale=1.0 / 32.0, bias=1.0 / 32.0)
-
         pcols = PAGE // 16
-        kws, scores, ps, wis, wq = {}, {}, {}, {}, {}
+        kws, ps, wis, wq = {}, {}, {}, {}
 
         def gather_keys(j):
-            kw = work.tile([P, PAGE], U32, name="kw", bufs=4, align_bytes=64)
+            kw = work.tile([P, PAGE], U32, name="kw", align_bytes=64)
             nc.vector.tensor_copy(kw[:], kw_win[:].indirect(off_t[:, j * pcols : (j + 1) * pcols]))
             kws[j] = kw
 
         def score(j):
             b = j // PAGES
-            kp = work.tile([P, PASSES * PAGE], U16, name="kp", bufs=4, align_bytes=64)
+            kp = work.tile([P, PASSES * PAGE], U16, name="kp", align_bytes=64)
             nc.vector.tensor_copy(
-                kp[:].rearrange("p (o n) -> p o n", o=PASSES),
-                kws[j][:].bitcast(U16).rearrange("p (n o) -> p o n", o=PASSES),
+                kp[:].rearrange("p (o t c i) -> p o c t i", o=PASSES, t=4, i=4),
+                kws[j][:].bitcast(U16).rearrange("p (c i t o) -> p o c t i", o=PASSES, t=4, i=4),
             )
-            bank = psum.tile([P, PAGE], F32, name="sc", bufs=3)
-            for o in range(PASSES):
-                g = b * PASSES + o
-                nc.tensor.matmul_mx(
-                    out=bank[:],
-                    lhsT=qw[:, g * NQ : (g + 1) * NQ].bitcast(FP8X4),
-                    lhsT_scale=qs[:, g * NQ : (g + 1) * NQ],
-                    rhs=kp[:, o * PAGE : (o + 1) * PAGE].bitcast(FP4X4),
-                    rhs_scale=ks[:, o * B * N + j * PAGE : o * B * N + (j + 1) * PAGE],
-                    start=(o == 0),
-                    stop=(o == PASSES - 1),
-                )
-            a = work.tile([P, PAGE], F32, name="a", bufs=4)
-            nc.scalar.copy(a[:], bank[:])
-            scores[j] = a
-
-        def bias_and_silu(j):
-            z = work.tile([P, PAGE], F32, name="z", bufs=4)
-            nc.vector.tensor_tensor(z[:], kb_win[:].indirect(off_t[:, j * pcols : (j + 1) * pcols]), scores[j][:], ALU.add)
-            p = late.tile([P, PAGE], F32, name="p%d" % j, offset=P_AT + 4 * PAGE * j, align_bytes=64)
-            nc.scalar.activation(p[:], z[:], ACT.Silu)
+            p = work.tile([P, PAGE], F32, name="p", align_bytes=64)
+            for h in range(2):
+                bank = psum.tile([P, 4, P], F32, name="sc%d_%d" % (j, h), offset=((2 * j + h) % SCORE_BANKS) * BANK)
+                for t in range(2 * h, 2 * h + 2):
+                    for o in range(PASSES):
+                        g = b * PASSES + o
+                        at = o * PLANE + (j % PAGES) * PAGE + t * P
+                        qat = o * PLANE + N
+                        nc.tensor.matmul_mx(
+                            out=bank[:, t, :],
+                            lhsT=kp[:, o * PAGE + t * P : o * PAGE + (t + 1) * P].bitcast(FP4X4),
+                            lhsT_scale=planes[b][:, at : at + P],
+                            rhs=qw[:, g * NQ : (g + 1) * NQ].bitcast(FP8X4),
+                            rhs_scale=planes[b][:, qat : qat + NQ],
+                            start=(o == 0),
+                            stop=(o == PASSES - 1),
+                        )
+                for t in range(2 * h, 2 * h + 2):
+                    nc.scalar.activation(
+                        p[:, t * NQ : (t + 1) * NQ], bank[:, t, :], ACT.Silu, bias=bias[:, j * PAGE + t : j * PAGE + t + 1]
+                    )
             ps[j] = p
 
         def weigh(j):
-            w = late.tile([P, PAGE], F32, name="w%d" % j, offset=W_AT + 4 * PAGE * j, align_bytes=64)
-            nc.vector.tensor_tensor(w[:], vs_win[:].indirect(off_t[:, j * pcols : (j + 1) * pcols]), ps[j][:], ALU.mult)
-            turned = psum.tile([P, 4, NQ], F32, name="turned", bufs=3)
-            for t in range(4):
-                nc.tensor.transpose(turned[:, t, :], w[:, t:PAGE:4], ident[:])
-            wi = work.tile([P, 4 * NQ], BF16, name="wi", bufs=4, align_bytes=64)
-            nc.scalar.copy(wi[:].rearrange("p (q t) -> p q t", t=4), turned[:].rearrange("p t q -> p q t"))
+            wi = work.tile([P, 4 * NQ], BF16, name="wi", align_bytes=64)
+            nc.vector.tensor_tensor(
+                wi[:].rearrange("p (c i t) -> p c t i", t=4, i=2),
+                ps[j][:].rearrange("p (t c i) -> p c t i", t=4, i=2),
+                scale[:, j * PAGE : j * PAGE + 4].rearrange("p (a t b) -> p a t b", a=1, b=1).to_broadcast([P, NQ // 2, 4, 2]),
+                ALU.mult,
+            )
             wis[j] = wi
 
         def quantise(j):
-            wc = work.tile([P, NQ], U32, name="wc", bufs=4, align_bytes=64)
-            wsc = work.tile([P, NQ], U8, name="wsc", bufs=4, align_bytes=64)
+            wc = work.tile([P, NQ], U32, name="wc", align_bytes=64)
+            wsc = work.tile([P, NQ], U8, name="wsc", align_bytes=64)
             nc.vector.quantize_mx(out=wc[:].bitcast(FP8X4), scales=wsc[:], in_=wis[j][:])
             wq[j] = (wc, wsc)
 
         def gather_values(b):
             vcols = PAGES * DV // 16
-            vw = late.tile([P, PAGES * DV], U32, name="vw%d" % b, offset=(P_AT, W_AT)[b] + 4 * PAGE * 2, align_bytes=64)
+            vw = work.tile([P, PAGES * DV], U32, name="vw", align_bytes=64)
             nc.vector.tensor_copy(vw[:], vw_win[:].indirect(voff_t[:, b * vcols : (b + 1) * vcols]))
-            return (vw[:, 0:DV], vw[:, DV : 2 * DV])
+            return vw
 
-        def weigh_values(b, pages):
-            y = psum.tile([P, DV], F32, name="y", bufs=2)
+        def weigh_values(b, vw):
+            y = psum.tile([P, DV], F32, name="y%d" % b, offset=(SCORE_BANKS + b) * BANK)
             for e in range(PAGES):
                 j = b * PAGES + e
                 nc.tensor.matmul_mx(
                     out=y[:],
                     lhsT=wq[j][0][:].bitcast(FP8X4),
                     lhsT_scale=wq[j][1][:],
-                    rhs=pages[e].bitcast(FP8X4),
+                    rhs=vw[:, e * DV : (e + 1) * DV].bitcast(FP8X4),
                     rhs_scale=vsc[:, j * DV : (j + 1) * DV],
                     start=(e == 0),
                     stop=(e == PAGES - 1),
                 )
             return y
 
-        def finish(b, y):
+        def finish(b, y, gate):
             res = work.tile([P, DV], F32, name="res")
             nc.vector.tensor_tensor(res[:], y[:], gate[:, b, :], ALU.mult)
             nc.sync.dma_start(out[b], res[:])
 
         gather_keys(0)
-        for j in range(B * PAGES):
-            if j + 1 < B * PAGES:
+        for j in range(LISTED):
+            if j + 1 < LISTED:
                 gather_keys(j + 1)
             score(j)
-        bias_and_silu(0)
-        for j in range(B * PAGES):
-            if j + 1 < B * PAGES:
-                bias_and_silu(j + 1)
-            weigh(j)
 
+        half = shared.tile([P, B, DV], F32, name="half", offset=BIAS_AT, align_bytes=64)
+        nc.scalar.activation(half[:], og_t[:], ACT.Tanh, scale=0.5)
+        gate = keep.tile([P, B, DV], F32, name="gate")
+        nc.scalar.activation(gate[:], half[:], ACT.Copy, scale=1.0 / 32.0, bias=1.0 / 32.0)
+
+        weigh(0)
+        weigh(1)
         values0 = gather_values(0)
         quantise(0)
         quantise(1)
         y0 = weigh_values(0, values0)
+        weigh(2)
         values1 = gather_values(1)
+        weigh(3)
         quantise(2)
         quantise(3)
-        finish(0, y0)
         y1 = weigh_values(1, values1)
-        finish(1, y1)
+        finish(0, y0, gate)
+        finish(1, y1, gate)

@@ -25,11 +25,11 @@ ALU = mybir.AluOpType
 
 KS_ROWS = 16 * PASSES
 VS_ROWS = 16
-PLANE = N + NQ
+PLANE = B * N + B * NQ
 VS_AT = 0
 ROWS_AT = VS_AT + 4 * T
-BIAS_AT = ROWS_AT + N
-POOL_FROM = 3800
+BIAS_AT = ROWS_AT + 4 * PAGE
+POOL_FROM = 1792
 BUILT = 4
 BANK = 2048
 SCORE_BANKS = 6
@@ -47,24 +47,32 @@ def tile_attend_pkv4q_silu_kb_gate_kernel(
         work = ctx.enter_context(tc.tile_pool(name="work", bufs=4))
         psum = ctx.enter_context(tc.psum_pool(name="psum", bufs=1))
 
-        kb_rows = keep.tile([P, PAGE], F32, name="kb_rows", align_bytes=64)
+        kb_rows = shared.tile([P, PAGE], F32, name="kb_rows", offset=ROWS_AT, align_bytes=64)
         nc.scalar.dma_start(kb_rows[P - POOL_PAGES : P, :], kb[0, :].rearrange("(u c) -> u c", u=POOL_PAGES))
-        vs_rows = keep.tile([P, PAGE], F32, name="vs_rows", align_bytes=64)
-        nc.scalar.dma_start(vs_rows[P - POOL_PAGES : P, :], vs[0, :].rearrange("(u c) -> u c", u=POOL_PAGES))
-        dealt = [keep.tile([P, PLANE], U8, name="dealt%d" % b, align_bytes=64) for b in range(B)]
+        dealt = keep.tile([P, PLANE], U8, name="dealt", align_bytes=64)
         for b in range(B):
             nc.scalar.dma_start(
-                dealt[b][P - KS_ROWS : P, N:PLANE].bitcast(I32),
+                dealt[P - KS_ROWS : P, B * N + b * NQ : B * N + (b + 1) * NQ].bitcast(I32),
                 q_scales[b].rearrange("o f q -> f o q").bitcast(I32),
             )
+        vsc_win = keep.tile([P, POOL_PAGES * DV], U8, name="vsc_win", align_bytes=64)
+        nc.sync.dma_start(
+            vsc_win[P - VS_ROWS : P, :].bitcast(I32).rearrange("f (u e) -> f u e", u=POOL_PAGES),
+            v_scales.rearrange("u f e -> f u e").bitcast(I32),
+        )
+        voff_t = lists.tile([P, LISTED * DV // 16], U16, name="voff_t")
+        nc.sync.dma_start(voff_t[:], voffs)
         ks_win = keep.tile([P, T], U8, name="ks_win", align_bytes=64)
         nc.sync.dma_start(ks_win[P - KS_ROWS : P, :].bitcast(I32), k_scales.rearrange("o f t -> f o t").bitcast(I32))
         off_t = lists.tile([P, B * N // 16], U16, name="off_t")
         nc.sync.dma_start(off_t[:], offs)
-        voff_t = lists.tile([P, LISTED * DV // 16], U16, name="voff_t")
-        nc.sync.dma_start(voff_t[:], voffs)
         kw_win = keep.tile([P, T], U32, name="kw_win", align_bytes=64)
         nc.sync.dma_start(kw_win[:].bitcast(I32), k_words[0].rearrange("p t r -> p (t r)").bitcast(I32))
+        qw = keep.tile([P, B * PASSES * NQ], U32, name="qw", align_bytes=64)
+        nc.sync.dma_start(
+            qw[:].bitcast(I32).rearrange("p (g q) -> p g q", q=NQ),
+            q_words.rearrange("b o p q r -> p (b o) (q r)").bitcast(I32),
+        )
 
         ident = keep.tile([P, P], F32, name="ident")
         make_identity(nc, ident[:])
@@ -72,15 +80,13 @@ def tile_attend_pkv4q_silu_kb_gate_kernel(
         nc.scalar.activation(warm[:], ident[:, 0:1], ACT.Silu)
 
         kb_win = keep.tile([P, T], F32, name="kb_win", align_bytes=64)
-        vsc_win = keep.tile([P, POOL_PAGES * DV], U8, name="vsc_win", align_bytes=64)
+        nc.vector.memset(vsc_win[0 : P - VS_ROWS, :].bitcast(I32), 0)
         nc.vector.memset(ks_win[0 : P - KS_ROWS, :].bitcast(I32), 0)
         nc.vector.memset(kb_win[:, 0:POOL_FROM], 0.0)
         nc.gpsimd.memset(kb_win[:, POOL_FROM - 8 : T], 0.0)
-        nc.gpsimd.memset(vsc_win[:].bitcast(I32), 0)
-        nc.scalar.dma_start(
-            vsc_win[P - VS_ROWS : P, :].bitcast(I32).rearrange("f (u e) -> f u e", u=POOL_PAGES),
-            v_scales.rearrange("u f e -> f u e").bitcast(I32),
-        )
+
+        vsc_rows = keep.tile([P, LISTED * DV], U8, name="vsc_rows", align_bytes=64)
+        nc.vector.tensor_copy(vsc_rows[:], vsc_win[:].indirect(voff_t[:]))
 
         def turn(rows, name):
             bank = psum.tile([P, 4, P], F32, name=name, offset=TURN_BANK * BANK)
@@ -88,34 +94,32 @@ def tile_attend_pkv4q_silu_kb_gate_kernel(
                 nc.tensor.transpose(bank[:, t, :], rows[:, t:PAGE:4], ident[:])
             return bank[:, :, P - POOL_PAGES : P].rearrange("p t u -> p u t")
 
-        nc.scalar.copy(kb_win[:].rearrange("p (u c) -> p u c", u=POOL_PAGES)[:, :, 0:4], turn(kb_rows, "kb_turned"))
+        kb_own = turn(kb_rows, "kb_turned")
+        vs_rows = shared.tile([P, PAGE], F32, name="vs_rows", offset=ROWS_AT, align_bytes=64)
+        nc.scalar.dma_start(vs_rows[P - POOL_PAGES : P, :], vs[0, :].rearrange("(u c) -> u c", u=POOL_PAGES))
+        nc.scalar.copy(kb_win[:].rearrange("p (u c) -> p u c", u=POOL_PAGES)[:, :, 0:4], kb_own)
         vs_own = turn(vs_rows, "vs_turned")
         bias = shared.tile([P, B * N], F32, name="bias", offset=BIAS_AT, align_bytes=64)
         nc.scalar.activation(bias[:], kb_win[:].indirect(off_t[:]), ACT.Copy)
 
         ks_rows = [
-            shared.tile([P, N], U8, name="ks_rows%d" % b, offset=(ROWS_AT, VS_AT)[b], align_bytes=64) for b in range(B)
+            keep.tile([P, N], U8, name="ks_rows0", align_bytes=64),
+            shared.tile([P, N], U8, name="ks_rows1", offset=VS_AT, align_bytes=64),
         ]
         for b in range(B):
             nc.vector.tensor_copy(ks_rows[b][:], ks_win[:].indirect(off_t[:, b * N // 16 : (b + 1) * N // 16]))
-        planes = [keep.tile([P, PASSES * PLANE], U8, name="planes%d" % b, align_bytes=64) for b in range(B)]
-        qw = keep.tile([P, B * PASSES * NQ], U32, name="qw", align_bytes=64)
         for b in range(B):
             nc.vector.tensor_copy(
-                dealt[b][:, 0:N].rearrange("p (j t m) -> p j t m", j=PAGES, t=4),
+                dealt[:, b * N : (b + 1) * N].rearrange("p (j t m) -> p j t m", j=PAGES, t=4),
                 ks_rows[b][:].rearrange("p (j m t) -> p j t m", j=PAGES, t=4),
             )
-            for quad in range(4):
-                first = P - KS_ROWS + 4 * PASSES * quad
-                nc.sync.dma_start(
-                    planes[b][32 * quad : 32 * quad + 4, :].bitcast(I32),
-                    dealt[b][first : first + 4 * PASSES, :].bitcast(I32),
-                )
-            if b == 0:
-                nc.sync.dma_start(
-                    qw[:].bitcast(I32).rearrange("p (g q) -> p g q", q=NQ),
-                    q_words.rearrange("b o p q r -> p (b o) (q r)").bitcast(I32),
-                )
+        planes = keep.tile([P, PASSES * PLANE], U8, name="planes", align_bytes=64)
+        for quad in range(4):
+            first = P - KS_ROWS + 4 * PASSES * quad
+            nc.sync.dma_start(
+                planes[32 * quad : 32 * quad + 4, :].bitcast(I32),
+                dealt[first : first + 4 * PASSES, :].bitcast(I32),
+            )
 
         vs_win = shared.tile([P, T], F32, name="vs_win", offset=VS_AT, align_bytes=64)
         nc.gpsimd.memset(vs_win[:, BUILT * PAGE : T], 0.0)
@@ -135,8 +139,6 @@ def tile_attend_pkv4q_silu_kb_gate_kernel(
         og_t = keep.tile([P, B, DV], F32, name="og_t", align_bytes=64)
         nc.sync.dma_start(og_t[:], og.rearrange("b q e -> q b e"))
 
-        vsc_rows = shared.tile([P, LISTED * DV], U8, name="vsc_rows", offset=ROWS_AT, align_bytes=64)
-        nc.vector.tensor_copy(vsc_rows[:], vsc_win[:].indirect(voff_t[:]))
         vsc = keep.tile([P, LISTED * DV], U8, name="vsc", align_bytes=64)
         for quad in range(4):
             first = P - VS_ROWS + 4 * quad
@@ -145,35 +147,38 @@ def tile_attend_pkv4q_silu_kb_gate_kernel(
                 vsc_rows[first : first + 4, :].bitcast(I32),
             )
 
-        pcols = PAGE // 16
-        kws, ps, wis, wq = {}, {}, {}, {}
+        kws, kps, ps, wis, wq = {}, {}, {}, {}, {}
 
-        def gather_keys(j):
-            kw = work.tile([P, PAGE], U32, name="kw", align_bytes=64)
-            nc.vector.tensor_copy(kw[:], kw_win[:].indirect(off_t[:, j * pcols : (j + 1) * pcols]))
-            kws[j] = kw
+        def gather_keys(b):
+            kw = work.tile([P, N], U32, name="kw", bufs=2, align_bytes=64)
+            nc.vector.tensor_copy(kw[:], kw_win[:].indirect(off_t[:, b * N // 16 : (b + 1) * N // 16]))
+            kws[b] = kw
 
-        def score(j):
-            b = j // PAGES
-            kp = work.tile([P, PASSES * PAGE], U16, name="kp", align_bytes=64)
+        def part(b):
+            kp = work.tile([P, PASSES * N], U16, name="kp", bufs=2, align_bytes=64)
             nc.vector.tensor_copy(
                 kp[:].rearrange("p (o t c i) -> p o c t i", o=PASSES, t=4, i=4),
-                kws[j][:].bitcast(U16).rearrange("p (c i t o) -> p o c t i", o=PASSES, t=4, i=4),
+                kws[b][:].bitcast(U16).rearrange("p (c i t o) -> p o c t i", o=PASSES, t=4, i=4),
             )
+            kps[b] = kp
+
+        def score(j):
+            b, e = divmod(j, PAGES)
             p = work.tile([P, PAGE], F32, name="p", align_bytes=64)
             for h in range(2):
                 bank = psum.tile([P, 4, P], F32, name="sc%d_%d" % (j, h), offset=((2 * j + h) % SCORE_BANKS) * BANK)
                 for t in range(2 * h, 2 * h + 2):
                     for o in range(PASSES):
                         g = b * PASSES + o
-                        at = o * PLANE + (j % PAGES) * PAGE + t * P
-                        qat = o * PLANE + N
+                        kat = o * N + (t * PAGES + e) * P
+                        at = o * PLANE + j * PAGE + t * P
+                        qat = o * PLANE + B * N + b * NQ
                         nc.tensor.matmul_mx(
                             out=bank[:, t, :],
-                            lhsT=kp[:, o * PAGE + t * P : o * PAGE + (t + 1) * P].bitcast(FP4X4),
-                            lhsT_scale=planes[b][:, at : at + P],
+                            lhsT=kps[b][:, kat : kat + P].bitcast(FP4X4),
+                            lhsT_scale=planes[:, at : at + P],
                             rhs=qw[:, g * NQ : (g + 1) * NQ].bitcast(FP8X4),
-                            rhs_scale=planes[b][:, qat : qat + NQ],
+                            rhs_scale=planes[:, qat : qat + NQ],
                             start=(o == 0),
                             stop=(o == PASSES - 1),
                         )
@@ -199,13 +204,7 @@ def tile_attend_pkv4q_silu_kb_gate_kernel(
             nc.vector.quantize_mx(out=wc[:].bitcast(FP8X4), scales=wsc[:], in_=wis[j][:])
             wq[j] = (wc, wsc)
 
-        def gather_values(b):
-            vcols = PAGES * DV // 16
-            vw = work.tile([P, PAGES * DV], U32, name="vw", align_bytes=64)
-            nc.vector.tensor_copy(vw[:], vw_win[:].indirect(voff_t[:, b * vcols : (b + 1) * vcols]))
-            return vw
-
-        def weigh_values(b, vw):
+        def weigh_values(b):
             y = psum.tile([P, DV], F32, name="y%d" % b, offset=(SCORE_BANKS + b) * BANK)
             for e in range(PAGES):
                 j = b * PAGES + e
@@ -213,7 +212,7 @@ def tile_attend_pkv4q_silu_kb_gate_kernel(
                     out=y[:],
                     lhsT=wq[j][0][:].bitcast(FP8X4),
                     lhsT_scale=wq[j][1][:],
-                    rhs=vw[:, e * DV : (e + 1) * DV].bitcast(FP8X4),
+                    rhs=vw[:, j * DV : (j + 1) * DV].bitcast(FP8X4),
                     rhs_scale=vsc[:, j * DV : (j + 1) * DV],
                     start=(e == 0),
                     stop=(e == PAGES - 1),
@@ -225,28 +224,26 @@ def tile_attend_pkv4q_silu_kb_gate_kernel(
             nc.vector.tensor_tensor(res[:], y[:], gate[:, b, :], ALU.mult)
             nc.sync.dma_start(out[b], res[:])
 
-        gather_keys(0)
-        for j in range(LISTED):
-            if j + 1 < LISTED:
-                gather_keys(j + 1)
-            score(j)
+        for b in range(B):
+            gather_keys(b)
+        for b in range(B):
+            part(b)
+            for e in range(PAGES):
+                score(b * PAGES + e)
 
         half = shared.tile([P, B, DV], F32, name="half", offset=BIAS_AT, align_bytes=64)
         nc.scalar.activation(half[:], og_t[:], ACT.Tanh, scale=0.5)
         gate = keep.tile([P, B, DV], F32, name="gate")
         nc.scalar.activation(gate[:], half[:], ACT.Copy, scale=1.0 / 32.0, bias=1.0 / 32.0)
 
-        weigh(0)
-        weigh(1)
-        values0 = gather_values(0)
-        quantise(0)
-        quantise(1)
-        y0 = weigh_values(0, values0)
-        weigh(2)
-        values1 = gather_values(1)
-        weigh(3)
-        quantise(2)
-        quantise(3)
-        y1 = weigh_values(1, values1)
-        finish(0, y0, gate)
-        finish(1, y1, gate)
+        vw = keep.tile([P, LISTED * DV], U32, name="vw", align_bytes=64)
+        nc.vector.tensor_copy(vw[:], vw_win[:].indirect(voff_t[:]))
+        ys = []
+        for b in range(B):
+            for e in range(PAGES):
+                weigh(b * PAGES + e)
+            for e in range(PAGES):
+                quantise(b * PAGES + e)
+            ys.append(weigh_values(b))
+        for b in range(B):
+            finish(b, ys[b], gate)

@@ -26,14 +26,13 @@ ALU = mybir.AluOpType
 KS_ROWS = 16 * PASSES
 VS_ROWS = 16
 PLANE = B * N + B * NQ
-VS_AT = 0
-ROWS_AT = VS_AT + 4 * T
+ROWS_AT = 0
 BIAS_AT = ROWS_AT + 4 * PAGE
-POOL_FROM = 1792
-BUILT = 4
+KW_AT = BIAS_AT + 4 * B * N
+POOL_FROM = 1024
+BUILT = 6
 BANK = 2048
 SCORE_BANKS = 6
-TURN_BANK = 7
 
 
 def tile_attend_pkv4q_silu_kb_gate_kernel(
@@ -47,8 +46,8 @@ def tile_attend_pkv4q_silu_kb_gate_kernel(
         work = ctx.enter_context(tc.tile_pool(name="work", bufs=4))
         psum = ctx.enter_context(tc.psum_pool(name="psum", bufs=1))
 
-        kb_rows = shared.tile([P, PAGE], F32, name="kb_rows", offset=ROWS_AT, align_bytes=64)
-        nc.scalar.dma_start(kb_rows[P - POOL_PAGES : P, :], kb[0, :].rearrange("(u c) -> u c", u=POOL_PAGES))
+        vs_rows = shared.tile([P, PAGE], F32, name="vs_rows", offset=ROWS_AT, align_bytes=64)
+        nc.scalar.dma_start(vs_rows[P - POOL_PAGES : P, :], vs[0, :].rearrange("(u c) -> u c", u=POOL_PAGES))
         dealt = keep.tile([P, PLANE], U8, name="dealt", align_bytes=64)
         for b in range(B):
             nc.scalar.dma_start(
@@ -82,30 +81,37 @@ def tile_attend_pkv4q_silu_kb_gate_kernel(
         kb_win = keep.tile([P, T], F32, name="kb_win", align_bytes=64)
         nc.vector.memset(vsc_win[0 : P - VS_ROWS, :].bitcast(I32), 0)
         nc.vector.memset(ks_win[0 : P - KS_ROWS, :].bitcast(I32), 0)
+        vs_win = keep.tile([P, T], F32, name="vs_win", align_bytes=64)
+        nc.vector.memset(vs_win[:, BUILT * PAGE : T], 0.0)
         nc.vector.memset(kb_win[:, 0:POOL_FROM], 0.0)
         nc.gpsimd.memset(kb_win[:, POOL_FROM - 8 : T], 0.0)
 
         vsc_rows = keep.tile([P, LISTED * DV], U8, name="vsc_rows", align_bytes=64)
         nc.vector.tensor_copy(vsc_rows[:], vsc_win[:].indirect(voff_t[:]))
 
-        def turn(rows, name):
-            bank = psum.tile([P, 4, P], F32, name=name, offset=TURN_BANK * BANK)
+        def turn(rows, name, at):
+            bank = psum.tile([P, 4, P], F32, name=name, offset=at * BANK)
             for t in range(4):
                 nc.tensor.transpose(bank[:, t, :], rows[:, t:PAGE:4], ident[:])
             return bank[:, :, P - POOL_PAGES : P].rearrange("p t u -> p u t")
 
-        kb_own = turn(kb_rows, "kb_turned")
-        vs_rows = shared.tile([P, PAGE], F32, name="vs_rows", offset=ROWS_AT, align_bytes=64)
-        nc.scalar.dma_start(vs_rows[P - POOL_PAGES : P, :], vs[0, :].rearrange("(u c) -> u c", u=POOL_PAGES))
+        vs_own = turn(vs_rows, "vs_turned", SCORE_BANKS)
+        kb_rows = shared.tile([P, PAGE], F32, name="kb_rows", offset=ROWS_AT, align_bytes=64)
+        nc.scalar.dma_start(kb_rows[P - POOL_PAGES : P, :], kb[0, :].rearrange("(u c) -> u c", u=POOL_PAGES))
+        nc.scalar.copy(
+            vs_win[:, 0 : BUILT * PAGE].rearrange("p (u r t) -> p u r t", u=BUILT, t=4),
+            vs_own[:, 0:BUILT, :].rearrange("p u (r t) -> p u r t", r=1).to_broadcast([P, BUILT, PAGE // 4, 4]),
+        )
+        nc.scalar.copy(vs_win[:].rearrange("p (u c) -> p u c", u=POOL_PAGES)[:, BUILT:, 0:4], vs_own[:, BUILT:, :])
+        kb_own = turn(kb_rows, "kb_turned", SCORE_BANKS + 1)
         nc.scalar.copy(kb_win[:].rearrange("p (u c) -> p u c", u=POOL_PAGES)[:, :, 0:4], kb_own)
-        vs_own = turn(vs_rows, "vs_turned")
-        bias = shared.tile([P, B * N], F32, name="bias", offset=BIAS_AT, align_bytes=64)
-        nc.scalar.activation(bias[:], kb_win[:].indirect(off_t[:]), ACT.Copy)
+        bias = [shared.tile([P, N], F32, name="bias%d" % b, offset=BIAS_AT + 4 * N * b, align_bytes=64) for b in range(B)]
+        scale = [keep.tile([P, N], F32, name="scale%d" % b, align_bytes=64) for b in range(B)]
+        for b in range(B):
+            nc.scalar.activation(bias[b][:], kb_win[:].indirect(off_t[:, b * N // 16 : (b + 1) * N // 16]), ACT.Copy)
+            nc.scalar.activation(scale[b][:], vs_win[:].indirect(off_t[:, b * N // 16 : (b + 1) * N // 16]), ACT.Copy)
 
-        ks_rows = [
-            keep.tile([P, N], U8, name="ks_rows0", align_bytes=64),
-            shared.tile([P, N], U8, name="ks_rows1", offset=VS_AT, align_bytes=64),
-        ]
+        ks_rows = [keep.tile([P, N], U8, name="ks_rows%d" % b, align_bytes=64) for b in range(B)]
         for b in range(B):
             nc.vector.tensor_copy(ks_rows[b][:], ks_win[:].indirect(off_t[:, b * N // 16 : (b + 1) * N // 16]))
         for b in range(B):
@@ -114,22 +120,12 @@ def tile_attend_pkv4q_silu_kb_gate_kernel(
                 ks_rows[b][:].rearrange("p (j m t) -> p j t m", j=PAGES, t=4),
             )
         planes = keep.tile([P, PASSES * PLANE], U8, name="planes", align_bytes=64)
-        for quad in range(4):
+        for quad in (0, 2, 1, 3):
             first = P - KS_ROWS + 4 * PASSES * quad
             nc.sync.dma_start(
                 planes[32 * quad : 32 * quad + 4, :].bitcast(I32),
                 dealt[first : first + 4 * PASSES, :].bitcast(I32),
             )
-
-        vs_win = shared.tile([P, T], F32, name="vs_win", offset=VS_AT, align_bytes=64)
-        nc.gpsimd.memset(vs_win[:, BUILT * PAGE : T], 0.0)
-        nc.scalar.copy(
-            vs_win[:, 0 : BUILT * PAGE].rearrange("p (u r t) -> p u r t", u=BUILT, t=4),
-            vs_own[:, 0:BUILT, :].rearrange("p u (r t) -> p u r t", r=1).to_broadcast([P, BUILT, PAGE // 4, 4]),
-        )
-        nc.scalar.copy(vs_win[:].rearrange("p (u c) -> p u c", u=POOL_PAGES)[:, BUILT:, 0:4], vs_own[:, BUILT:, :])
-        scale = keep.tile([P, B * N], F32, name="scale", align_bytes=64)
-        nc.scalar.activation(scale[:], vs_win[:].indirect(off_t[:]), ACT.Copy)
 
         vw_win = keep.tile([P, POOL_PAGES * DV], U32, name="vw_win", align_bytes=64)
         nc.sync.dma_start(
@@ -139,18 +135,12 @@ def tile_attend_pkv4q_silu_kb_gate_kernel(
         og_t = keep.tile([P, B, DV], F32, name="og_t", align_bytes=64)
         nc.sync.dma_start(og_t[:], og.rearrange("b q e -> q b e"))
 
-        vsc = keep.tile([P, LISTED * DV], U8, name="vsc", align_bytes=64)
-        for quad in range(4):
-            first = P - VS_ROWS + 4 * quad
-            nc.sync.dma_start(
-                vsc[32 * quad : 32 * quad + 4, :].bitcast(I32),
-                vsc_rows[first : first + 4, :].bitcast(I32),
-            )
+        vsc = shared.tile([P, LISTED * DV], U8, name="vsc", offset=KW_AT, align_bytes=64)
 
         kws, kps, ps, wis, wq = {}, {}, {}, {}, {}
 
         def gather_keys(b):
-            kw = work.tile([P, N], U32, name="kw", bufs=2, align_bytes=64)
+            kw = shared.tile([P, N], U32, name="kw%d" % b, offset=KW_AT + 4 * N * b, align_bytes=64)
             nc.vector.tensor_copy(kw[:], kw_win[:].indirect(off_t[:, b * N // 16 : (b + 1) * N // 16]))
             kws[b] = kw
 
@@ -184,7 +174,7 @@ def tile_attend_pkv4q_silu_kb_gate_kernel(
                         )
                 for t in range(2 * h, 2 * h + 2):
                     nc.scalar.activation(
-                        p[:, t * NQ : (t + 1) * NQ], bank[:, t, :], ACT.Silu, bias=bias[:, j * PAGE + t : j * PAGE + t + 1]
+                        p[:, t * NQ : (t + 1) * NQ], bank[:, t, :], ACT.Silu, bias=bias[b][:, e * PAGE + t : e * PAGE + t + 1]
                     )
             ps[j] = p
 
@@ -193,7 +183,7 @@ def tile_attend_pkv4q_silu_kb_gate_kernel(
             nc.vector.tensor_tensor(
                 wi[:].rearrange("p (c i t) -> p c t i", t=4, i=2),
                 ps[j][:].rearrange("p (t c i) -> p c t i", t=4, i=2),
-                scale[:, j * PAGE : j * PAGE + 4].rearrange("p (a t b) -> p a t b", a=1, b=1).to_broadcast([P, NQ // 2, 4, 2]),
+                scale[j // PAGES][:, (j % PAGES) * PAGE : (j % PAGES) * PAGE + 4].rearrange("p (a t b) -> p a t b", a=1, b=1).to_broadcast([P, NQ // 2, 4, 2]),
                 ALU.mult,
             )
             wis[j] = wi
@@ -231,7 +221,14 @@ def tile_attend_pkv4q_silu_kb_gate_kernel(
             for e in range(PAGES):
                 score(b * PAGES + e)
 
-        half = shared.tile([P, B, DV], F32, name="half", offset=BIAS_AT, align_bytes=64)
+        for quad in range(4):
+            first = P - VS_ROWS + 4 * quad
+            nc.sync.dma_start(
+                vsc[32 * quad : 32 * quad + 4, :].bitcast(I32),
+                vsc_rows[first : first + 4, :].bitcast(I32),
+            )
+
+        half = shared.tile([P, B, DV], F32, name="half", offset=BIAS_AT + 4 * N, align_bytes=64)
         nc.scalar.activation(half[:], og_t[:], ACT.Tanh, scale=0.5)
         gate = keep.tile([P, B, DV], F32, name="gate")
         nc.scalar.activation(gate[:], half[:], ACT.Copy, scale=1.0 / 32.0, bias=1.0 / 32.0)

@@ -141,14 +141,17 @@ def tile_attend_pkv4q_silu_kb_gate_kernel(
 
         def gather_keys(b):
             kw = shared.tile([P, N], U32, name="kw%d" % b, offset=KW_AT + 4 * N * b, align_bytes=64)
-            nc.vector.tensor_copy(kw[:], kw_win[:].indirect(off_t[:, b * N // 16 : (b + 1) * N // 16]))
+            nc.vector.tensor_copy(
+                kw[:].rearrange("p (a m s) -> p m a s", a=2, s=2),
+                kw_win[:].indirect(off_t[:, b * N // 16 : (b + 1) * N // 16]),
+            )
             kws[b] = kw
 
         def part(b):
             kp = work.tile([P, PASSES * N], U16, name="kp", bufs=2, align_bytes=64)
             nc.vector.tensor_copy(
-                kp[:].rearrange("p (o t c i) -> p o c t i", o=PASSES, t=4, i=4),
-                kws[b][:].bitcast(U16).rearrange("p (c i t o) -> p o c t i", o=PASSES, t=4, i=4),
+                kp[:].rearrange("p (o s c i) -> p o c s i", o=PASSES, s=2, i=4),
+                kws[b][:].bitcast(U16).rearrange("p (c i s o) -> p o c s i", o=PASSES, s=2, i=4),
             )
             kps[b] = kp
 
@@ -160,7 +163,7 @@ def tile_attend_pkv4q_silu_kb_gate_kernel(
                 for t in range(2 * h, 2 * h + 2):
                     for o in range(PASSES):
                         g = b * PASSES + o
-                        kat = o * N + (t * PAGES + e) * P
+                        kat = o * N + ((t % 2) * 2 * PAGES + (t // 2) * PAGES + e) * P
                         at = o * PLANE + j * PAGE + t * P
                         qat = o * PLANE + B * N + b * NQ
                         nc.tensor.matmul_mx(

@@ -25,12 +25,12 @@ ALU = mybir.AluOpType
 
 KS_ROWS = 16 * PASSES
 VS_ROWS = 16
-PLANE = B * N + B * NQ
+PLANE = N + NQ
 ROWS_AT = 0
 BIAS_AT = ROWS_AT + 4 * PAGE
 KW_AT = BIAS_AT + 4 * B * N
-POOL_FROM = 1024
-BUILT = 6
+VW_AT = KW_AT + 4 * B * N
+POOL_FROM = 2048
 BANK = 2048
 SCORE_BANKS = 6
 
@@ -48,12 +48,16 @@ def tile_attend_pkv4q_silu_kb_gate_kernel(
 
         vs_rows = shared.tile([P, PAGE], F32, name="vs_rows", offset=ROWS_AT, align_bytes=64)
         nc.scalar.dma_start(vs_rows[P - POOL_PAGES : P, :], vs[0, :].rearrange("(u c) -> u c", u=POOL_PAGES))
-        dealt = keep.tile([P, PLANE], U8, name="dealt", align_bytes=64)
+        dealt = [keep.tile([P, PLANE], U8, name="dealt%d" % b, align_bytes=64) for b in range(B)]
         for b in range(B):
             nc.scalar.dma_start(
-                dealt[P - KS_ROWS : P, B * N + b * NQ : B * N + (b + 1) * NQ].bitcast(I32),
+                dealt[b][P - KS_ROWS : P, N:PLANE].bitcast(I32),
                 q_scales[b].rearrange("o f q -> f o q").bitcast(I32),
             )
+        ks_win = keep.tile([P, T], U8, name="ks_win", align_bytes=64)
+        nc.sync.dma_start(ks_win[P - KS_ROWS : P, :].bitcast(I32), k_scales.rearrange("o f t -> f o t").bitcast(I32))
+        off_t = lists.tile([P, B * N // 16], U16, name="off_t")
+        nc.sync.dma_start(off_t[:], offs)
         vsc_win = keep.tile([P, POOL_PAGES * DV], U8, name="vsc_win", align_bytes=64)
         nc.sync.dma_start(
             vsc_win[P - VS_ROWS : P, :].bitcast(I32).rearrange("f (u e) -> f u e", u=POOL_PAGES),
@@ -61,10 +65,6 @@ def tile_attend_pkv4q_silu_kb_gate_kernel(
         )
         voff_t = lists.tile([P, LISTED * DV // 16], U16, name="voff_t")
         nc.sync.dma_start(voff_t[:], voffs)
-        ks_win = keep.tile([P, T], U8, name="ks_win", align_bytes=64)
-        nc.sync.dma_start(ks_win[P - KS_ROWS : P, :].bitcast(I32), k_scales.rearrange("o f t -> f o t").bitcast(I32))
-        off_t = lists.tile([P, B * N // 16], U16, name="off_t")
-        nc.sync.dma_start(off_t[:], offs)
         kw_win = keep.tile([P, T], U32, name="kw_win", align_bytes=64)
         nc.sync.dma_start(kw_win[:].bitcast(I32), k_words[0].rearrange("p t r -> p (t r)").bitcast(I32))
         qw = keep.tile([P, B * PASSES * NQ], U32, name="qw", align_bytes=64)
@@ -72,6 +72,8 @@ def tile_attend_pkv4q_silu_kb_gate_kernel(
             qw[:].bitcast(I32).rearrange("p (g q) -> p g q", q=NQ),
             q_words.rearrange("b o p q r -> p (b o) (q r)").bitcast(I32),
         )
+        og_t = keep.tile([P, B, DV], F32, name="og_t", align_bytes=64)
+        nc.sync.dma_start(og_t[:], og.rearrange("b q e -> q b e"))
 
         ident = keep.tile([P, P], F32, name="ident")
         make_identity(nc, ident[:])
@@ -79,15 +81,11 @@ def tile_attend_pkv4q_silu_kb_gate_kernel(
         nc.scalar.activation(warm[:], ident[:, 0:1], ACT.Silu)
 
         kb_win = keep.tile([P, T], F32, name="kb_win", align_bytes=64)
-        nc.vector.memset(vsc_win[0 : P - VS_ROWS, :].bitcast(I32), 0)
         nc.vector.memset(ks_win[0 : P - KS_ROWS, :].bitcast(I32), 0)
+        nc.vector.memset(vsc_win[0 : P - VS_ROWS, :].bitcast(I32), 0)
         vs_win = keep.tile([P, T], F32, name="vs_win", align_bytes=64)
-        nc.vector.memset(vs_win[:, BUILT * PAGE : T], 0.0)
         nc.vector.memset(kb_win[:, 0:POOL_FROM], 0.0)
         nc.gpsimd.memset(kb_win[:, POOL_FROM - 8 : T], 0.0)
-
-        vsc_rows = keep.tile([P, LISTED * DV], U8, name="vsc_rows", align_bytes=64)
-        nc.vector.tensor_copy(vsc_rows[:], vsc_win[:].indirect(voff_t[:]))
 
         def turn(rows, name, at):
             bank = psum.tile([P, 4, P], F32, name=name, offset=at * BANK)
@@ -99,10 +97,9 @@ def tile_attend_pkv4q_silu_kb_gate_kernel(
         kb_rows = shared.tile([P, PAGE], F32, name="kb_rows", offset=ROWS_AT, align_bytes=64)
         nc.scalar.dma_start(kb_rows[P - POOL_PAGES : P, :], kb[0, :].rearrange("(u c) -> u c", u=POOL_PAGES))
         nc.scalar.copy(
-            vs_win[:, 0 : BUILT * PAGE].rearrange("p (u r t) -> p u r t", u=BUILT, t=4),
-            vs_own[:, 0:BUILT, :].rearrange("p u (r t) -> p u r t", r=1).to_broadcast([P, BUILT, PAGE // 4, 4]),
+            vs_win[:].rearrange("p (u r t) -> p u r t", u=POOL_PAGES, t=4),
+            vs_own.rearrange("p u (r t) -> p u r t", r=1).to_broadcast([P, POOL_PAGES, PAGE // 4, 4]),
         )
-        nc.scalar.copy(vs_win[:].rearrange("p (u c) -> p u c", u=POOL_PAGES)[:, BUILT:, 0:4], vs_own[:, BUILT:, :])
         kb_own = turn(kb_rows, "kb_turned", SCORE_BANKS + 1)
         nc.scalar.copy(kb_win[:].rearrange("p (u c) -> p u c", u=POOL_PAGES)[:, :, 0:4], kb_own)
         bias = [shared.tile([P, N], F32, name="bias%d" % b, offset=BIAS_AT + 4 * N * b, align_bytes=64) for b in range(B)]
@@ -111,29 +108,33 @@ def tile_attend_pkv4q_silu_kb_gate_kernel(
             nc.scalar.activation(bias[b][:], kb_win[:].indirect(off_t[:, b * N // 16 : (b + 1) * N // 16]), ACT.Copy)
             nc.scalar.activation(scale[b][:], vs_win[:].indirect(off_t[:, b * N // 16 : (b + 1) * N // 16]), ACT.Copy)
 
-        ks_rows = [keep.tile([P, N], U8, name="ks_rows%d" % b, align_bytes=64) for b in range(B)]
+        ks_rows = [
+            shared.tile([P, N], U8, name="ks_rows0", offset=VW_AT, align_bytes=64),
+            keep.tile([P, N], U8, name="ks_rows1", align_bytes=64),
+        ]
         for b in range(B):
             nc.vector.tensor_copy(ks_rows[b][:], ks_win[:].indirect(off_t[:, b * N // 16 : (b + 1) * N // 16]))
+        planes = [keep.tile([P, PASSES * PLANE], U8, name="planes%d" % b, align_bytes=64) for b in range(B)]
+        vw_win = shared.tile([P, POOL_PAGES * DV], U32, name="vw_win", offset=VW_AT, align_bytes=64)
         for b in range(B):
             nc.vector.tensor_copy(
-                dealt[:, b * N : (b + 1) * N].rearrange("p (j t m) -> p j t m", j=PAGES, t=4),
+                dealt[b][:, 0:N].rearrange("p (j t m) -> p j t m", j=PAGES, t=4),
                 ks_rows[b][:].rearrange("p (j m t) -> p j t m", j=PAGES, t=4),
             )
-        planes = keep.tile([P, PASSES * PLANE], U8, name="planes", align_bytes=64)
-        for quad in (0, 2, 1, 3):
-            first = P - KS_ROWS + 4 * PASSES * quad
-            nc.sync.dma_start(
-                planes[32 * quad : 32 * quad + 4, :].bitcast(I32),
-                dealt[first : first + 4 * PASSES, :].bitcast(I32),
-            )
+            for quad in (0, 2, 1, 3):
+                first = P - KS_ROWS + 4 * PASSES * quad
+                nc.sync.dma_start(
+                    planes[b][32 * quad : 32 * quad + 4, :].bitcast(I32),
+                    dealt[b][first : first + 4 * PASSES, :].bitcast(I32),
+                )
+            if b == 0:
+                nc.sync.dma_start(
+                    vw_win[:].bitcast(I32).rearrange("p (u e) -> p u e", u=POOL_PAGES),
+                    v_words.rearrange("u p e r -> p u (e r)").bitcast(I32),
+                )
 
-        vw_win = keep.tile([P, POOL_PAGES * DV], U32, name="vw_win", align_bytes=64)
-        nc.sync.dma_start(
-            vw_win[:].bitcast(I32).rearrange("p (u e) -> p u e", u=POOL_PAGES),
-            v_words.rearrange("u p e r -> p u (e r)").bitcast(I32),
-        )
-        og_t = keep.tile([P, B, DV], F32, name="og_t", align_bytes=64)
-        nc.sync.dma_start(og_t[:], og.rearrange("b q e -> q b e"))
+        vsc_rows = keep.tile([P, LISTED * DV], U8, name="vsc_rows", align_bytes=64)
+        nc.vector.tensor_copy(vsc_rows[:], vsc_win[:].indirect(voff_t[:]))
 
         vsc = shared.tile([P, LISTED * DV], U8, name="vsc", offset=KW_AT, align_bytes=64)
 
@@ -164,14 +165,14 @@ def tile_attend_pkv4q_silu_kb_gate_kernel(
                     for o in range(PASSES):
                         g = b * PASSES + o
                         kat = o * N + ((t % 2) * 2 * PAGES + (t // 2) * PAGES + e) * P
-                        at = o * PLANE + j * PAGE + t * P
-                        qat = o * PLANE + B * N + b * NQ
+                        at = o * PLANE + e * PAGE + t * P
+                        qat = o * PLANE + N
                         nc.tensor.matmul_mx(
                             out=bank[:, t, :],
                             lhsT=kps[b][:, kat : kat + P].bitcast(FP4X4),
-                            lhsT_scale=planes[:, at : at + P],
+                            lhsT_scale=planes[b][:, at : at + P],
                             rhs=qw[:, g * NQ : (g + 1) * NQ].bitcast(FP8X4),
-                            rhs_scale=planes[:, qat : qat + NQ],
+                            rhs_scale=planes[b][:, qat : qat + NQ],
                             start=(o == 0),
                             stop=(o == PASSES - 1),
                         )
@@ -182,7 +183,10 @@ def tile_attend_pkv4q_silu_kb_gate_kernel(
             ps[j] = p
 
         def weigh(j):
-            wi = work.tile([P, 4 * NQ], BF16, name="wi", align_bytes=64)
+            if j == 0:
+                wi = keep.tile([P, 4 * NQ], BF16, name="wi0", align_bytes=64)
+            else:
+                wi = shared.tile([P, 4 * NQ], BF16, name="wi%d" % j, offset=VW_AT + 8 * NQ * j, align_bytes=64)
             nc.vector.tensor_tensor(
                 wi[:].rearrange("p (c i t) -> p c t i", t=4, i=2),
                 ps[j][:].rearrange("p (t c i) -> p c t i", t=4, i=2),

@@ -26,11 +26,15 @@ ALU = mybir.AluOpType
 KS_ROWS = 16 * PASSES
 VS_ROWS = 16
 PLANE = N + NQ
-ROWS_AT = 0
-BIAS_AT = ROWS_AT + 4 * PAGE
+BIAS_AT = 0
 KW_AT = BIAS_AT + 4 * B * N
 VW_AT = KW_AT + 4 * B * N
-POOL_FROM = 2048
+OG_AT = VW_AT + 4 * POOL_PAGES * DV
+VS_AT = OG_AT + 4 * B * DV
+KB_AT = VS_AT + 4 * T
+POOL_FROM = 768
+KB_ZEROED = 6
+VS_ZEROED = 5
 BANK = 2048
 SCORE_BANKS = 6
 
@@ -46,14 +50,19 @@ def tile_attend_pkv4q_silu_kb_gate_kernel(
         work = ctx.enter_context(tc.tile_pool(name="work", bufs=4))
         psum = ctx.enter_context(tc.psum_pool(name="psum", bufs=1))
 
-        vs_rows = shared.tile([P, PAGE], F32, name="vs_rows", offset=ROWS_AT, align_bytes=64)
+        kb_rows = keep.tile([P, PAGE], F32, name="kb_rows", align_bytes=64)
+        nc.scalar.dma_start(kb_rows[P - POOL_PAGES : P, :], kb[0, :].rearrange("(u c) -> u c", u=POOL_PAGES))
+        vs_rows = keep.tile([P, PAGE], F32, name="vs_rows", align_bytes=64)
         nc.scalar.dma_start(vs_rows[P - POOL_PAGES : P, :], vs[0, :].rearrange("(u c) -> u c", u=POOL_PAGES))
         dealt = [keep.tile([P, PLANE], U8, name="dealt%d" % b, align_bytes=64) for b in range(B)]
-        for b in range(B):
-            nc.scalar.dma_start(
+
+        def load_query_scales(queue, b):
+            queue.dma_start(
                 dealt[b][P - KS_ROWS : P, N:PLANE].bitcast(I32),
                 q_scales[b].rearrange("o f q -> f o q").bitcast(I32),
             )
+
+        load_query_scales(nc.scalar, 0)
         ks_win = keep.tile([P, T], U8, name="ks_win", align_bytes=64)
         nc.sync.dma_start(ks_win[P - KS_ROWS : P, :].bitcast(I32), k_scales.rearrange("o f t -> f o t").bitcast(I32))
         off_t = lists.tile([P, B * N // 16], U16, name="off_t")
@@ -72,20 +81,18 @@ def tile_attend_pkv4q_silu_kb_gate_kernel(
             qw[:].bitcast(I32).rearrange("p (g q) -> p g q", q=NQ),
             q_words.rearrange("b o p q r -> p (b o) (q r)").bitcast(I32),
         )
-        og_t = keep.tile([P, B, DV], F32, name="og_t", align_bytes=64)
-        nc.sync.dma_start(og_t[:], og.rearrange("b q e -> q b e"))
+        load_query_scales(nc.sync, 1)
 
         ident = keep.tile([P, P], F32, name="ident")
         make_identity(nc, ident[:])
         warm = keep.tile([P, 1], F32, name="warm")
         nc.scalar.activation(warm[:], ident[:, 0:1], ACT.Silu)
 
-        kb_win = keep.tile([P, T], F32, name="kb_win", align_bytes=64)
+        kb_win = shared.tile([P, T], F32, name="kb_win", offset=KB_AT, align_bytes=64)
         nc.vector.memset(ks_win[0 : P - KS_ROWS, :].bitcast(I32), 0)
         nc.vector.memset(vsc_win[0 : P - VS_ROWS, :].bitcast(I32), 0)
-        vs_win = keep.tile([P, T], F32, name="vs_win", align_bytes=64)
         nc.vector.memset(kb_win[:, 0:POOL_FROM], 0.0)
-        nc.gpsimd.memset(kb_win[:, POOL_FROM - 8 : T], 0.0)
+        nc.gpsimd.memset(kb_win[:, POOL_FROM - 8 : KB_ZEROED * PAGE], 0.0)
 
         def turn(rows, name, at):
             bank = psum.tile([P, 4, P], F32, name=name, offset=at * BANK)
@@ -93,24 +100,26 @@ def tile_attend_pkv4q_silu_kb_gate_kernel(
                 nc.tensor.transpose(bank[:, t, :], rows[:, t:PAGE:4], ident[:])
             return bank[:, :, P - POOL_PAGES : P].rearrange("p t u -> p u t")
 
-        vs_own = turn(vs_rows, "vs_turned", SCORE_BANKS)
-        kb_rows = shared.tile([P, PAGE], F32, name="kb_rows", offset=ROWS_AT, align_bytes=64)
-        nc.scalar.dma_start(kb_rows[P - POOL_PAGES : P, :], kb[0, :].rearrange("(u c) -> u c", u=POOL_PAGES))
-        nc.scalar.copy(
-            vs_win[:].rearrange("p (u r t) -> p u r t", u=POOL_PAGES, t=4),
-            vs_own.rearrange("p u (r t) -> p u r t", r=1).to_broadcast([P, POOL_PAGES, PAGE // 4, 4]),
-        )
-        kb_own = turn(kb_rows, "kb_turned", SCORE_BANKS + 1)
-        nc.scalar.copy(kb_win[:].rearrange("p (u c) -> p u c", u=POOL_PAGES)[:, :, 0:4], kb_own)
+        def lay(win, turned, zeroed, own):
+            nc.scalar.copy(own[:, :, 0, :], turned)
+            pages = win[:].rearrange("p (u r t) -> p u r t", u=POOL_PAGES, t=4)
+            nc.scalar.copy(pages[:, zeroed:, :, :], own[:, zeroed:, :, :].to_broadcast([P, POOL_PAGES - zeroed, PAGE // 4, 4]))
+            nc.scalar.copy(pages[:, 0:zeroed, 0, :], own[:, 0:zeroed, 0, :])
+
+        def gather_floats(dst, win):
+            for b in range(B):
+                nc.scalar.activation(dst[b][:], win[:].indirect(off_t[:, b * N // 16 : (b + 1) * N // 16]), ACT.Copy)
+
+        kb_turned = turn(kb_rows, "kb_turned", SCORE_BANKS)
+        kb_own = keep.tile([P, POOL_PAGES, 1, 4], F32, name="kb_own", align_bytes=64)
+        lay(kb_win, kb_turned, KB_ZEROED, kb_own)
         bias = [shared.tile([P, N], F32, name="bias%d" % b, offset=BIAS_AT + 4 * N * b, align_bytes=64) for b in range(B)]
-        scale = [keep.tile([P, N], F32, name="scale%d" % b, align_bytes=64) for b in range(B)]
-        for b in range(B):
-            nc.scalar.activation(bias[b][:], kb_win[:].indirect(off_t[:, b * N // 16 : (b + 1) * N // 16]), ACT.Copy)
-            nc.scalar.activation(scale[b][:], vs_win[:].indirect(off_t[:, b * N // 16 : (b + 1) * N // 16]), ACT.Copy)
+        gather_floats(bias, kb_win)
+        vs_turned = turn(vs_rows, "vs_turned", SCORE_BANKS + 1)
 
         ks_rows = [
             shared.tile([P, N], U8, name="ks_rows0", offset=VW_AT, align_bytes=64),
-            keep.tile([P, N], U8, name="ks_rows1", align_bytes=64),
+            shared.tile([P, N], U8, name="ks_rows1", offset=VS_AT - N // 2, align_bytes=64),
         ]
         for b in range(B):
             nc.vector.tensor_copy(ks_rows[b][:], ks_win[:].indirect(off_t[:, b * N // 16 : (b + 1) * N // 16]))
@@ -132,6 +141,16 @@ def tile_attend_pkv4q_silu_kb_gate_kernel(
                     vw_win[:].bitcast(I32).rearrange("p (u e) -> p u e", u=POOL_PAGES),
                     v_words.rearrange("u p e r -> p u (e r)").bitcast(I32),
                 )
+
+        og_t = shared.tile([P, B, DV], F32, name="og_t", offset=OG_AT, align_bytes=64)
+        nc.sync.dma_start(og_t[:], og.rearrange("b q e -> q b e"))
+
+        vs_win = shared.tile([P, T], F32, name="vs_win", offset=VS_AT, align_bytes=64)
+        nc.gpsimd.memset(vs_win[:, 0 : VS_ZEROED * PAGE], 0.0)
+        vs_own = shared.tile([P, POOL_PAGES, 1, 4], F32, name="vs_own", offset=KB_AT, align_bytes=64)
+        lay(vs_win, vs_turned, VS_ZEROED, vs_own)
+        scale = [keep.tile([P, N], F32, name="scale%d" % b, align_bytes=64) for b in range(B)]
+        gather_floats(scale, vs_win)
 
         vsc_rows = keep.tile([P, LISTED * DV], U8, name="vsc_rows", align_bytes=64)
         nc.vector.tensor_copy(vsc_rows[:], vsc_win[:].indirect(voff_t[:]))
@@ -158,7 +177,7 @@ def tile_attend_pkv4q_silu_kb_gate_kernel(
 
         def score(j):
             b, e = divmod(j, PAGES)
-            p = work.tile([P, PAGE], F32, name="p", align_bytes=64)
+            p = shared.tile([P, PAGE], F32, name="p%d" % j, offset=VS_AT + 4 * PAGE * j, align_bytes=64)
             for h in range(2):
                 bank = psum.tile([P, 4, P], F32, name="sc%d_%d" % (j, h), offset=((2 * j + h) % SCORE_BANKS) * BANK)
                 for t in range(2 * h, 2 * h + 2):

@@ -30,11 +30,12 @@ BIAS_AT = 0
 KW_AT = BIAS_AT + 4 * B * N
 VW_AT = KW_AT + 4 * B * N
 OG_AT = VW_AT + 4 * POOL_PAGES * DV
-VS_AT = OG_AT + 4 * B * DV
-KB_AT = VS_AT + 4 * T
-POOL_FROM = 768
-KB_ZEROED = 6
-VS_ZEROED = 5
+KB_AT = OG_AT + 4 * B * DV
+VS_AT = KB_AT + 4 * T
+POOL_FROM = 5 * PAGE // 2
+VS_ZEROED = 7 * PAGE
+KB_ZEROED = 11 * PAGE // 2
+OWN = 4 * POOL_PAGES
 BANK = 2048
 SCORE_BANKS = 6
 
@@ -50,10 +51,10 @@ def tile_attend_pkv4q_silu_kb_gate_kernel(
         work = ctx.enter_context(tc.tile_pool(name="work", bufs=4))
         psum = ctx.enter_context(tc.psum_pool(name="psum", bufs=1))
 
-        kb_rows = keep.tile([P, PAGE], F32, name="kb_rows", align_bytes=64)
-        nc.scalar.dma_start(kb_rows[P - POOL_PAGES : P, :], kb[0, :].rearrange("(u c) -> u c", u=POOL_PAGES))
         vs_rows = keep.tile([P, PAGE], F32, name="vs_rows", align_bytes=64)
         nc.scalar.dma_start(vs_rows[P - POOL_PAGES : P, :], vs[0, :].rearrange("(u c) -> u c", u=POOL_PAGES))
+        kb_rows = keep.tile([P, PAGE], F32, name="kb_rows", align_bytes=64)
+        nc.scalar.dma_start(kb_rows[P - POOL_PAGES : P, :], kb[0, :].rearrange("(u c) -> u c", u=POOL_PAGES))
         dealt = [keep.tile([P, PLANE], U8, name="dealt%d" % b, align_bytes=64) for b in range(B)]
 
         def load_query_scales(queue, b):
@@ -88,11 +89,11 @@ def tile_attend_pkv4q_silu_kb_gate_kernel(
         warm = keep.tile([P, 1], F32, name="warm")
         nc.scalar.activation(warm[:], ident[:, 0:1], ACT.Silu)
 
-        kb_win = shared.tile([P, T], F32, name="kb_win", offset=KB_AT, align_bytes=64)
+        vs_win = shared.tile([P, T], F32, name="vs_win", offset=VS_AT, align_bytes=64)
         nc.vector.memset(ks_win[0 : P - KS_ROWS, :].bitcast(I32), 0)
         nc.vector.memset(vsc_win[0 : P - VS_ROWS, :].bitcast(I32), 0)
-        nc.vector.memset(kb_win[:, 0:POOL_FROM], 0.0)
-        nc.gpsimd.memset(kb_win[:, POOL_FROM - 8 : KB_ZEROED * PAGE], 0.0)
+        nc.vector.memset(vs_win[:, 0:POOL_FROM], 0.0)
+        nc.gpsimd.memset(vs_win[:, POOL_FROM - 8 : VS_ZEROED], 0.0)
 
         def turn(rows, name, at):
             bank = psum.tile([P, 4, P], F32, name=name, offset=at * BANK)
@@ -101,25 +102,26 @@ def tile_attend_pkv4q_silu_kb_gate_kernel(
             return bank[:, :, P - POOL_PAGES : P].rearrange("p t u -> p u t")
 
         def lay(win, turned, zeroed, own):
-            nc.scalar.copy(own[:, :, 0, :], turned)
-            pages = win[:].rearrange("p (u r t) -> p u r t", u=POOL_PAGES, t=4)
-            nc.scalar.copy(pages[:, zeroed:, :, :], own[:, zeroed:, :, :].to_broadcast([P, POOL_PAGES - zeroed, PAGE // 4, 4]))
-            nc.scalar.copy(pages[:, 0:zeroed, 0, :], own[:, 0:zeroed, 0, :])
+            nc.scalar.copy(own[:, 0, :].rearrange("p (u t) -> p u t", t=4), turned)
+            nc.scalar.copy(
+                win[:, zeroed:T].rearrange("p (r c) -> p r c", c=OWN),
+                own[:].to_broadcast([P, (T - zeroed) // OWN, OWN]),
+            )
+            nc.scalar.copy(
+                win[:].rearrange("p (u c) -> p u c", u=POOL_PAGES)[:, :, 0:4],
+                own[:, 0, :].rearrange("p (u t) -> p u t", t=4),
+            )
 
-        def gather_floats(dst, win):
-            for b in range(B):
-                nc.scalar.activation(dst[b][:], win[:].indirect(off_t[:, b * N // 16 : (b + 1) * N // 16]), ACT.Copy)
-
-        kb_turned = turn(kb_rows, "kb_turned", SCORE_BANKS)
-        kb_own = keep.tile([P, POOL_PAGES, 1, 4], F32, name="kb_own", align_bytes=64)
-        lay(kb_win, kb_turned, KB_ZEROED, kb_own)
-        bias = [shared.tile([P, N], F32, name="bias%d" % b, offset=BIAS_AT + 4 * N * b, align_bytes=64) for b in range(B)]
-        gather_floats(bias, kb_win)
-        vs_turned = turn(vs_rows, "vs_turned", SCORE_BANKS + 1)
+        vs_turned = turn(vs_rows, "vs_turned", SCORE_BANKS)
+        kb_turned = turn(kb_rows, "kb_turned", SCORE_BANKS + 1)
+        vs_own = keep.tile([P, 1, OWN], F32, name="vs_own", align_bytes=64)
+        lay(vs_win, vs_turned, VS_ZEROED, vs_own)
+        scale = keep.tile([P, B * N], F32, name="scale", align_bytes=64)
+        nc.scalar.activation(scale[:], vs_win[:].indirect(off_t[:]), ACT.Copy)
 
         ks_rows = [
             shared.tile([P, N], U8, name="ks_rows0", offset=VW_AT, align_bytes=64),
-            shared.tile([P, N], U8, name="ks_rows1", offset=VS_AT - N // 2, align_bytes=64),
+            shared.tile([P, N], U8, name="ks_rows1", offset=KB_AT - N // 2, align_bytes=64),
         ]
         for b in range(B):
             nc.vector.tensor_copy(ks_rows[b][:], ks_win[:].indirect(off_t[:, b * N // 16 : (b + 1) * N // 16]))
@@ -145,12 +147,12 @@ def tile_attend_pkv4q_silu_kb_gate_kernel(
         og_t = shared.tile([P, B, DV], F32, name="og_t", offset=OG_AT, align_bytes=64)
         nc.sync.dma_start(og_t[:], og.rearrange("b q e -> q b e"))
 
-        vs_win = shared.tile([P, T], F32, name="vs_win", offset=VS_AT, align_bytes=64)
-        nc.gpsimd.memset(vs_win[:, 0 : VS_ZEROED * PAGE], 0.0)
-        vs_own = shared.tile([P, POOL_PAGES, 1, 4], F32, name="vs_own", offset=KB_AT, align_bytes=64)
-        lay(vs_win, vs_turned, VS_ZEROED, vs_own)
-        scale = [keep.tile([P, N], F32, name="scale%d" % b, align_bytes=64) for b in range(B)]
-        gather_floats(scale, vs_win)
+        kb_win = shared.tile([P, T], F32, name="kb_win", offset=KB_AT, align_bytes=64)
+        nc.gpsimd.memset(kb_win[:, 0:KB_ZEROED], 0.0)
+        kb_own = shared.tile([P, 1, OWN], F32, name="kb_own", offset=VS_AT, align_bytes=64)
+        lay(kb_win, kb_turned, KB_ZEROED, kb_own)
+        bias = shared.tile([P, B * N], F32, name="bias", offset=BIAS_AT, align_bytes=64)
+        nc.scalar.activation(bias[:], kb_win[:].indirect(off_t[:]), ACT.Copy)
 
         vsc_rows = keep.tile([P, LISTED * DV], U8, name="vsc_rows", align_bytes=64)
         nc.vector.tensor_copy(vsc_rows[:], vsc_win[:].indirect(voff_t[:]))
@@ -177,7 +179,7 @@ def tile_attend_pkv4q_silu_kb_gate_kernel(
 
         def score(j):
             b, e = divmod(j, PAGES)
-            p = shared.tile([P, PAGE], F32, name="p%d" % j, offset=VS_AT + 4 * PAGE * j, align_bytes=64)
+            p = work.tile([P, PAGE], F32, name="p", align_bytes=64)
             for h in range(2):
                 bank = psum.tile([P, 4, P], F32, name="sc%d_%d" % (j, h), offset=((2 * j + h) % SCORE_BANKS) * BANK)
                 for t in range(2 * h, 2 * h + 2):
@@ -197,7 +199,7 @@ def tile_attend_pkv4q_silu_kb_gate_kernel(
                         )
                 for t in range(2 * h, 2 * h + 2):
                     nc.scalar.activation(
-                        p[:, t * NQ : (t + 1) * NQ], bank[:, t, :], ACT.Silu, bias=bias[b][:, e * PAGE + t : e * PAGE + t + 1]
+                        p[:, t * NQ : (t + 1) * NQ], bank[:, t, :], ACT.Silu, bias=bias[:, j * PAGE + t : j * PAGE + t + 1]
                     )
             ps[j] = p
 
@@ -209,7 +211,7 @@ def tile_attend_pkv4q_silu_kb_gate_kernel(
             nc.vector.tensor_tensor(
                 wi[:].rearrange("p (c i t) -> p c t i", t=4, i=2),
                 ps[j][:].rearrange("p (t c i) -> p c t i", t=4, i=2),
-                scale[j // PAGES][:, (j % PAGES) * PAGE : (j % PAGES) * PAGE + 4].rearrange("p (a t b) -> p a t b", a=1, b=1).to_broadcast([P, NQ // 2, 4, 2]),
+                scale[:, j * PAGE : j * PAGE + 4].rearrange("p (a t b) -> p a t b", a=1, b=1).to_broadcast([P, NQ // 2, 4, 2]),
                 ALU.mult,
             )
             wis[j] = wi
@@ -236,7 +238,7 @@ def tile_attend_pkv4q_silu_kb_gate_kernel(
             return y
 
         def finish(b, y, gate):
-            res = work.tile([P, DV], F32, name="res")
+            res = shared.tile([P, DV], F32, name="res%d" % b, offset=VW_AT + 8 * NQ * (LISTED - 1 + b), align_bytes=64)
             nc.vector.tensor_tensor(res[:], y[:], gate[:, b, :], ALU.mult)
             nc.sync.dma_start(out[b], res[:])
 
@@ -254,7 +256,7 @@ def tile_attend_pkv4q_silu_kb_gate_kernel(
                 vsc_rows[first : first + 4, :].bitcast(I32),
             )
 
-        half = shared.tile([P, B, DV], F32, name="half", offset=BIAS_AT + 4 * N, align_bytes=64)
+        half = shared.tile([P, B, DV], F32, name="half", offset=BIAS_AT, align_bytes=64)
         nc.scalar.activation(half[:], og_t[:], ACT.Tanh, scale=0.5)
         gate = keep.tile([P, B, DV], F32, name="gate")
         nc.scalar.activation(gate[:], half[:], ACT.Copy, scale=1.0 / 32.0, bias=1.0 / 32.0)

@@ -32,8 +32,8 @@ VW_AT = KW_AT + 4 * B * N
 OG_AT = VW_AT + 4 * POOL_PAGES * DV
 KB_AT = OG_AT + 4 * B * DV
 VS_AT = KB_AT + 4 * T
-POOL_FROM = 5 * PAGE // 2
-VS_ZEROED = 7 * PAGE
+POOL_FROM = 3 * PAGE // 2
+VS_ZEROED = 11 * PAGE // 2
 KB_ZEROED = 11 * PAGE // 2
 OWN = 4 * POOL_PAGES
 BANK = 2048
@@ -52,9 +52,9 @@ def tile_attend_pkv4q_silu_kb_gate_kernel(
         psum = ctx.enter_context(tc.psum_pool(name="psum", bufs=1))
 
         vs_rows = keep.tile([P, PAGE], F32, name="vs_rows", align_bytes=64)
-        nc.scalar.dma_start(vs_rows[P - POOL_PAGES : P, :], vs[0, :].rearrange("(u c) -> u c", u=POOL_PAGES))
+        nc.scalar.dma_start(vs_rows[0 : 4 * POOL_PAGES : 4, :], vs[0, :].rearrange("(u c) -> u c", u=POOL_PAGES))
         kb_rows = keep.tile([P, PAGE], F32, name="kb_rows", align_bytes=64)
-        nc.scalar.dma_start(kb_rows[P - POOL_PAGES : P, :], kb[0, :].rearrange("(u c) -> u c", u=POOL_PAGES))
+        nc.scalar.dma_start(kb_rows[0 : 4 * POOL_PAGES : 4, :], kb[0, :].rearrange("(u c) -> u c", u=POOL_PAGES))
         dealt = [keep.tile([P, PLANE], U8, name="dealt%d" % b, align_bytes=64) for b in range(B)]
 
         def load_query_scales(queue, b):
@@ -85,7 +85,8 @@ def tile_attend_pkv4q_silu_kb_gate_kernel(
         load_query_scales(nc.sync, 1)
 
         ident = keep.tile([P, P], F32, name="ident")
-        make_identity(nc, ident[:])
+        nc.vector.memset(ident[:], 0.0)
+        make_identity(nc, ident[:], nomemset=True)
         warm = keep.tile([P, 1], F32, name="warm")
         nc.scalar.activation(warm[:], ident[:, 0:1], ACT.Silu)
 
@@ -99,7 +100,7 @@ def tile_attend_pkv4q_silu_kb_gate_kernel(
             bank = psum.tile([P, 4, P], F32, name=name, offset=at * BANK)
             for t in range(4):
                 nc.tensor.transpose(bank[:, t, :], rows[:, t:PAGE:4], ident[:])
-            return bank[:, :, P - POOL_PAGES : P].rearrange("p t u -> p u t")
+            return bank[:, :, 0 : 4 * POOL_PAGES : 4].rearrange("p t u -> p u t")
 
         def lay(win, turned, zeroed, own):
             nc.scalar.copy(own[:, 0, :].rearrange("p (u t) -> p u t", t=4), turned)

@@ -26,16 +26,17 @@ ALU = mybir.AluOpType
 KS_ROWS = 16 * PASSES
 VS_ROWS = 16
 PLANE = N + NQ
-BIAS_AT = 0
-KW_AT = BIAS_AT + 4 * B * N
+KW_AT = 0
 VW_AT = KW_AT + 4 * B * N
-OG_AT = VW_AT + 4 * POOL_PAGES * DV
-KB_AT = OG_AT + 4 * B * DV
-VS_AT = KB_AT + 4 * T
-POOL_FROM = 3 * PAGE // 2
-VS_ZEROED = 11 * PAGE // 2
-KB_ZEROED = 11 * PAGE // 2
-OWN = 4 * POOL_PAGES
+KB_AT = VW_AT + 4 * POOL_PAGES * DV
+OG_AT = KB_AT + 4 * T
+OWN_AT = OG_AT + 4 * B * DV
+KP_AT = OWN_AT + 4 * POOL_PAGES * 8
+RUN = 8
+VS_FILLED = 64
+KB_FILLED = 160
+SLOW_TO = VS_FILLED + 7 * RUN
+POOL_FROM = 272
 BANK = 2048
 SCORE_BANKS = 6
 
@@ -90,11 +91,13 @@ def tile_attend_pkv4q_silu_kb_gate_kernel(
         warm = keep.tile([P, 1], F32, name="warm")
         nc.scalar.activation(warm[:], ident[:, 0:1], ACT.Silu)
 
-        vs_win = shared.tile([P, T], F32, name="vs_win", offset=VS_AT, align_bytes=64)
+        vs_win = keep.tile([P, T], F32, name="vs_win", align_bytes=64)
+        vs_pages = vs_win[:].rearrange("p (u c) -> p u c", u=POOL_PAGES)
+        nc.vector.memset(vs_pages[:, :, VS_FILLED:SLOW_TO].rearrange("p u (a c) -> p a u c", c=RUN), 0.0)
         nc.vector.memset(ks_win[0 : P - KS_ROWS, :].bitcast(I32), 0)
         nc.vector.memset(vsc_win[0 : P - VS_ROWS, :].bitcast(I32), 0)
-        nc.vector.memset(vs_win[:, 0:POOL_FROM], 0.0)
-        nc.gpsimd.memset(vs_win[:, POOL_FROM - 8 : VS_ZEROED], 0.0)
+        nc.vector.memset(vs_pages[:, :, SLOW_TO : POOL_FROM + 8], 0.0)
+        nc.gpsimd.memset(vs_pages[:, :, POOL_FROM:PAGE], 0.0)
 
         def turn(rows, name, at):
             bank = psum.tile([P, 4, P], F32, name=name, offset=at * BANK)
@@ -102,27 +105,30 @@ def tile_attend_pkv4q_silu_kb_gate_kernel(
                 nc.tensor.transpose(bank[:, t, :], rows[:, t:PAGE:4], ident[:])
             return bank[:, :, 0 : 4 * POOL_PAGES : 4].rearrange("p t u -> p u t")
 
-        def lay(win, turned, zeroed, own):
-            nc.scalar.copy(own[:, 0, :].rearrange("p (u t) -> p u t", t=4), turned)
+        def own_values(turned, name):
+            own = shared.tile([P, POOL_PAGES, RUN], F32, name=name, offset=OWN_AT, align_bytes=64)
             nc.scalar.copy(
-                win[:, zeroed:T].rearrange("p (r c) -> p r c", c=OWN),
-                own[:].to_broadcast([P, (T - zeroed) // OWN, OWN]),
+                own[:].rearrange("p u (r t) -> p u r t", t=4),
+                turned.unsqueeze(2).to_broadcast([P, POOL_PAGES, RUN // 4, 4]),
             )
+            return own
+
+        def fill(pages, own, filled):
             nc.scalar.copy(
-                win[:].rearrange("p (u c) -> p u c", u=POOL_PAGES)[:, :, 0:4],
-                own[:, 0, :].rearrange("p (u t) -> p u t", t=4),
+                pages[:, :, 0:filled].rearrange("p u (r c) -> p u r c", c=RUN),
+                own[:].unsqueeze(2).to_broadcast([P, POOL_PAGES, filled // RUN, RUN]),
             )
 
         vs_turned = turn(vs_rows, "vs_turned", SCORE_BANKS)
         kb_turned = turn(kb_rows, "kb_turned", SCORE_BANKS + 1)
-        vs_own = keep.tile([P, 1, OWN], F32, name="vs_own", align_bytes=64)
-        lay(vs_win, vs_turned, VS_ZEROED, vs_own)
+        fill(vs_pages, own_values(vs_turned, "vs_own"), VS_FILLED)
+        kb_own = own_values(kb_turned, "kb_own")
         scale = keep.tile([P, B * N], F32, name="scale", align_bytes=64)
         nc.scalar.activation(scale[:], vs_win[:].indirect(off_t[:]), ACT.Copy)
 
         ks_rows = [
             shared.tile([P, N], U8, name="ks_rows0", offset=VW_AT, align_bytes=64),
-            shared.tile([P, N], U8, name="ks_rows1", offset=KB_AT - N // 2, align_bytes=64),
+            shared.tile([P, N], U8, name="ks_rows1", offset=OG_AT - N // 2, align_bytes=64),
         ]
         for b in range(B):
             nc.vector.tensor_copy(ks_rows[b][:], ks_win[:].indirect(off_t[:, b * N // 16 : (b + 1) * N // 16]))
@@ -149,11 +155,12 @@ def tile_attend_pkv4q_silu_kb_gate_kernel(
         nc.sync.dma_start(og_t[:], og.rearrange("b q e -> q b e"))
 
         kb_win = shared.tile([P, T], F32, name="kb_win", offset=KB_AT, align_bytes=64)
-        nc.gpsimd.memset(kb_win[:, 0:KB_ZEROED], 0.0)
-        kb_own = shared.tile([P, 1, OWN], F32, name="kb_own", offset=VS_AT, align_bytes=64)
-        lay(kb_win, kb_turned, KB_ZEROED, kb_own)
-        bias = shared.tile([P, B * N], F32, name="bias", offset=BIAS_AT, align_bytes=64)
-        nc.scalar.activation(bias[:], kb_win[:].indirect(off_t[:]), ACT.Copy)
+        kb_pages = kb_win[:].rearrange("p (u c) -> p u c", u=POOL_PAGES)
+        nc.gpsimd.memset(kb_pages[:, :, KB_FILLED:PAGE], 0.0)
+        fill(kb_pages, kb_own, KB_FILLED)
+        bias = [keep.tile([P, N], F32, name="bias%d" % b, align_bytes=64) for b in range(B)]
+        for b in range(B):
+            nc.scalar.activation(bias[b][:], kb_win[:].indirect(off_t[:, b * N // 16 : (b + 1) * N // 16]), ACT.Copy)
 
         vsc_rows = keep.tile([P, LISTED * DV], U8, name="vsc_rows", align_bytes=64)
         nc.vector.tensor_copy(vsc_rows[:], vsc_win[:].indirect(voff_t[:]))
@@ -171,7 +178,7 @@ def tile_attend_pkv4q_silu_kb_gate_kernel(
             kws[b] = kw
 
         def part(b):
-            kp = work.tile([P, PASSES * N], U16, name="kp", bufs=2, align_bytes=64)
+            kp = shared.tile([P, PASSES * N], U16, name="kp%d" % b, offset=KP_AT + 2 * PASSES * N * b, align_bytes=64)
             nc.vector.tensor_copy(
                 kp[:].rearrange("p (o s c i) -> p o c s i", o=PASSES, s=2, i=4),
                 kws[b][:].bitcast(U16).rearrange("p (c i s o) -> p o c s i", o=PASSES, s=2, i=4),
@@ -200,7 +207,7 @@ def tile_attend_pkv4q_silu_kb_gate_kernel(
                         )
                 for t in range(2 * h, 2 * h + 2):
                     nc.scalar.activation(
-                        p[:, t * NQ : (t + 1) * NQ], bank[:, t, :], ACT.Silu, bias=bias[:, j * PAGE + t : j * PAGE + t + 1]
+                        p[:, t * NQ : (t + 1) * NQ], bank[:, t, :], ACT.Silu, bias=bias[b][:, e * PAGE + t : e * PAGE + t + 1]
                     )
             ps[j] = p
 
@@ -223,25 +230,36 @@ def tile_attend_pkv4q_silu_kb_gate_kernel(
             nc.vector.quantize_mx(out=wc[:].bitcast(FP8X4), scales=wsc[:], in_=wis[j][:])
             wq[j] = (wc, wsc)
 
-        def weigh_values(b):
-            y = psum.tile([P, DV], F32, name="y%d" % b, offset=(SCORE_BANKS + b) * BANK)
+        def weigh_values(b, parts):
+            width = DV // parts
+            ys = [
+                psum.tile([P, width], F32, name="y%d_%d" % (b, h), offset=(SCORE_BANKS + b if h == 0 else 2) * BANK)
+                for h in range(parts)
+            ]
             for e in range(PAGES):
                 j = b * PAGES + e
-                nc.tensor.matmul_mx(
-                    out=y[:],
-                    lhsT=wq[j][0][:].bitcast(FP8X4),
-                    lhsT_scale=wq[j][1][:],
-                    rhs=vw[:, j * DV : (j + 1) * DV].bitcast(FP8X4),
-                    rhs_scale=vsc[:, j * DV : (j + 1) * DV],
-                    start=(e == 0),
-                    stop=(e == PAGES - 1),
-                )
-            return y
+                for h in range(parts):
+                    at = j * DV + h * width
+                    nc.tensor.matmul_mx(
+                        out=ys[h][:],
+                        lhsT=wq[j][0][:].bitcast(FP8X4),
+                        lhsT_scale=wq[j][1][:],
+                        rhs=vw[:, at : at + width].bitcast(FP8X4),
+                        rhs_scale=vsc[:, at : at + width],
+                        start=(e == 0),
+                        stop=(e == PAGES - 1),
+                    )
+            return ys
 
-        def finish(b, y, gate):
-            res = shared.tile([P, DV], F32, name="res%d" % b, offset=VW_AT + 8 * NQ * (LISTED - 1 + b), align_bytes=64)
-            nc.vector.tensor_tensor(res[:], y[:], gate[:, b, :], ALU.mult)
-            nc.sync.dma_start(out[b], res[:])
+        def finish(b, ys, gate):
+            width = DV // len(ys)
+            for h, y in enumerate(ys):
+                res = shared.tile(
+                    [P, width], F32, name="res%d_%d" % (b, h), offset=VW_AT + 8 * NQ * (LISTED - 1 + b) + 4 * width * h, align_bytes=64
+                )
+                cols = slice(h * width, (h + 1) * width)
+                nc.vector.tensor_tensor(res[:], y[:], gate[:, cols], ALU.mult)
+                nc.sync.dma_start(out[b][:, cols], res[:])
 
         for b in range(B):
             gather_keys(b)
@@ -257,10 +275,15 @@ def tile_attend_pkv4q_silu_kb_gate_kernel(
                 vsc_rows[first : first + 4, :].bitcast(I32),
             )
 
-        half = shared.tile([P, B, DV], F32, name="half", offset=BIAS_AT, align_bytes=64)
-        nc.scalar.activation(half[:], og_t[:], ACT.Tanh, scale=0.5)
-        gate = keep.tile([P, B, DV], F32, name="gate")
-        nc.scalar.activation(gate[:], half[:], ACT.Copy, scale=1.0 / 32.0, bias=1.0 / 32.0)
+        halves = [
+            shared.tile([P, DV], F32, name="half%d" % b, offset=KP_AT + 2 * PASSES * N + 4 * DV * b, align_bytes=64)
+            for b in range(B)
+        ]
+        gates = [keep.tile([P, DV], F32, name="gate%d" % b) for b in range(B)]
+        for b in range(B):
+            nc.scalar.activation(halves[b][:], og_t[:, b, :], ACT.Tanh, scale=0.5)
+        for b in range(B):
+            nc.scalar.activation(gates[b][:], halves[b][:], ACT.Copy, scale=1.0 / 32.0, bias=1.0 / 32.0)
 
         vw = keep.tile([P, LISTED * DV], U32, name="vw", align_bytes=64)
         nc.vector.tensor_copy(vw[:], vw_win[:].indirect(voff_t[:]))
@@ -270,6 +293,6 @@ def tile_attend_pkv4q_silu_kb_gate_kernel(
                 weigh(b * PAGES + e)
             for e in range(PAGES):
                 quantise(b * PAGES + e)
-            ys.append(weigh_values(b))
+            ys.append(weigh_values(b, b + 1))
         for b in range(B):
-            finish(b, ys[b], gate)
+            finish(b, ys[b], gates[b])

@@ -28,15 +28,16 @@ VS_ROWS = 16
 PLANE = N + NQ
 KW_AT = 0
 VW_AT = KW_AT + 4 * B * N
-KB_AT = VW_AT + 4 * POOL_PAGES * DV
-OG_AT = KB_AT + 4 * T
-OWN_AT = OG_AT + 4 * B * DV
-KP_AT = OWN_AT + 4 * POOL_PAGES * 8
+OG_AT = VW_AT + 4 * POOL_PAGES * DV
+KP_AT = OG_AT + 4 * B * DV
 RUN = 8
-VS_FILLED = 64
-KB_FILLED = 160
+SHIFTED = PAGE - 3
+VS_FILLED = 56
 SLOW_TO = VS_FILLED + 7 * RUN
-POOL_FROM = 272
+VS_POOL_FROM = 264
+KB_LATE_TO = 120
+KB_POOL_TO = 240
+KB_FILLED_FROM = KB_POOL_TO + RUN
 BANK = 2048
 SCORE_BANKS = 6
 
@@ -52,10 +53,30 @@ def tile_attend_pkv4q_silu_kb_gate_kernel(
         work = ctx.enter_context(tc.tile_pool(name="work", bufs=4))
         psum = ctx.enter_context(tc.psum_pool(name="psum", bufs=1))
 
-        vs_rows = keep.tile([P, PAGE], F32, name="vs_rows", align_bytes=64)
-        nc.scalar.dma_start(vs_rows[0 : 4 * POOL_PAGES : 4, :], vs[0, :].rearrange("(u c) -> u c", u=POOL_PAGES))
-        kb_rows = keep.tile([P, PAGE], F32, name="kb_rows", align_bytes=64)
-        nc.scalar.dma_start(kb_rows[0 : 4 * POOL_PAGES : 4, :], kb[0, :].rearrange("(u c) -> u c", u=POOL_PAGES))
+        def load_shifted(values, name):
+            rows = keep.tile([P, PAGE], F32, name=name, align_bytes=256)
+            shifted = values.rearrange("a b -> (a b)")[0 : 4 * (T + 1)].rearrange("(t x) -> t x", t=4)
+            nc.scalar.dma_start(
+                rows[0 : 8 * POOL_PAGES : 2, 0:SHIFTED],
+                shifted[:, 0:T].rearrange("t (u c) -> u t c", u=POOL_PAGES)[:, :, 0:SHIFTED],
+            )
+            return rows
+
+        voff_t = lists.tile([P, LISTED * DV // 16], U16, name="voff_t")
+        nc.sync.dma_start(voff_t[:], voffs)
+        vs_rows = load_shifted(vs, "vs_rows")
+        vsc_win = keep.tile([P, POOL_PAGES * DV], U8, name="vsc_win", align_bytes=256)
+        nc.sync.dma_start(
+            vsc_win[P - VS_ROWS : P, :].bitcast(I32).rearrange("f (u e) -> f u e", u=POOL_PAGES),
+            v_scales.rearrange("u f e -> f u e").bitcast(I32),
+        )
+        kb_rows = load_shifted(kb, "kb_rows")
+        ks_win = keep.tile([P, T], U8, name="ks_win", align_bytes=256)
+        nc.sync.dma_start(ks_win[P - KS_ROWS : P, :].bitcast(I32), k_scales.rearrange("o f t -> f o t").bitcast(I32))
+        off_t = lists.tile([P, B * N // 16], U16, name="off_t")
+        nc.sync.dma_start(off_t[:], offs)
+        kw_win = keep.tile([P, T], U32, name="kw_win", align_bytes=256)
+        nc.sync.dma_start(kw_win[:].bitcast(I32), k_words[0].rearrange("p t r -> p (t r)").bitcast(I32))
         dealt = [keep.tile([P, PLANE], U8, name="dealt%d" % b, align_bytes=64) for b in range(B)]
 
         def load_query_scales(queue, b):
@@ -65,20 +86,7 @@ def tile_attend_pkv4q_silu_kb_gate_kernel(
             )
 
         load_query_scales(nc.scalar, 0)
-        ks_win = keep.tile([P, T], U8, name="ks_win", align_bytes=64)
-        nc.sync.dma_start(ks_win[P - KS_ROWS : P, :].bitcast(I32), k_scales.rearrange("o f t -> f o t").bitcast(I32))
-        off_t = lists.tile([P, B * N // 16], U16, name="off_t")
-        nc.sync.dma_start(off_t[:], offs)
-        vsc_win = keep.tile([P, POOL_PAGES * DV], U8, name="vsc_win", align_bytes=64)
-        nc.sync.dma_start(
-            vsc_win[P - VS_ROWS : P, :].bitcast(I32).rearrange("f (u e) -> f u e", u=POOL_PAGES),
-            v_scales.rearrange("u f e -> f u e").bitcast(I32),
-        )
-        voff_t = lists.tile([P, LISTED * DV // 16], U16, name="voff_t")
-        nc.sync.dma_start(voff_t[:], voffs)
-        kw_win = keep.tile([P, T], U32, name="kw_win", align_bytes=64)
-        nc.sync.dma_start(kw_win[:].bitcast(I32), k_words[0].rearrange("p t r -> p (t r)").bitcast(I32))
-        qw = keep.tile([P, B * PASSES * NQ], U32, name="qw", align_bytes=64)
+        qw = keep.tile([P, B * PASSES * NQ], U32, name="qw", align_bytes=256)
         nc.sync.dma_start(
             qw[:].bitcast(I32).rearrange("p (g q) -> p g q", q=NQ),
             q_words.rearrange("b o p q r -> p (b o) (q r)").bitcast(I32),
@@ -93,47 +101,54 @@ def tile_attend_pkv4q_silu_kb_gate_kernel(
 
         vs_win = keep.tile([P, T], F32, name="vs_win", align_bytes=64)
         vs_pages = vs_win[:].rearrange("p (u c) -> p u c", u=POOL_PAGES)
+        kb_win = keep.tile([P, T], F32, name="kb_win", align_bytes=64)
+        kb_pages = kb_win[:].rearrange("p (u c) -> p u c", u=POOL_PAGES)
         nc.vector.memset(vs_pages[:, :, VS_FILLED:SLOW_TO].rearrange("p u (a c) -> p a u c", c=RUN), 0.0)
         nc.vector.memset(ks_win[0 : P - KS_ROWS, :].bitcast(I32), 0)
         nc.vector.memset(vsc_win[0 : P - VS_ROWS, :].bitcast(I32), 0)
-        nc.vector.memset(vs_pages[:, :, SLOW_TO : POOL_FROM + 8], 0.0)
-        nc.gpsimd.memset(vs_pages[:, :, POOL_FROM:PAGE], 0.0)
+        nc.vector.memset(vs_pages[:, :, SLOW_TO : VS_POOL_FROM + RUN], 0.0)
+        nc.vector.memset(kb_pages[:, :, KB_POOL_TO - RUN : KB_FILLED_FROM], 0.0)
+        nc.gpsimd.memset(vs_pages[:, :, VS_POOL_FROM:PAGE], 0.0)
+        nc.gpsimd.memset(kb_pages[:, :, KB_LATE_TO:KB_POOL_TO], 0.0)
 
         def turn(rows, name, at):
-            bank = psum.tile([P, 4, P], F32, name=name, offset=at * BANK)
-            for t in range(4):
-                nc.tensor.transpose(bank[:, t, :], rows[:, t:PAGE:4], ident[:])
-            return bank[:, :, 0 : 4 * POOL_PAGES : 4].rearrange("p t u -> p u t")
+            bank = psum.tile([P, P], F32, name=name, offset=at * BANK)
+            nc.tensor.transpose(bank[:], rows[:, 0:PAGE:4], ident[:])
+            turned = bank[:, 0 : 8 * POOL_PAGES : 2].rearrange("p (u t) -> p u t", t=4)
+            return turned.unsqueeze(2).to_broadcast([P, POOL_PAGES, RUN // 4, 4])
 
         def own_values(turned, name):
-            own = shared.tile([P, POOL_PAGES, RUN], F32, name=name, offset=OWN_AT, align_bytes=64)
-            nc.scalar.copy(
-                own[:].rearrange("p u (r t) -> p u r t", t=4),
-                turned.unsqueeze(2).to_broadcast([P, POOL_PAGES, RUN // 4, 4]),
-            )
+            own = keep.tile([P, POOL_PAGES, RUN], F32, name=name, align_bytes=64)
+            nc.scalar.copy(own[:].rearrange("p u (r t) -> p u r t", t=4), turned)
             return own
 
-        def fill(pages, own, filled):
+        def fill(columns, own, width):
             nc.scalar.copy(
-                pages[:, :, 0:filled].rearrange("p u (r c) -> p u r c", c=RUN),
-                own[:].unsqueeze(2).to_broadcast([P, POOL_PAGES, filled // RUN, RUN]),
+                columns.rearrange("p u (r c) -> p u r c", c=RUN),
+                own[:].unsqueeze(2).to_broadcast([P, POOL_PAGES, width // RUN, RUN]),
             )
 
         vs_turned = turn(vs_rows, "vs_turned", SCORE_BANKS)
+        kb_first = turn(kb_rows, "kb_first", SCORE_BANKS - 1)
         kb_turned = turn(kb_rows, "kb_turned", SCORE_BANKS + 1)
-        fill(vs_pages, own_values(vs_turned, "vs_own"), VS_FILLED)
+        vs_own = own_values(vs_turned, "vs_own")
         kb_own = own_values(kb_turned, "kb_own")
+        fill(vs_pages[:, :, 0:VS_FILLED], vs_own, VS_FILLED)
+        fill(kb_pages[:, :, KB_FILLED_FROM:PAGE], kb_own, PAGE - KB_FILLED_FROM)
         scale = keep.tile([P, B * N], F32, name="scale", align_bytes=64)
         nc.scalar.activation(scale[:], vs_win[:].indirect(off_t[:]), ACT.Copy)
 
+        vsc_rows = keep.tile([P, LISTED * DV], U8, name="vsc_rows", align_bytes=64)
+        nc.vector.tensor_copy(vsc_rows[:], vsc_win[:].indirect(voff_t[:]))
+
         ks_rows = [
-            shared.tile([P, N], U8, name="ks_rows0", offset=VW_AT, align_bytes=64),
-            shared.tile([P, N], U8, name="ks_rows1", offset=OG_AT - N // 2, align_bytes=64),
+            shared.tile([P, N], U8, name="ks_rows0", offset=VW_AT, align_bytes=256),
+            shared.tile([P, N], U8, name="ks_rows1", offset=OG_AT, align_bytes=256),
         ]
         for b in range(B):
             nc.vector.tensor_copy(ks_rows[b][:], ks_win[:].indirect(off_t[:, b * N // 16 : (b + 1) * N // 16]))
         planes = [keep.tile([P, PASSES * PLANE], U8, name="planes%d" % b, align_bytes=64) for b in range(B)]
-        vw_win = shared.tile([P, POOL_PAGES * DV], U32, name="vw_win", offset=VW_AT, align_bytes=64)
+        vw_win = shared.tile([P, POOL_PAGES * DV], U32, name="vw_win", offset=VW_AT, align_bytes=256)
         for b in range(B):
             nc.vector.tensor_copy(
                 dealt[b][:, 0:N].rearrange("p (j t m) -> p j t m", j=PAGES, t=4),
@@ -146,44 +161,39 @@ def tile_attend_pkv4q_silu_kb_gate_kernel(
                     dealt[b][first : first + 4 * PASSES, :].bitcast(I32),
                 )
             if b == 0:
+                nc.vector.tensor_copy(kb_pages[:, :, 0:RUN].rearrange("p u (r t) -> p u r t", t=4), kb_first)
+                nc.gpsimd.memset(kb_pages[:, :, 4:KB_LATE_TO], 0.0)
                 nc.sync.dma_start(
                     vw_win[:].bitcast(I32).rearrange("p (u e) -> p u e", u=POOL_PAGES),
                     v_words.rearrange("u p e r -> p u (e r)").bitcast(I32),
                 )
 
-        og_t = shared.tile([P, B, DV], F32, name="og_t", offset=OG_AT, align_bytes=64)
+        og_t = shared.tile([P, B, DV], F32, name="og_t", offset=OG_AT, align_bytes=256)
         nc.sync.dma_start(og_t[:], og.rearrange("b q e -> q b e"))
 
-        kb_win = shared.tile([P, T], F32, name="kb_win", offset=KB_AT, align_bytes=64)
-        kb_pages = kb_win[:].rearrange("p (u c) -> p u c", u=POOL_PAGES)
-        nc.gpsimd.memset(kb_pages[:, :, KB_FILLED:PAGE], 0.0)
-        fill(kb_pages, kb_own, KB_FILLED)
         bias = [keep.tile([P, N], F32, name="bias%d" % b, align_bytes=64) for b in range(B)]
         for b in range(B):
             nc.scalar.activation(bias[b][:], kb_win[:].indirect(off_t[:, b * N // 16 : (b + 1) * N // 16]), ACT.Copy)
 
-        vsc_rows = keep.tile([P, LISTED * DV], U8, name="vsc_rows", align_bytes=64)
-        nc.vector.tensor_copy(vsc_rows[:], vsc_win[:].indirect(voff_t[:]))
-
-        vsc = shared.tile([P, LISTED * DV], U8, name="vsc", offset=KW_AT, align_bytes=64)
+        vsc = shared.tile([P, LISTED * DV], U8, name="vsc", offset=KW_AT, align_bytes=256)
 
         kws, kps, ps, wis, wq = {}, {}, {}, {}, {}
 
-        def gather_keys(b):
-            kw = shared.tile([P, N], U32, name="kw%d" % b, offset=KW_AT + 4 * N * b, align_bytes=64)
+        def gather_keys(j):
+            kw = shared.tile([P, PAGE], U32, name="kw%d" % j, offset=KW_AT + 4 * PAGE * j, align_bytes=256)
             nc.vector.tensor_copy(
                 kw[:].rearrange("p (a m s) -> p m a s", a=2, s=2),
-                kw_win[:].indirect(off_t[:, b * N // 16 : (b + 1) * N // 16]),
+                kw_win[:].indirect(off_t[:, j * PAGE // 16 : (j + 1) * PAGE // 16]),
             )
-            kws[b] = kw
+            kws[j] = kw
 
-        def part(b):
-            kp = shared.tile([P, PASSES * N], U16, name="kp%d" % b, offset=KP_AT + 2 * PASSES * N * b, align_bytes=64)
+        def part(j):
+            kp = shared.tile([P, PASSES * PAGE], U16, name="kp%d" % j, offset=KP_AT + 2 * PASSES * PAGE * j, align_bytes=256)
             nc.vector.tensor_copy(
                 kp[:].rearrange("p (o s c i) -> p o c s i", o=PASSES, s=2, i=4),
-                kws[b][:].bitcast(U16).rearrange("p (c i s o) -> p o c s i", o=PASSES, s=2, i=4),
+                kws[j][:].bitcast(U16).rearrange("p (c i s o) -> p o c s i", o=PASSES, s=2, i=4),
             )
-            kps[b] = kp
+            kps[j] = kp
 
         def score(j):
             b, e = divmod(j, PAGES)
@@ -193,12 +203,12 @@ def tile_attend_pkv4q_silu_kb_gate_kernel(
                 for t in range(2 * h, 2 * h + 2):
                     for o in range(PASSES):
                         g = b * PASSES + o
-                        kat = o * N + ((t % 2) * 2 * PAGES + (t // 2) * PAGES + e) * P
+                        kat = o * PAGE + ((t % 2) * 2 + t // 2) * P
                         at = o * PLANE + e * PAGE + t * P
                         qat = o * PLANE + N
                         nc.tensor.matmul_mx(
                             out=bank[:, t, :],
-                            lhsT=kps[b][:, kat : kat + P].bitcast(FP4X4),
+                            lhsT=kps[j][:, kat : kat + P].bitcast(FP4X4),
                             lhsT_scale=planes[b][:, at : at + P],
                             rhs=qw[:, g * NQ : (g + 1) * NQ].bitcast(FP8X4),
                             rhs_scale=planes[b][:, qat : qat + NQ],
@@ -215,7 +225,7 @@ def tile_attend_pkv4q_silu_kb_gate_kernel(
             if j == 0:
                 wi = keep.tile([P, 4 * NQ], BF16, name="wi0", align_bytes=64)
             else:
-                wi = shared.tile([P, 4 * NQ], BF16, name="wi%d" % j, offset=VW_AT + 8 * NQ * j, align_bytes=64)
+                wi = shared.tile([P, 4 * NQ], BF16, name="wi%d" % j, offset=VW_AT + 8 * NQ * j, align_bytes=256)
             nc.vector.tensor_tensor(
                 wi[:].rearrange("p (c i t) -> p c t i", t=4, i=2),
                 ps[j][:].rearrange("p (t c i) -> p c t i", t=4, i=2),
@@ -255,18 +265,18 @@ def tile_attend_pkv4q_silu_kb_gate_kernel(
             width = DV // len(ys)
             for h, y in enumerate(ys):
                 res = shared.tile(
-                    [P, width], F32, name="res%d_%d" % (b, h), offset=VW_AT + 8 * NQ * (LISTED - 1 + b) + 4 * width * h, align_bytes=64
+                    [P, width], F32, name="res%d_%d" % (b, h), offset=VW_AT + 8 * NQ * (LISTED - 1 + b) + 4 * width * h, align_bytes=256
                 )
                 cols = slice(h * width, (h + 1) * width)
                 nc.vector.tensor_tensor(res[:], y[:], gate[:, cols], ALU.mult)
                 nc.sync.dma_start(out[b][:, cols], res[:])
 
-        for b in range(B):
-            gather_keys(b)
-        for b in range(B):
-            part(b)
-            for e in range(PAGES):
-                score(b * PAGES + e)
+        gather_keys(0)
+        for j in range(LISTED):
+            if j + 1 < LISTED:
+                gather_keys(j + 1)
+            part(j)
+            score(j)
 
         for quad in range(4):
             first = P - VS_ROWS + 4 * quad
@@ -276,7 +286,7 @@ def tile_attend_pkv4q_silu_kb_gate_kernel(
             )
 
         halves = [
-            shared.tile([P, DV], F32, name="half%d" % b, offset=KP_AT + 2 * PASSES * N + 4 * DV * b, align_bytes=64)
+            shared.tile([P, DV], F32, name="half%d" % b, offset=KP_AT + 2 * PASSES * PAGE * (LISTED - 1) + 4 * DV * b, align_bytes=256)
             for b in range(B)
         ]
         gates = [keep.tile([P, DV], F32, name="gate%d" % b) for b in range(B)]

@@ -223,15 +223,24 @@ def tile_attend_pkv4q_silu_kb_gate_kernel(
 
         def weigh(j):
             if j == 0:
-                wi = keep.tile([P, 4 * NQ], BF16, name="wi0", align_bytes=64)
+                wi = shared.tile([P, 4 * NQ], BF16, name="wi0", offset=KW_AT + 4 * PAGE * (LISTED - 2), align_bytes=256)
+                nc.gpsimd.tensor_tensor(
+                    wi[:].rearrange("p (q t) -> p q t", t=4),
+                    ps[j][:].rearrange("p (t q) -> p q t", t=4),
+                    scale[:, 0:4].unsqueeze(1).to_broadcast([P, NQ, 4]),
+                    ALU.mult,
+                )
             else:
-                wi = shared.tile([P, 4 * NQ], BF16, name="wi%d" % j, offset=VW_AT + 8 * NQ * j, align_bytes=256)
-            nc.vector.tensor_tensor(
-                wi[:].rearrange("p (c i t) -> p c t i", t=4, i=2),
-                ps[j][:].rearrange("p (t c i) -> p c t i", t=4, i=2),
-                scale[:, j * PAGE : j * PAGE + 4].rearrange("p (a t b) -> p a t b", a=1, b=1).to_broadcast([P, NQ // 2, 4, 2]),
-                ALU.mult,
-            )
+                if j == 1:
+                    wi = keep.tile([P, 4 * NQ], BF16, name="wi1", align_bytes=64)
+                else:
+                    wi = shared.tile([P, 4 * NQ], BF16, name="wi%d" % j, offset=VW_AT + 8 * NQ * j, align_bytes=256)
+                nc.vector.tensor_tensor(
+                    wi[:].rearrange("p (c i t) -> p c t i", t=4, i=2),
+                    ps[j][:].rearrange("p (t c i) -> p c t i", t=4, i=2),
+                    scale[:, j * PAGE : j * PAGE + 4].rearrange("p (a t b) -> p a t b", a=1, b=1).to_broadcast([P, NQ // 2, 4, 2]),
+                    ALU.mult,
+                )
             wis[j] = wi
 
         def quantise(j):

@@ -32,12 +32,10 @@ OG_AT = VW_AT + 4 * POOL_PAGES * DV
 KP_AT = OG_AT + 4 * B * DV
 RUN = 8
 SHIFTED = PAGE - 3
-VS_FILLED = 56
-SLOW_TO = VS_FILLED + 7 * RUN
-VS_POOL_FROM = 264
-KB_LATE_TO = 120
-KB_POOL_TO = 240
-KB_FILLED_FROM = KB_POOL_TO + RUN
+SLOW_TO = RUN + 7 * RUN
+VS_POOL_FROM = 200
+KB_POOL_TO = 112
+KB_FILLED_FROM = 248
 BANK = 2048
 SCORE_BANKS = 6
 
@@ -64,13 +62,13 @@ def tile_attend_pkv4q_silu_kb_gate_kernel(
 
         voff_t = lists.tile([P, LISTED * DV // 16], U16, name="voff_t")
         nc.sync.dma_start(voff_t[:], voffs)
-        vs_rows = load_shifted(vs, "vs_rows")
+        kb_rows = load_shifted(kb, "kb_rows")
         vsc_win = keep.tile([P, POOL_PAGES * DV], U8, name="vsc_win", align_bytes=256)
         nc.sync.dma_start(
             vsc_win[P - VS_ROWS : P, :].bitcast(I32).rearrange("f (u e) -> f u e", u=POOL_PAGES),
             v_scales.rearrange("u f e -> f u e").bitcast(I32),
         )
-        kb_rows = load_shifted(kb, "kb_rows")
+        vs_rows = load_shifted(vs, "vs_rows")
         ks_win = keep.tile([P, T], U8, name="ks_win", align_bytes=256)
         nc.sync.dma_start(ks_win[P - KS_ROWS : P, :].bitcast(I32), k_scales.rearrange("o f t -> f o t").bitcast(I32))
         off_t = lists.tile([P, B * N // 16], U16, name="off_t")
@@ -103,13 +101,12 @@ def tile_attend_pkv4q_silu_kb_gate_kernel(
         vs_pages = vs_win[:].rearrange("p (u c) -> p u c", u=POOL_PAGES)
         kb_win = keep.tile([P, T], F32, name="kb_win", align_bytes=64)
         kb_pages = kb_win[:].rearrange("p (u c) -> p u c", u=POOL_PAGES)
-        nc.vector.memset(vs_pages[:, :, VS_FILLED:SLOW_TO].rearrange("p u (a c) -> p a u c", c=RUN), 0.0)
+        nc.vector.memset(vs_pages[:, :, RUN:SLOW_TO].rearrange("p u (a c) -> p a u c", c=RUN), 0.0)
         nc.vector.memset(ks_win[0 : P - KS_ROWS, :].bitcast(I32), 0)
         nc.vector.memset(vsc_win[0 : P - VS_ROWS, :].bitcast(I32), 0)
+        nc.vector.memset(kb_pages[:, :, KB_POOL_TO:KB_FILLED_FROM], 0.0)
         nc.vector.memset(vs_pages[:, :, SLOW_TO : VS_POOL_FROM + RUN], 0.0)
-        nc.vector.memset(kb_pages[:, :, KB_POOL_TO - RUN : KB_FILLED_FROM], 0.0)
         nc.gpsimd.memset(vs_pages[:, :, VS_POOL_FROM:PAGE], 0.0)
-        nc.gpsimd.memset(kb_pages[:, :, KB_LATE_TO:KB_POOL_TO], 0.0)
 
         def turn(rows, name, at):
             bank = psum.tile([P, P], F32, name=name, offset=at * BANK)
@@ -117,24 +114,16 @@ def tile_attend_pkv4q_silu_kb_gate_kernel(
             turned = bank[:, 0 : 8 * POOL_PAGES : 2].rearrange("p (u t) -> p u t", t=4)
             return turned.unsqueeze(2).to_broadcast([P, POOL_PAGES, RUN // 4, 4])
 
-        def own_values(turned, name):
-            own = keep.tile([P, POOL_PAGES, RUN], F32, name=name, align_bytes=64)
-            nc.scalar.copy(own[:].rearrange("p u (r t) -> p u r t", t=4), turned)
-            return own
-
-        def fill(columns, own, width):
-            nc.scalar.copy(
-                columns.rearrange("p u (r c) -> p u r c", c=RUN),
-                own[:].unsqueeze(2).to_broadcast([P, POOL_PAGES, width // RUN, RUN]),
-            )
-
+        kb_turned = turn(kb_rows, "kb_turned", SCORE_BANKS + 1)
         vs_turned = turn(vs_rows, "vs_turned", SCORE_BANKS)
         kb_first = turn(kb_rows, "kb_first", SCORE_BANKS - 1)
-        kb_turned = turn(kb_rows, "kb_turned", SCORE_BANKS + 1)
-        vs_own = own_values(vs_turned, "vs_own")
-        kb_own = own_values(kb_turned, "kb_own")
-        fill(vs_pages[:, :, 0:VS_FILLED], vs_own, VS_FILLED)
-        fill(kb_pages[:, :, KB_FILLED_FROM:PAGE], kb_own, PAGE - KB_FILLED_FROM)
+        kb_own = keep.tile([P, POOL_PAGES, RUN], F32, name="kb_own", align_bytes=64)
+        nc.scalar.copy(kb_own[:].rearrange("p u (r t) -> p u r t", t=4), kb_turned)
+        nc.scalar.copy(vs_pages[:, :, 0:RUN].rearrange("p u (r t) -> p u r t", t=4), vs_turned)
+        nc.scalar.copy(
+            kb_pages[:, :, KB_FILLED_FROM:PAGE].rearrange("p u (r c) -> p u r c", c=RUN),
+            kb_own[:].unsqueeze(2).to_broadcast([P, POOL_PAGES, (PAGE - KB_FILLED_FROM) // RUN, RUN]),
+        )
         scale = keep.tile([P, B * N], F32, name="scale", align_bytes=64)
         nc.scalar.activation(scale[:], vs_win[:].indirect(off_t[:]), ACT.Copy)
 
@@ -162,7 +151,7 @@ def tile_attend_pkv4q_silu_kb_gate_kernel(
                 )
             if b == 0:
                 nc.vector.tensor_copy(kb_pages[:, :, 0:RUN].rearrange("p u (r t) -> p u r t", t=4), kb_first)
-                nc.gpsimd.memset(kb_pages[:, :, 4:KB_LATE_TO], 0.0)
+                nc.gpsimd.memset(kb_pages[:, :, 4:KB_POOL_TO], 0.0)
                 nc.sync.dma_start(
                     vw_win[:].bitcast(I32).rearrange("p (u e) -> p u e", u=POOL_PAGES),
                     v_words.rearrange("u p e r -> p u (e r)").bitcast(I32),
@@ -223,24 +212,15 @@ def tile_attend_pkv4q_silu_kb_gate_kernel(
 
         def weigh(j):
             if j == 0:
-                wi = shared.tile([P, 4 * NQ], BF16, name="wi0", offset=KW_AT + 4 * PAGE * (LISTED - 2), align_bytes=256)
-                nc.gpsimd.tensor_tensor(
-                    wi[:].rearrange("p (q t) -> p q t", t=4),
-                    ps[j][:].rearrange("p (t q) -> p q t", t=4),
-                    scale[:, 0:4].unsqueeze(1).to_broadcast([P, NQ, 4]),
-                    ALU.mult,
-                )
+                wi = keep.tile([P, 4 * NQ], BF16, name="wi0", align_bytes=64)
             else:
-                if j == 1:
-                    wi = keep.tile([P, 4 * NQ], BF16, name="wi1", align_bytes=64)
-                else:
-                    wi = shared.tile([P, 4 * NQ], BF16, name="wi%d" % j, offset=VW_AT + 8 * NQ * j, align_bytes=256)
-                nc.vector.tensor_tensor(
-                    wi[:].rearrange("p (c i t) -> p c t i", t=4, i=2),
-                    ps[j][:].rearrange("p (t c i) -> p c t i", t=4, i=2),
-                    scale[:, j * PAGE : j * PAGE + 4].rearrange("p (a t b) -> p a t b", a=1, b=1).to_broadcast([P, NQ // 2, 4, 2]),
-                    ALU.mult,
-                )
+                wi = shared.tile([P, 4 * NQ], BF16, name="wi%d" % j, offset=VW_AT + 8 * NQ * j, align_bytes=256)
+            nc.vector.tensor_tensor(
+                wi[:].rearrange("p (c i t) -> p c t i", t=4, i=2),
+                ps[j][:].rearrange("p (t c i) -> p c t i", t=4, i=2),
+                scale[:, j * PAGE : j * PAGE + 4].rearrange("p (a t b) -> p a t b", a=1, b=1).to_broadcast([P, NQ // 2, 4, 2]),
+                ALU.mult,
+            )
             wis[j] = wi
 
         def quantise(j):

@@ -31,11 +31,11 @@ VW_AT = KW_AT + 4 * B * N
 OG_AT = VW_AT + 4 * POOL_PAGES * DV
 KP_AT = OG_AT + 4 * B * DV
 RUN = 8
-SHIFTED = PAGE - 3
+SHIFTED = PAGE - 2
 SLOW_TO = RUN + 7 * RUN
-VS_POOL_FROM = 200
+VS_POOL_FROM = 176
 KB_POOL_TO = 112
-KB_FILLED_FROM = 248
+KB_FILLED_FROM = 200
 BANK = 2048
 SCORE_BANKS = 6
 
@@ -51,24 +51,21 @@ def tile_attend_pkv4q_silu_kb_gate_kernel(
         work = ctx.enter_context(tc.tile_pool(name="work", bufs=4))
         psum = ctx.enter_context(tc.psum_pool(name="psum", bufs=1))
 
-        def load_shifted(values, name):
-            rows = keep.tile([P, PAGE], F32, name=name, align_bytes=256)
-            shifted = values.rearrange("a b -> (a b)")[0 : 4 * (T + 1)].rearrange("(t x) -> t x", t=4)
-            nc.scalar.dma_start(
-                rows[0 : 8 * POOL_PAGES : 2, 0:SHIFTED],
-                shifted[:, 0:T].rearrange("t (u c) -> u t c", u=POOL_PAGES)[:, :, 0:SHIFTED],
-            )
-            return rows
-
         voff_t = lists.tile([P, LISTED * DV // 16], U16, name="voff_t")
         nc.sync.dma_start(voff_t[:], voffs)
-        kb_rows = load_shifted(kb, "kb_rows")
+        kb_rows = keep.tile([P, PAGE], F32, name="kb_rows", align_bytes=256)
+        shifted = kb.rearrange("a b -> (a b)")[0 : 2 * (T + 2)].rearrange("(h x) -> h x", h=2)
+        nc.scalar.dma_start(
+            kb_rows[0 : 8 * POOL_PAGES : 4, 0:SHIFTED],
+            shifted[:, 0:T].rearrange("h (u c) -> u h c", u=POOL_PAGES)[:, :, 0:SHIFTED],
+        )
         vsc_win = keep.tile([P, POOL_PAGES * DV], U8, name="vsc_win", align_bytes=256)
         nc.sync.dma_start(
             vsc_win[P - VS_ROWS : P, :].bitcast(I32).rearrange("f (u e) -> f u e", u=POOL_PAGES),
             v_scales.rearrange("u f e -> f u e").bitcast(I32),
         )
-        vs_rows = load_shifted(vs, "vs_rows")
+        vs_rows = keep.tile([P, PAGE], F32, name="vs_rows", align_bytes=256)
+        nc.scalar.dma_start(vs_rows[0 : 4 * POOL_PAGES : 4, :], vs[0, :].rearrange("(u c) -> u c", u=POOL_PAGES))
         ks_win = keep.tile([P, T], U8, name="ks_win", align_bytes=256)
         nc.sync.dma_start(ks_win[P - KS_ROWS : P, :].bitcast(I32), k_scales.rearrange("o f t -> f o t").bitcast(I32))
         off_t = lists.tile([P, B * N // 16], U16, name="off_t")
@@ -108,22 +105,25 @@ def tile_attend_pkv4q_silu_kb_gate_kernel(
         nc.vector.memset(vs_pages[:, :, SLOW_TO : VS_POOL_FROM + RUN], 0.0)
         nc.gpsimd.memset(vs_pages[:, :, VS_POOL_FROM:PAGE], 0.0)
 
-        def turn(rows, name, at):
-            bank = psum.tile([P, P], F32, name=name, offset=at * BANK)
-            nc.tensor.transpose(bank[:], rows[:, 0:PAGE:4], ident[:])
-            turned = bank[:, 0 : 8 * POOL_PAGES : 2].rearrange("p (u t) -> p u t", t=4)
-            return turned.unsqueeze(2).to_broadcast([P, POOL_PAGES, RUN // 4, 4])
+        def turn_biases(name, at):
+            bank = psum.tile([P, 2, P], F32, name=name, offset=at * BANK)
+            for s in range(2):
+                nc.tensor.transpose(bank[:, s, :], kb_rows[:, s:PAGE:4], ident[:])
+            return bank[:, :, 0 : 8 * POOL_PAGES : 4].rearrange("p s (u h) -> p u h s", h=2)
 
-        kb_turned = turn(kb_rows, "kb_turned", SCORE_BANKS + 1)
-        vs_turned = turn(vs_rows, "vs_turned", SCORE_BANKS)
-        kb_first = turn(kb_rows, "kb_first", SCORE_BANKS - 1)
-        kb_own = keep.tile([P, POOL_PAGES, RUN], F32, name="kb_own", align_bytes=64)
-        nc.scalar.copy(kb_own[:].rearrange("p u (r t) -> p u r t", t=4), kb_turned)
-        nc.scalar.copy(vs_pages[:, :, 0:RUN].rearrange("p u (r t) -> p u r t", t=4), vs_turned)
+        kb_turned = turn_biases("kb_turned", SCORE_BANKS + 1)
+        kb_first = turn_biases("kb_first", SCORE_BANKS - 1)
+        vs_bank = psum.tile([P, 4, P], F32, name="vs_bank", offset=SCORE_BANKS * BANK)
+        for t in range(4):
+            nc.tensor.transpose(vs_bank[:, t, :], vs_rows[:, t:PAGE:4], ident[:])
+        vs_turned = vs_bank[:, :, 0 : 4 * POOL_PAGES : 4].rearrange("p t u -> p u t").unsqueeze(2).to_broadcast([P, POOL_PAGES, RUN // 4, 4])
+        kb_own = keep.tile([P, POOL_PAGES, 4], F32, name="kb_own", align_bytes=64)
+        nc.scalar.copy(kb_own[:].rearrange("p u (h s) -> p u h s", s=2), kb_turned)
         nc.scalar.copy(
-            kb_pages[:, :, KB_FILLED_FROM:PAGE].rearrange("p u (r c) -> p u r c", c=RUN),
-            kb_own[:].unsqueeze(2).to_broadcast([P, POOL_PAGES, (PAGE - KB_FILLED_FROM) // RUN, RUN]),
+            kb_pages[:, :, KB_FILLED_FROM:PAGE].rearrange("p u (r c) -> p u r c", c=4),
+            kb_own[:].unsqueeze(2).to_broadcast([P, POOL_PAGES, (PAGE - KB_FILLED_FROM) // 4, 4]),
         )
+        nc.scalar.copy(vs_pages[:, :, 0:RUN].rearrange("p u (r t) -> p u r t", t=4), vs_turned)
         scale = keep.tile([P, B * N], F32, name="scale", align_bytes=64)
         nc.scalar.activation(scale[:], vs_win[:].indirect(off_t[:]), ACT.Copy)
 
@@ -150,7 +150,10 @@ def tile_attend_pkv4q_silu_kb_gate_kernel(
                     dealt[b][first : first + 4 * PASSES, :].bitcast(I32),
                 )
             if b == 0:
-                nc.vector.tensor_copy(kb_pages[:, :, 0:RUN].rearrange("p u (r t) -> p u r t", t=4), kb_first)
+                nc.vector.tensor_copy(
+                    kb_pages[:, :, 0:RUN].rearrange("p u (r h s) -> p u r h s", h=2, s=2),
+                    kb_first.unsqueeze(2).to_broadcast([P, POOL_PAGES, RUN // 4, 2, 2]),
+                )
                 nc.gpsimd.memset(kb_pages[:, :, 4:KB_POOL_TO], 0.0)
                 nc.sync.dma_start(
                     vw_win[:].bitcast(I32).rearrange("p (u e) -> p u e", u=POOL_PAGES),

@@ -174,7 +174,7 @@ def tile_attend_pkv4q_silu_kb_gate_kernel(
         def gather_keys(j):
             kw = shared.tile([P, PAGE], U32, name="kw%d" % j, offset=KW_AT + 4 * PAGE * j, align_bytes=256)
             nc.vector.tensor_copy(
-                kw[:].rearrange("p (a m s) -> p m a s", a=2, s=2),
+                kw[:],
                 kw_win[:].indirect(off_t[:, j * PAGE // 16 : (j + 1) * PAGE // 16]),
             )
             kws[j] = kw
@@ -182,8 +182,8 @@ def tile_attend_pkv4q_silu_kb_gate_kernel(
         def part(j):
             kp = shared.tile([P, PASSES * PAGE], U16, name="kp%d" % j, offset=KP_AT + 2 * PASSES * PAGE * j, align_bytes=256)
             nc.vector.tensor_copy(
-                kp[:].rearrange("p (o s c i) -> p o c s i", o=PASSES, s=2, i=4),
-                kws[j][:].bitcast(U16).rearrange("p (c i s o) -> p o c s i", o=PASSES, s=2, i=4),
+                kp[:].rearrange("p (o t c i) -> p o c t i", o=PASSES, t=4, i=2),
+                kws[j][:].bitcast(U16).rearrange("p (c i t o) -> p o c t i", o=PASSES, t=4, i=2),
             )
             kps[j] = kp
 
@@ -195,7 +195,7 @@ def tile_attend_pkv4q_silu_kb_gate_kernel(
                 for t in range(2 * h, 2 * h + 2):
                     for o in range(PASSES):
                         g = b * PASSES + o
-                        kat = o * PAGE + ((t % 2) * 2 + t // 2) * P
+                        kat = o * PAGE + t * P
                         at = o * PLANE + e * PAGE + t * P
                         qat = o * PLANE + N
                         nc.tensor.matmul_mx(

@@ -34,8 +34,9 @@ RUN = 8
 SHIFTED = PAGE - 2
 SLOW_TO = RUN + 7 * RUN
 VS_POOL_FROM = 176
-KB_POOL_TO = 112
+KB_POOL_TO = 168
 KB_FILLED_FROM = 200
+KB_SPLIT = 448
 BANK = 2048
 SCORE_BANKS = 6
 
@@ -119,11 +120,16 @@ def tile_attend_pkv4q_silu_kb_gate_kernel(
         vs_turned = vs_bank[:, :, 0 : 4 * POOL_PAGES : 4].rearrange("p t u -> p u t").unsqueeze(2).to_broadcast([P, POOL_PAGES, RUN // 4, 4])
         kb_own = keep.tile([P, POOL_PAGES, 4], F32, name="kb_own", align_bytes=64)
         nc.scalar.copy(kb_own[:].rearrange("p u (h s) -> p u h s", s=2), kb_turned)
-        nc.scalar.copy(
-            kb_pages[:, :, KB_FILLED_FROM:PAGE].rearrange("p u (r c) -> p u r c", c=4),
-            kb_own[:].unsqueeze(2).to_broadcast([P, POOL_PAGES, (PAGE - KB_FILLED_FROM) // 4, 4]),
-        )
+
+        def fill(first, end):
+            nc.scalar.copy(
+                kb_pages[:, :, first:end].rearrange("p u (r c) -> p u r c", c=4),
+                kb_own[:].unsqueeze(2).to_broadcast([P, POOL_PAGES, (end - first) // 4, 4]),
+            )
+
+        fill(KB_FILLED_FROM, KB_SPLIT)
         nc.scalar.copy(vs_pages[:, :, 0:RUN].rearrange("p u (r t) -> p u r t", t=4), vs_turned)
+        fill(KB_SPLIT, PAGE)
         scale = keep.tile([P, B * N], F32, name="scale", align_bytes=64)
         nc.scalar.activation(scale[:], vs_win[:].indirect(off_t[:]), ACT.Copy)
 
@@ -171,19 +177,17 @@ def tile_attend_pkv4q_silu_kb_gate_kernel(
 
         kws, kps, ps, wis, wq = {}, {}, {}, {}, {}
 
-        def gather_keys(j):
-            kw = shared.tile([P, PAGE], U32, name="kw%d" % j, offset=KW_AT + 4 * PAGE * j, align_bytes=256)
-            nc.vector.tensor_copy(
-                kw[:],
-                kw_win[:].indirect(off_t[:, j * PAGE // 16 : (j + 1) * PAGE // 16]),
-            )
-            kws[j] = kw
+        def gather_keys(j, pages):
+            kw = shared.tile([P, pages * PAGE], U32, name="kw%d" % j, offset=KW_AT + 4 * PAGE * j, align_bytes=256)
+            nc.vector.tensor_copy(kw[:], kw_win[:].indirect(off_t[:, j * PAGE // 16 : (j + pages) * PAGE // 16]))
+            for e in range(pages):
+                kws[j + e] = kw[:, e * PAGE : (e + 1) * PAGE]
 
         def part(j):
             kp = shared.tile([P, PASSES * PAGE], U16, name="kp%d" % j, offset=KP_AT + 2 * PASSES * PAGE * j, align_bytes=256)
             nc.vector.tensor_copy(
                 kp[:].rearrange("p (o t c i) -> p o c t i", o=PASSES, t=4, i=2),
-                kws[j][:].bitcast(U16).rearrange("p (c i t o) -> p o c t i", o=PASSES, t=4, i=2),
+                kws[j].bitcast(U16).rearrange("p (c i t o) -> p o c t i", o=PASSES, t=4, i=2),
             )
             kps[j] = kp
 
@@ -263,10 +267,10 @@ def tile_attend_pkv4q_silu_kb_gate_kernel(
                 nc.vector.tensor_tensor(res[:], y[:], gate[:, cols], ALU.mult)
                 nc.sync.dma_start(out[b][:, cols], res[:])
 
-        gather_keys(0)
+        gather_keys(0, PAGES)
         for j in range(LISTED):
-            if j + 1 < LISTED:
-                gather_keys(j + 1)
+            if j + PAGES < LISTED:
+                gather_keys(j + PAGES, 1)
             part(j)
             score(j)
 

from contextlib import ExitStack

import concourse.mybir as mybir
from concourse.masks import make_identity

B, N, T, D, DV, NQ = 2, 1024, 4096, 1024, 256, 128
P = 128
PAGE = 512
PAGES = N // PAGE
LISTED = B * PAGES
POOL_PAGES = T // PAGE
PASSES = D // PAGE
FLOPS = 2 * B * NQ * N * (D + DV)

F32 = mybir.dt.float32
BF16 = mybir.dt.bfloat16
I32 = mybir.dt.int32
U32 = mybir.dt.uint32
U16 = mybir.dt.uint16
U8 = mybir.dt.uint8
FP8X4 = mybir.dt.float8_e4m3fn_x4
FP4X4 = mybir.dt.float4_e2m1fn_x4
ACT = mybir.ActivationFunctionType
ALU = mybir.AluOpType

KS_ROWS = 16 * PASSES
VS_ROWS = 16
PLANE = N + NQ
KW_AT = 0
VW_AT = KW_AT + 4 * B * N
OG_AT = VW_AT + 4 * POOL_PAGES * DV
KP_AT = OG_AT + 4 * B * DV
RUN = 8
SHIFTED = PAGE - 2
SLOW_TO = RUN + 7 * RUN
VS_POOL_FROM = 176
KB_POOL_TO = 168
KB_FILLED_FROM = 200
KB_SPLIT = 448
BANK = 2048
SCORE_BANKS = 6


def tile_attend_pkv4q_silu_kb_gate_kernel(
    tc, q_words, q_scales, k_words, k_scales, v_words, v_scales, vs, kb, og, offs, voffs, out
):
    nc = tc.nc
    with ExitStack() as ctx:
        lists = ctx.enter_context(tc.tile_pool(name="lists", bufs=1))
        keep = ctx.enter_context(tc.tile_pool(name="keep", bufs=1))
        shared = ctx.enter_context(tc.tile_pool(name="shared", bufs=1))
        work = ctx.enter_context(tc.tile_pool(name="work", bufs=4))
        psum = ctx.enter_context(tc.psum_pool(name="psum", bufs=1))

        voff_t = lists.tile([P, LISTED * DV // 16], U16, name="voff_t")
        nc.sync.dma_start(voff_t[:], voffs)
        kb_rows = keep.tile([P, PAGE], F32, name="kb_rows", align_bytes=256)
        shifted = kb.rearrange("a b -> (a b)")[0 : 2 * (T + 2)].rearrange("(h x) -> h x", h=2)
        nc.scalar.dma_start(
            kb_rows[0 : 8 * POOL_PAGES : 4, 0:SHIFTED],
            shifted[:, 0:T].rearrange("h (u c) -> u h c", u=POOL_PAGES)[:, :, 0:SHIFTED],
        )
        vsc_win = keep.tile([P, POOL_PAGES * DV], U8, name="vsc_win", align_bytes=256)
        nc.sync.dma_start(
            vsc_win[P - VS_ROWS : P, :].bitcast(I32).rearrange("f (u e) -> f u e", u=POOL_PAGES),
            v_scales.rearrange("u f e -> f u e").bitcast(I32),
        )
        vs_rows = keep.tile([P, PAGE], F32, name="vs_rows", align_bytes=256)
        nc.scalar.dma_start(vs_rows[0 : 4 * POOL_PAGES : 4, :], vs[0, :].rearrange("(u c) -> u c", u=POOL_PAGES))
        ks_win = keep.tile([P, T], U8, name="ks_win", align_bytes=256)
        nc.sync.dma_start(ks_win[P - KS_ROWS : P, :].bitcast(I32), k_scales.rearrange("o f t -> f o t").bitcast(I32))
        off_t = lists.tile([P, B * N // 16], U16, name="off_t")
        nc.sync.dma_start(off_t[:], offs)
        kw_win = keep.tile([P, T], U32, name="kw_win", align_bytes=256)
        nc.sync.dma_start(kw_win[:].bitcast(I32), k_words[0].rearrange("p t r -> p (t r)").bitcast(I32))
        dealt = [keep.tile([P, PLANE], U8, name="dealt%d" % b, align_bytes=64) for b in range(B)]

        def load_query_scales(queue, b):
            queue.dma_start(
                dealt[b][P - KS_ROWS : P, N:PLANE].bitcast(I32),
                q_scales[b].rearrange("o f q -> f o q").bitcast(I32),
            )

        load_query_scales(nc.scalar, 0)
        qw = keep.tile([P, B * PASSES * NQ], U32, name="qw", align_bytes=256)
        nc.sync.dma_start(
            qw[:].bitcast(I32).rearrange("p (g q) -> p g q", q=NQ),
            q_words.rearrange("b o p q r -> p (b o) (q r)").bitcast(I32),
        )
        load_query_scales(nc.sync, 1)

        ident = keep.tile([P, P], F32, name="ident")
        nc.vector.memset(ident[:], 0.0)
        make_identity(nc, ident[:], nomemset=True)
        warm = keep.tile([P, 1], F32, name="warm")
        nc.scalar.activation(warm[:], ident[:, 0:1], ACT.Silu)

        vs_win = keep.tile([P, T], F32, name="vs_win", align_bytes=64)
        vs_pages = vs_win[:].rearrange("p (u c) -> p u c", u=POOL_PAGES)
        kb_win = keep.tile([P, T], F32, name="kb_win", align_bytes=64)
        kb_pages = kb_win[:].rearrange("p (u c) -> p u c", u=POOL_PAGES)
        nc.vector.memset(vs_pages[:, :, RUN:SLOW_TO].rearrange("p u (a c) -> p a u c", c=RUN), 0.0)
        nc.vector.memset(ks_win[0 : P - KS_ROWS, :].bitcast(I32), 0)
        nc.vector.memset(vsc_win[0 : P - VS_ROWS, :].bitcast(I32), 0)
        nc.vector.memset(kb_pages[:, :, KB_POOL_TO:KB_FILLED_FROM], 0.0)
        nc.vector.memset(vs_pages[:, :, SLOW_TO : VS_POOL_FROM + RUN], 0.0)
        nc.gpsimd.memset(vs_pages[:, :, VS_POOL_FROM:PAGE], 0.0)

        def turn_biases(name, at):
            bank = psum.tile([P, 2, P], F32, name=name, offset=at * BANK)
            for s in range(2):
                nc.tensor.transpose(bank[:, s, :], kb_rows[:, s:PAGE:4], ident[:])
            return bank[:, :, 0 : 8 * POOL_PAGES : 4].rearrange("p s (u h) -> p u h s", h=2)

        kb_turned = turn_biases("kb_turned", SCORE_BANKS + 1)
        kb_first = turn_biases("kb_first", SCORE_BANKS - 1)
        vs_bank = psum.tile([P, 4, P], F32, name="vs_bank", offset=SCORE_BANKS * BANK)
        for t in range(4):
            nc.tensor.transpose(vs_bank[:, t, :], vs_rows[:, t:PAGE:4], ident[:])
        vs_turned = vs_bank[:, :, 0 : 4 * POOL_PAGES : 4].rearrange("p t u -> p u t").unsqueeze(2).to_broadcast([P, POOL_PAGES, RUN // 4, 4])
        kb_own = keep.tile([P, POOL_PAGES, 4], F32, name="kb_own", align_bytes=64)
        nc.scalar.copy(kb_own[:].rearrange("p u (h s) -> p u h s", s=2), kb_turned)

        def fill(first, end):
            nc.scalar.copy(
                kb_pages[:, :, first:end].rearrange("p u (r c) -> p u r c", c=4),
                kb_own[:].unsqueeze(2).to_broadcast([P, POOL_PAGES, (end - first) // 4, 4]),
            )

        fill(KB_FILLED_FROM, KB_SPLIT)
        nc.scalar.copy(vs_pages[:, :, 0:RUN].rearrange("p u (r t) -> p u r t", t=4), vs_turned)
        fill(KB_SPLIT, PAGE)
        scale = keep.tile([P, B * N], F32, name="scale", align_bytes=64)
        nc.scalar.activation(scale[:], vs_win[:].indirect(off_t[:]), ACT.Copy)

        vsc_rows = keep.tile([P, LISTED * DV], U8, name="vsc_rows", align_bytes=64)
        nc.vector.tensor_copy(vsc_rows[:], vsc_win[:].indirect(voff_t[:]))

        ks_rows = [
            shared.tile([P, N], U8, name="ks_rows0", offset=VW_AT, align_bytes=256),
            shared.tile([P, N], U8, name="ks_rows1", offset=OG_AT, align_bytes=256),
        ]
        for b in range(B):
            nc.vector.tensor_copy(ks_rows[b][:], ks_win[:].indirect(off_t[:, b * N // 16 : (b + 1) * N // 16]))
        planes = [keep.tile([P, PASSES * PLANE], U8, name="planes%d" % b, align_bytes=64) for b in range(B)]
        vw_win = shared.tile([P, POOL_PAGES * DV], U32, name="vw_win", offset=VW_AT, align_bytes=256)
        for b in range(B):
            nc.vector.tensor_copy(
                dealt[b][:, 0:N].rearrange("p (j t m) -> p j t m", j=PAGES, t=4),
                ks_rows[b][:].rearrange("p (j m t) -> p j t m", j=PAGES, t=4),
            )
            for quad in (0, 2, 1, 3):
                first = P - KS_ROWS + 4 * PASSES * quad
                nc.sync.dma_start(
                    planes[b][32 * quad : 32 * quad + 4, :].bitcast(I32),
                    dealt[b][first : first + 4 * PASSES, :].bitcast(I32),
                )
            if b == 0:
                nc.vector.tensor_copy(
                    kb_pages[:, :, 0:RUN].rearrange("p u (r h s) -> p u r h s", h=2, s=2),
                    kb_first.unsqueeze(2).to_broadcast([P, POOL_PAGES, RUN // 4, 2, 2]),
                )
                nc.gpsimd.memset(kb_pages[:, :, 4:KB_POOL_TO], 0.0)
                nc.sync.dma_start(
                    vw_win[:].bitcast(I32).rearrange("p (u e) -> p u e", u=POOL_PAGES),
                    v_words.rearrange("u p e r -> p u (e r)").bitcast(I32),
                )

        og_t = shared.tile([P, B, DV], F32, name="og_t", offset=OG_AT, align_bytes=256)
        nc.sync.dma_start(og_t[:], og.rearrange("b q e -> q b e"))

        bias = [keep.tile([P, N], F32, name="bias%d" % b, align_bytes=64) for b in range(B)]
        for b in range(B):
            nc.scalar.activation(bias[b][:], kb_win[:].indirect(off_t[:, b * N // 16 : (b + 1) * N // 16]), ACT.Copy)

        vsc = shared.tile([P, LISTED * DV], U8, name="vsc", offset=KW_AT, align_bytes=256)

        kws, kps, ps, wis, wq = {}, {}, {}, {}, {}

        def gather_keys(j, pages):
            kw = shared.tile([P, pages * PAGE], U32, name="kw%d" % j, offset=KW_AT + 4 * PAGE * j, align_bytes=256)
            nc.vector.tensor_copy(kw[:], kw_win[:].indirect(off_t[:, j * PAGE // 16 : (j + pages) * PAGE // 16]))
            for e in range(pages):
                kws[j + e] = kw[:, e * PAGE : (e + 1) * PAGE]

        def part(j):
            kp = shared.tile([P, PASSES * PAGE], U16, name="kp%d" % j, offset=KP_AT + 2 * PASSES * PAGE * j, align_bytes=256)
            nc.vector.tensor_copy(
                kp[:].rearrange("p (o t c i) -> p o c t i", o=PASSES, t=4, i=2),
                kws[j].bitcast(U16).rearrange("p (c i t o) -> p o c t i", o=PASSES, t=4, i=2),
            )
            kps[j] = kp

        def score(j):
            b, e = divmod(j, PAGES)
            p = work.tile([P, PAGE], F32, name="p", align_bytes=64)
            for h in range(2):
                bank = psum.tile([P, 4, P], F32, name="sc%d_%d" % (j, h), offset=((2 * j + h) % SCORE_BANKS) * BANK)
                for t in range(2 * h, 2 * h + 2):
                    for o in range(PASSES):
                        g = b * PASSES + o
                        kat = o * PAGE + t * P
                        at = o * PLANE + e * PAGE + t * P
                        qat = o * PLANE + N
                        nc.tensor.matmul_mx(
                            out=bank[:, t, :],
                            lhsT=kps[j][:, kat : kat + P].bitcast(FP4X4),
                            lhsT_scale=planes[b][:, at : at + P],
                            rhs=qw[:, g * NQ : (g + 1) * NQ].bitcast(FP8X4),
                            rhs_scale=planes[b][:, qat : qat + NQ],
                            start=(o == 0),
                            stop=(o == PASSES - 1),
                        )
                for t in range(2 * h, 2 * h + 2):
                    nc.scalar.activation(
                        p[:, t * NQ : (t + 1) * NQ], bank[:, t, :], ACT.Silu, bias=bias[b][:, e * PAGE + t : e * PAGE + t + 1]
                    )
            ps[j] = p

        def weigh(j):
            if j == 0:
                wi = keep.tile([P, 4 * NQ], BF16, name="wi0", align_bytes=64)
            else:
                wi = shared.tile([P, 4 * NQ], BF16, name="wi%d" % j, offset=VW_AT + 8 * NQ * j, align_bytes=256)
            nc.vector.tensor_tensor(
                wi[:].rearrange("p (c i t) -> p c t i", t=4, i=2),
                ps[j][:].rearrange("p (t c i) -> p c t i", t=4, i=2),
                scale[:, j * PAGE : j * PAGE + 4].rearrange("p (a t b) -> p a t b", a=1, b=1).to_broadcast([P, NQ // 2, 4, 2]),
                ALU.mult,
            )
            wis[j] = wi

        def quantise(j):
            wc = work.tile([P, NQ], U32, name="wc", align_bytes=64)
            wsc = work.tile([P, NQ], U8, name="wsc", align_bytes=64)
            nc.vector.quantize_mx(out=wc[:].bitcast(FP8X4), scales=wsc[:], in_=wis[j][:])
            wq[j] = (wc, wsc)

        def weigh_values(b, parts):
            width = DV // parts
            ys = [
                psum.tile([P, width], F32, name="y%d_%d" % (b, h), offset=(SCORE_BANKS + b if h == 0 else 2) * BANK)
                for h in range(parts)
            ]
            for e in range(PAGES):
                j = b * PAGES + e
                for h in range(parts):
                    at = j * DV + h * width
                    nc.tensor.matmul_mx(
                        out=ys[h][:],
                        lhsT=wq[j][0][:].bitcast(FP8X4),
                        lhsT_scale=wq[j][1][:],
                        rhs=vw[:, at : at + width].bitcast(FP8X4),
                        rhs_scale=vsc[:, at : at + width],
                        start=(e == 0),
                        stop=(e == PAGES - 1),
                    )
            return ys

        def finish(b, ys, gate):
            width = DV // len(ys)
            for h, y in enumerate(ys):
                res = shared.tile(
                    [P, width], F32, name="res%d_%d" % (b, h), offset=VW_AT + 8 * NQ * (LISTED - 1 + b) + 4 * width * h, align_bytes=256
                )
                cols = slice(h * width, (h + 1) * width)
                nc.vector.tensor_tensor(res[:], y[:], gate[:, cols], ALU.mult)
                nc.sync.dma_start(out[b][:, cols], res[:])

        gather_keys(0, PAGES)
        for j in range(LISTED):
            if j + PAGES < LISTED:
                gather_keys(j + PAGES, 1)
            part(j)
            score(j)

        for quad in range(4):
            first = P - VS_ROWS + 4 * quad
            nc.sync.dma_start(
                vsc[32 * quad : 32 * quad + 4, :].bitcast(I32),
                vsc_rows[first : first + 4, :].bitcast(I32),
            )

        halves = [
            shared.tile([P, DV], F32, name="half%d" % b, offset=KP_AT + 2 * PASSES * PAGE * (LISTED - 1) + 4 * DV * b, align_bytes=256)
            for b in range(B)
        ]
        gates = [keep.tile([P, DV], F32, name="gate%d" % b) for b in range(B)]
        for b in range(B):
            nc.scalar.activation(halves[b][:], og_t[:, b, :], ACT.Tanh, scale=0.5)
        for b in range(B):
            nc.scalar.activation(gates[b][:], halves[b][:], ACT.Copy, scale=1.0 / 32.0, bias=1.0 / 32.0)

        vw = keep.tile([P, LISTED * DV], U32, name="vw", align_bytes=64)
        nc.vector.tensor_copy(vw[:], vw_win[:].indirect(voff_t[:]))
        ys = []
        for b in range(B):
            for e in range(PAGES):
                weigh(b * PAGES + e)
            for e in range(PAGES):
                quantise(b * PAGES + e)
            ys.append(weigh_values(b, b + 1))
        for b in range(B):
            finish(b, ys[b], gates[b])
